import numpy as np
import ml_dtypes


def mxq(x, axis, fmt="e4m3"):
    dtype, down = {"e4m3": (ml_dtypes.float8_e4m3fn, 7), "e5m2": (ml_dtypes.float8_e5m2, 14)}[fmt]
    v = np.moveaxis(np.asarray(x, np.float32).astype(ml_dtypes.bfloat16).astype(np.float64), axis, -1)
    blocks = v.reshape(v.shape[:-1] + (-1, 32))
    amax = np.abs(blocks).max(-1, keepdims=True)
    byte = np.maximum(np.where(amax > 0, np.frexp(amax)[1] - 1 + 127, 0) - down, 1)
    scale = np.exp2(byte - 127.0)
    codes = (blocks / scale).astype(np.float32).astype(dtype).astype(np.float64)
    return np.moveaxis((codes * scale).reshape(v.shape), -1, axis)


WIDE = False


def mx_kscale(k):
    if not WIDE:
        return np.ones(k)
    levels = np.array([10, -10, 5, -5, 0])
    if k % 512:
        return np.exp2(np.random.permutation(np.resize(levels, k // 32))).repeat(32)
    a = np.empty((k // 512, 16))
    for p in range(k // 512):
        a[p, :8] = np.random.permutation(np.resize(levels, 8))
        for g in range(8):
            far = levels[np.abs(levels - a[p, g]) >= 10]
            a[p, g + 8] = far[np.random.randint(len(far))]
    return np.exp2(a.ravel()).repeat(32)


def f64(x):
    return np.asarray(x).astype(np.float64)


def striped(idx):
    return np.tile(idx.reshape(-1, 16).T, (8, 1)).astype(np.uint16)


def unstriped(offs):
    return offs[:16].T.reshape(-1).astype(np.int64)


E2M1 = np.array([0.0, 0.5, 1.0, 1.5, 2.0, 3.0, 4.0, 6.0, -0.0, -0.5, -1.0, -1.5, -2.0, -3.0, -4.0, -6.0])


def pack_weight(w, fmt):
    k, n = w.shape
    w = f64(np.asarray(w, np.float32).astype(ml_dtypes.bfloat16)).reshape(k // 32, 32, n)
    amax = np.abs(w).max(1)
    if fmt == "e4m3":
        byte = np.frexp(amax)[1] - 1 + 127 - 7
    else:
        mant, ex = np.frexp(amax / 6.0)
        byte = np.where(mant > 0.5, ex, ex - 1) + 127
    byte = np.clip(np.where(amax > 0, byte, 1), 1, 254)
    scaled = (w * np.exp2(127.0 - byte)[:, None, :]).reshape(k, n).astype(np.float32)
    by_word = np.ascontiguousarray(scaled.reshape(k // 512, 128, 4, n).transpose(0, 1, 3, 2))
    if fmt == "e4m3":
        words = by_word.astype(ml_dtypes.float8_e4m3fn).view(np.uint8)
    else:
        c = by_word.astype(ml_dtypes.float4_e2m1fn).view(np.uint8) & 0xF
        words = (c[..., 0::2] | (c[..., 1::2] << 4)).reshape(k // 512, 128, 2 * n)
    return np.ascontiguousarray(words), np.ascontiguousarray(byte.astype(np.uint8).reshape(k // 512, 16, n))


def unpack_weight(words, scales, fmt):
    g, _, n = scales.shape
    words = np.ascontiguousarray(words).reshape(g, 128, n, -1)
    if fmt == "e4m3":
        vals = words.view(ml_dtypes.float8_e4m3fn).astype(np.float64)
    else:
        nib = np.empty((g, 128, n, 4), np.uint8)
        nib[..., 0::2] = words & 0xF
        nib[..., 1::2] = words >> 4
        vals = E2M1[nib]
    vals = vals * np.repeat(np.exp2(scales.astype(np.float64) - 127.0), 8, axis=1)[..., None]
    return vals.transpose(0, 1, 3, 2).reshape(g * 512, n)


def gelu(v):
    return 0.5 * v * (1.0 + np.tanh(np.sqrt(2.0 / np.pi) * (v + 0.044715 * v**3)))


K1, K2, H, N, T, T2, S = 512, 1024, 1024, 768, 4096, 2048, 1024

def setup_inputs():
    n = np.random.standard_normal
    s1 = mx_kscale(K1)[:, None]
    s2 = mx_kscale(K2)[:, None]
    u = mx_kscale(H)[:, None]
    tab_words, tab_scales = pack_weight(n((K1, T)) * s1, "e4m3")
    tab2_words, tab2_scales = pack_weight(n((K2, T2)) * s2, "e4m3")
    wk_words, wk_scales = pack_weight(n((K1, H)) / np.sqrt(K1) / s1, "e2m1")
    wv = (n((K2, H)) / np.sqrt(K2) / s2 * u.T).astype(np.float32)
    wd = (n((H, N)) / np.sqrt(H) / u).astype(np.float32)
    offs = striped(np.random.permutation(T)[:S])
    offs2 = striped(np.random.permutation(T2)[:S])
    return {"tab_words": tab_words, "tab_scales": tab_scales,
            "tab2_words": tab2_words, "tab2_scales": tab2_scales,
            "offs": offs, "offs2": offs2,
            "wk_words": wk_words, "wk_scales": wk_scales,
            "wv": wv, "wd": wd}

def reference(tab_words, tab_scales, tab2_words, tab2_scales, offs, offs2,
              wk_words, wk_scales, wv, wd):
    v = unpack_weight(tab_words, tab_scales, "e4m3")[:, unstriped(offs)]
    v2 = unpack_weight(tab2_words, tab2_scales, "e4m3")[:, unstriped(offs2)]
    wk = unpack_weight(wk_words, wk_scales, "e2m1")
    a = wk.T @ v
    b = mxq(f64(wv), 0, "e4m3").T @ v2
    h = a / (1.0 + np.exp(-a)) * b
    return mxq(f64(wd), 0, "e4m3").T @ mxq(h, 0, "e4m3")

@@ -1,0 +1,304 @@
+from contextlib import ExitStack
+
+import concourse.mybir as mybir
+
+K1, K2, H, N, T, T2, S = 512, 1024, 1024, 768, 4096, 2048, 1024
+FLOPS = 2 * S * (K1 * H + K2 * H + H * N)
+
+F32 = mybir.dt.float32
+BF16 = mybir.dt.bfloat16
+I32 = mybir.dt.int32
+U32 = mybir.dt.uint32
+U16 = mybir.dt.uint16
+U8 = mybir.dt.uint8
+FP8X4 = mybir.dt.float8_e4m3fn_x4
+FP4X4 = mybir.dt.float4_e2m1fn_x4
+SILU = mybir.ActivationFunctionType.Silu
+MULT = mybir.AluOpType.mult
+
+P = 128
+PACK = 4
+PASS = P * PACK
+HALF = S // 2
+CHUNK = 128
+PAIR = 2 * CHUNK
+WD_COLS = 256
+
+
+def tile_list_memory_kv_swiglu_kernel(tc, tab_words, tab_scales, tab2_words, tab2_scales, offs, offs2,
+                                               wk_words, wk_scales, wv, wd, out):
+    nc = tc.nc
+    with ExitStack() as ctx:
+        keep = ctx.enter_context(tc.tile_pool(name="keep", bufs=1))
+        stage = ctx.enter_context(tc.tile_pool(name="stage", bufs=3))
+        psum = ctx.enter_context(tc.psum_pool(name="psum", bufs=1))
+
+        def held(shape, dtype, name):
+            return keep.tile(shape, dtype, name=name, align_bytes=64)
+
+        key_list = keep.tile([P, S // 16], U16, name="key_list")
+        val_list = keep.tile([P, S // 16], U16, name="val_list")
+        key_scale_tab = held([P, T], U8, "key_scale_tab")
+        val_scale_tab = held([P, T2], U8, "val_scale_tab")
+        wk_scale_raw = held([P, H], U8, "wk_scale_raw")
+        wk_raw = held([P, H // 2], I32, "wk_raw")
+        key_tab = held([P, T], U32, "key_tab")
+        val_tab = [held([P, T2], U32, "val_tab%d" % a) for a in range(2)]
+        wv_raw = {}
+        wd_raw = {}
+
+        nc.vector.memset(key_scale_tab[:, :T // 2].bitcast(I32), 0)
+        nc.gpsimd.memset(key_scale_tab[:, T // 2:].bitcast(I32), 0)
+        nc.vector.memset(wk_scale_raw[:].bitcast(I32), 0)
+        nc.gpsimd.memset(val_scale_tab[:, :T2 // 2].bitcast(I32), 0)
+        nc.vector.memset(val_scale_tab[:, T2 // 2:].bitcast(I32), 0)
+
+        def load_wv(a, b, c0, width):
+            raw = held([P, PACK, width], F32, "wv_raw%d%d%d" % (a, b, c0))
+            rows = wv[a * PASS:(a + 1) * PASS, b * PASS + c0:b * PASS + c0 + width]
+            nc.sync.dma_start(out=raw[:], in_=rows.rearrange("(p i) r -> p i r", i=PACK))
+            wv_raw[a, b, c0] = raw
+
+        def load_wd(b, c):
+            raw = held([P, PACK, WD_COLS], F32, "wd_raw%d%d" % (b, c))
+            rows = wd[b * PASS:(b + 1) * PASS, c * WD_COLS:(c + 1) * WD_COLS]
+            nc.sync.dma_start(out=raw[:], in_=rows.rearrange("(p i) n -> p i n", i=PACK))
+            wd_raw[b, c] = raw
+
+        def words_of(table, a):
+            return table[a].rearrange("p t i -> p (t i)").bitcast(I32)
+
+        def load_planes(queue, plane, scales):
+            passes = scales.shape[0]
+            for q in range(4):
+                queue.dma_start(out=plane[32 * q:32 * q + 4 * passes, :].bitcast(I32),
+                                in_=scales[:, 4 * q:4 * q + 4, :].bitcast(I32))
+
+        nc.sync.dma_start(key_list[:], offs)
+        nc.sync.dma_start(out=wk_raw[:], in_=wk_words[0].bitcast(I32))
+        load_planes(nc.sync, key_scale_tab, tab_scales)
+        nc.sync.dma_start(out=key_tab[:].bitcast(I32), in_=words_of(tab_words, 0))
+        nc.sync.dma_start(val_list[:], offs2)
+        load_planes(nc.scalar, wk_scale_raw, wk_scales)
+        nc.sync.dma_start(out=val_tab[0][:].bitcast(I32), in_=words_of(tab2_words, 0))
+        load_planes(nc.sync, val_scale_tab, tab2_scales)
+        load_wv(0, 0, 0, 256)
+        load_wv(0, 0, 256, 256)
+        load_wv(1, 0, 0, PASS)
+        nc.sync.dma_start(out=val_tab[1][:].bitcast(I32), in_=words_of(tab2_words, 1))
+        load_wv(0, 1, 0, PASS)
+        load_wv(1, 1, 0, 256)
+        load_wv(1, 1, 256, 256)
+        for c in range(N // WD_COLS):
+            for b in range(2):
+                load_wd(b, c)
+
+        def gather(window, lst, dtype, name, u):
+            picked = held([P, HALF], dtype, "%s%d" % (name, u))
+            nc.vector.tensor_copy(out=picked[:], in_=window[:].indirect(lst[:, u * HALF // 16:(u + 1) * HALF // 16]))
+            return picked
+
+        def copy_on(engine, dst, src):
+            if engine == "scalar":
+                nc.scalar.copy(out=dst, in_=src)
+            else:
+                nc.vector.tensor_copy(out=dst, in_=src)
+
+        wv_bf = {}
+        wv_codes = {}
+        wv_planes = {}
+
+        def cast_wv(a, b, c0, width, engine):
+            if (a, b) not in wv_bf:
+                wv_bf[a, b] = stage.tile([P, PACK, P, PACK], BF16, name="wv_bf", bufs=4, align_bytes=64)
+            q0 = c0 // PACK
+            dst = wv_bf[a, b][:, :, q0:q0 + width // PACK, :].rearrange("p t q i -> p q i t")
+            copy_on(engine, dst, wv_raw[a, b, c0][:].rearrange("p i (q t) -> p q i t", t=PACK))
+
+        def quantize(src, width, name):
+            codes = held([P, width], U32, name + "_codes")
+            plane = held([P, width], U8, name + "_plane")
+            nc.vector.quantize_mx(out=codes[:].bitcast(FP8X4), scales=plane[:], in_=src)
+            return codes, plane
+
+        def quantize_wv(a, b):
+            wv_codes[a, b], wv_planes[a, b] = quantize(
+                wv_bf[a, b][:].rearrange("p t q i -> p (t q i)"), PASS, "wv%d%d" % (a, b))
+
+        key_planes = [gather(key_scale_tab, key_list, U8, "key_plane", u) for u in range(2)]
+        wk_codes = held([P, 2 * H], U8, "wk_codes")
+        wk_plane = held([P, H], U8, "wk_plane")
+        nc.vector.tensor_copy(
+            out=wk_codes[:].bitcast(U16).rearrange("p (b t q) -> p b q t", b=2, t=PACK),
+            in_=wk_raw[:].bitcast(U16).rearrange("p (b q t) -> p b q t", b=2, t=PACK))
+        nc.vector.tensor_copy(
+            out=wk_plane[:].rearrange("p (b t q) -> p b q t", b=2, t=PACK),
+            in_=wk_scale_raw[:].rearrange("p (b q t) -> p b q t", b=2, t=PACK))
+
+        gates = {}
+
+        def gate(b, jc, room=None):
+            u, cols = divmod(jc * CHUNK, HALF)
+            cols = slice(cols, cols + CHUNK)
+            bank = psum.tile([P, PACK, CHUNK], F32, name="side_bank", bufs=3)
+            for t in range(PACK):
+                r0 = b * PASS + t * P
+                nc.tensor.matmul_mx(out=bank[:, t, :],
+                                    lhsT=wk_codes[:, 2 * r0:2 * (r0 + P)].bitcast(FP4X4),
+                                    lhsT_scale=wk_plane[:, r0:r0 + P],
+                                    rhs=key_codes[u][:, cols].bitcast(FP8X4), rhs_scale=key_planes[u][:, cols],
+                                    start=True, stop=True)
+            if room is None:
+                room = held([P, CHUNK * PACK], F32, "gate%d%d" % (b, jc))[:]
+            gates[b, jc] = room.rearrange("p (j t) -> p j t", t=PACK)
+            nc.scalar.activation(out=gates[b, jc], in_=bank[:].rearrange("p t j -> p j t"), func=SILU)
+
+        h_bf = {}
+        h_codes = {}
+        h_planes = {}
+
+        def hidden(b, jc, room=None):
+            u, cols = divmod(jc * CHUNK, HALF)
+            cols = slice(cols, cols + CHUNK)
+            bank = psum.tile([P, PACK, CHUNK], F32, name="val_bank", bufs=5)
+            for t in range(PACK):
+                for a in range(2):
+                    nc.tensor.matmul_mx(out=bank[:, t, :],
+                                        lhsT=wv_codes[a, b][:, t * P:(t + 1) * P].bitcast(FP8X4),
+                                        lhsT_scale=wv_planes[a, b][:, t * P:(t + 1) * P],
+                                        rhs=val_codes[a][u][:, cols].bitcast(FP8X4),
+                                        rhs_scale=val_planes[u][4 * a:, cols],
+                                        start=(a == 0), stop=(a == 1))
+            jp, e = divmod(jc, 2)
+            if e == 0:
+                if room is None:
+                    room = stage.tile([P, PAIR * PACK], BF16, name="h_bf", bufs=4, align_bytes=64)[:]
+                h_bf[b, jp] = room
+            nc.vector.tensor_tensor(out=h_bf[b, jp].rearrange("p (e j t) -> p e j t", e=2, t=PACK)[:, e, :, :], in0=bank[:].rearrange("p t j -> p j t"),
+                                    in1=gates[b, jc], op=MULT)
+
+        def quantize_h(b, jp):
+            h_codes[b, jp], h_planes[b, jp] = quantize(
+                h_bf[b, jp], PAIR, "h%d%d" % (b, jp))
+
+        def quantize_h_chunk(b, jc):
+            jp, e = divmod(jc, 2)
+            h_codes[b, jp, e], h_planes[b, jp, e] = quantize(
+                h_bf[b, jp][:, e * CHUNK * PACK:(e + 1) * CHUNK * PACK], CHUNK, "hc%d%d" % (b, jc))
+
+        wd_codes = {}
+        wd_planes = {}
+        wd_bf = {}
+
+        def cast_wd(b, c, engine):
+            wd_bf[b, c] = stage.tile([P, WD_COLS, PACK], BF16, name="wd_bf", bufs=6, align_bytes=64)
+            copy_on(engine, wd_bf[b, c][:].rearrange("p (m e) i -> p m i e", e=4),
+                    wd_raw[b, c][:].rearrange("p i (m e) -> p m i e", e=4))
+
+        def quantize_wd(b, c):
+            wd_codes[b, c], wd_planes[b, c] = quantize(
+                wd_bf[b, c][:].rearrange("p n i -> p (n i)"), WD_COLS, "wd%d%d" % (b, c))
+
+        def project(c, jp, engine):
+            bank = psum.tile([P, 2, PAIR], F32, name="side_bank", bufs=3)
+            for v in range(2):
+                for b in range(2):
+                    nc.tensor.matmul_mx(out=bank[:, v, :],
+                                        lhsT=wd_codes[b, c][:, v * P:(v + 1) * P].bitcast(FP8X4),
+                                        lhsT_scale=wd_planes[b, c][:, v * P:(v + 1) * P],
+                                        rhs=h_codes[b, jp][:].bitcast(FP8X4), rhs_scale=h_planes[b, jp][:],
+                                        start=(b == 0), stop=(b == 1))
+            result = stage.tile([P, 2, PAIR], F32, name="result", bufs=6)
+            copy_on(engine, result[:], bank[:])
+            rows = out[c * WD_COLS:(c + 1) * WD_COLS, jp * PAIR:(jp + 1) * PAIR]
+            nc.sync.dma_start(out=rows.rearrange("(v p) j -> p v j", p=P), in_=result[:])
+
+        def project_chunk(g, jc, engine):
+            jp, e = divmod(jc, 2)
+            bank = psum.tile([P, 3, CHUNK], F32, name="side_bank", bufs=3)
+            for w in range(3):
+                c, v = divmod(3 * g + w, 2)
+                for b in range(2):
+                    nc.tensor.matmul_mx(out=bank[:, w, :],
+                                        lhsT=wd_codes[b, c][:, v * P:(v + 1) * P].bitcast(FP8X4),
+                                        lhsT_scale=wd_planes[b, c][:, v * P:(v + 1) * P],
+                                        rhs=h_codes[b, jp, e][:].bitcast(FP8X4), rhs_scale=h_planes[b, jp, e][:],
+                                        start=(b == 0), stop=(b == 1))
+            result = stage.tile([P, 3, CHUNK], F32, name="result", bufs=6)
+            copy_on(engine, result[:], bank[:])
+            rows = out[3 * g * P:3 * (g + 1) * P, jc * CHUNK:(jc + 1) * CHUNK]
+            nc.sync.dma_start(out=rows.rearrange("(w p) j -> p w j", p=P), in_=result[:])
+
+        key_codes = [gather(key_tab, key_list, U32, "key_codes", u) for u in range(2)]
+        val_planes = [gather(val_scale_tab, val_list, U8, "val_plane", u) for u in range(2)]
+        val_codes = [[gather(val_tab[0], val_list, U32, "val_codes0", u) for u in range(2)]]
+        cast_wv(0, 0, 0, 256, "scalar")
+        cast_wv(0, 0, 256, 256, "vector")
+        cast_wv(1, 0, 0, PASS, "vector")
+        quantize_wv(0, 0)
+        quantize_wv(1, 0)
+        val_codes.append([gather(val_tab[1], val_list, U32, "val_codes1", u) for u in range(2)])
+        for jc in range(8):
+            gate(0, jc)
+        cast_wv(0, 1, 0, PASS, "scalar")
+        cast_wv(1, 1, 0, 256, "scalar")
+        cast_wv(1, 1, 256, 256, "vector")
+        for jc in range(4):
+            gate(1, jc)
+        raw_room = wv_raw[1, 1, 0][:].rearrange("p i r -> p (i r)")
+        for jc in range(4, 6):
+            gate(1, jc, raw_room[:, (jc - 4) * CHUNK * PACK:(jc - 3) * CHUNK * PACK])
+        raw_room = wv_raw[1, 1, 256][:].rearrange("p i r -> p (i r)")
+        for jc in range(6, 8):
+            gate(1, jc, raw_room[:, (jc - 6) * CHUNK * PACK:(jc - 5) * CHUNK * PACK])
+        quantize_wv(0, 1)
+        quantize_wv(1, 1)
+        wv_room = wv_bf[1, 1][:].rearrange("p t q i -> p (t q i)")
+        for b in range(2):
+            cast_wd(b, 0, "scalar")
+            quantize_wd(b, 0)
+        hidden(0, 0)
+        hidden(0, 1)
+        hidden(0, 2, wv_room[:, :PAIR * PACK])
+        quantize_h(0, 0)
+        hidden(0, 3)
+        hidden(1, 0)
+        quantize_h(0, 1)
+        hidden(1, 1)
+        for b in range(2):
+            cast_wd(b, 1, "scalar")
+            quantize_wd(b, 1)
+        hidden(1, 2)
+        quantize_h(1, 0)
+        project(0, 0, "scalar")
+        hidden(1, 3)
+        hidden(0, 4, wv_room[:, PAIR * PACK:])
+        quantize_h(1, 1)
+        project(1, 0, "scalar")
+        hidden(0, 5)
+        for b in range(2):
+            cast_wd(b, 2, "scalar")
+            quantize_wd(b, 2)
+        hidden(1, 4, wd_bf[1, 1][:].rearrange("p n i -> p (n i)"))
+        quantize_h(0, 2)
+        project(0, 1, "scalar")
+        hidden(1, 5)
+        project(1, 1, "scalar")
+        hidden(0, 6, wd_bf[0, 1][:].rearrange("p n i -> p (n i)"))
+        quantize_h(1, 2)
+        project(2, 0, "scalar")
+        project(2, 1, "scalar")
+        hidden(1, 6, wd_bf[1, 2][:].rearrange("p n i -> p (n i)"))
+        quantize_h_chunk(0, 6)
+        project(0, 2, "scalar")
+        hidden(0, 7)
+        quantize_h_chunk(1, 6)
+        project(1, 2, "scalar")
+        hidden(1, 7)
+        quantize_h_chunk(0, 7)
+        quantize_h_chunk(1, 7)
+        project(2, 2, "scalar")
+        project_chunk(0, 6, "scalar")
+        project_chunk(1, 6, "vector")
+        project_chunk(0, 7, "vector")
+        project_chunk(1, 7, "scalar")

@@ -59,11 +59,14 @@ def tile_list_memory_kv_swiglu_kernel(tc, tab_words, tab_scales, tab2_words, tab
             nc.sync.dma_start(out=raw[:], in_=rows.rearrange("(p i) r -> p i r", i=PACK))
             wv_raw[a, b, c0] = raw
 
-        def load_wd(b, c):
-            raw = held([P, PACK, WD_COLS], F32, "wd_raw%d%d" % (b, c))
-            rows = wd[b * PASS:(b + 1) * PASS, c * WD_COLS:(c + 1) * WD_COLS]
-            nc.sync.dma_start(out=raw[:], in_=rows.rearrange("(p i) n -> p i n", i=PACK))
-            wd_raw[b, c] = raw
+        def load_wd(b, c0, chunks):
+            raw = held([P, PACK, chunks * WD_COLS], F32, "wd_raw%d%d" % (b, c0))
+            rows = wd[b * PASS:(b + 1) * PASS, c0 * WD_COLS:(c0 + chunks) * WD_COLS]
+            rows = rows.rearrange("(m t e) n -> t m e n", t=PACK, e=4)
+            for t in range(PACK):
+                nc.sync.dma_start(out=raw[:, t, :], in_=rows[t])
+            for c in range(chunks):
+                wd_raw[b, c0 + c] = raw[:, :, c * WD_COLS:(c + 1) * WD_COLS]
 
         def words_of(table, a):
             return table[a].rearrange("p t i -> p (t i)").bitcast(I32)
@@ -79,24 +82,27 @@ def tile_list_memory_kv_swiglu_kernel(tc, tab_words, tab_scales, tab2_words, tab
         load_planes(nc.sync, key_scale_tab, tab_scales)
         nc.sync.dma_start(out=key_tab[:].bitcast(I32), in_=words_of(tab_words, 0))
         nc.sync.dma_start(val_list[:], offs2)
-        load_planes(nc.scalar, wk_scale_raw, wk_scales)
+        load_planes(nc.sync, wk_scale_raw, wk_scales)
         nc.sync.dma_start(out=val_tab[0][:].bitcast(I32), in_=words_of(tab2_words, 0))
         load_planes(nc.sync, val_scale_tab, tab2_scales)
-        load_wv(0, 0, 0, 256)
-        load_wv(0, 0, 256, 256)
+        load_wv(0, 0, 0, PASS)
         load_wv(1, 0, 0, PASS)
         nc.sync.dma_start(out=val_tab[1][:].bitcast(I32), in_=words_of(tab2_words, 1))
         load_wv(0, 1, 0, PASS)
-        load_wv(1, 1, 0, 256)
-        load_wv(1, 1, 256, 256)
-        for c in range(N // WD_COLS):
+        load_wv(1, 1, 0, PASS)
+        for c0, chunks in ((0, 3),):
             for b in range(2):
-                load_wd(b, c)
+                load_wd(b, c0, chunks)
 
-        def gather(window, lst, dtype, name, u):
-            picked = held([P, HALF], dtype, "%s%d" % (name, u))
+        def gather(window, lst, dtype, name, u, tag=None):
+            picked = keep.tile([P, HALF], dtype, name="%s%d" % (name, u), tag=tag or "%s%d" % (name, u), align_bytes=64)
             nc.vector.tensor_copy(out=picked[:], in_=window[:].indirect(lst[:, u * HALF // 16:(u + 1) * HALF // 16]))
-            return picked
+            return picked[:]
+
+        def gather_all(window, lst, dtype, name):
+            picked = held([P, S], dtype, name)
+            nc.vector.tensor_copy(out=picked[:], in_=window[:].indirect(lst[:]))
+            return [picked[:, :HALF], picked[:, HALF:]]
 
         def copy_on(engine, dst, src):
             if engine == "scalar":
@@ -112,8 +118,8 @@ def tile_list_memory_kv_swiglu_kernel(tc, tab_words, tab_scales, tab2_words, tab
             if (a, b) not in wv_bf:
                 wv_bf[a, b] = stage.tile([P, PACK, P, PACK], BF16, name="wv_bf", bufs=4, align_bytes=64)
             q0 = c0 // PACK
-            dst = wv_bf[a, b][:, :, q0:q0 + width // PACK, :].rearrange("p t q i -> p q i t")
-            copy_on(engine, dst, wv_raw[a, b, c0][:].rearrange("p i (q t) -> p q i t", t=PACK))
+            dst = wv_bf[a, b][:, :, q0:q0 + width // PACK, :].rearrange("p t (m e) i -> p m t i e", e=4)
+            copy_on(engine, dst, wv_raw[a, b, c0][:].rearrange("p i (m t e) -> p m t i e", t=PACK, e=4))
 
         def quantize(src, width, name):
             codes = held([P, width], U32, name + "_codes")
@@ -125,15 +131,18 @@ def tile_list_memory_kv_swiglu_kernel(tc, tab_words, tab_scales, tab2_words, tab
             wv_codes[a, b], wv_planes[a, b] = quantize(
                 wv_bf[a, b][:].rearrange("p t q i -> p (t q i)"), PASS, "wv%d%d" % (a, b))
 
-        key_planes = [gather(key_scale_tab, key_list, U8, "key_plane", u) for u in range(2)]
+        key_planes = gather_all(key_scale_tab, key_list, U8, "key_plane")
         wk_codes = held([P, 2 * H], U8, "wk_codes")
         wk_plane = held([P, H], U8, "wk_plane")
         nc.vector.tensor_copy(
-            out=wk_codes[:].bitcast(U16).rearrange("p (b t q) -> p b q t", b=2, t=PACK),
-            in_=wk_raw[:].bitcast(U16).rearrange("p (b q t) -> p b q t", b=2, t=PACK))
+            out=wk_codes[:].bitcast(I32).rearrange("p (b t m w) -> p b t m w", b=2, t=PACK, w=2),
+            in_=wk_raw[:].rearrange("p (b m t w) -> p b t m w", b=2, t=PACK, w=2))
         nc.vector.tensor_copy(
-            out=wk_plane[:].rearrange("p (b t q) -> p b q t", b=2, t=PACK),
-            in_=wk_scale_raw[:].rearrange("p (b q t) -> p b q t", b=2, t=PACK))
+            out=wk_plane[:].bitcast(I32).rearrange("p (b t m) -> p b t m", b=2, t=PACK),
+            in_=wk_scale_raw[:].bitcast(I32).rearrange("p (b m t) -> p b t m", b=2, t=PACK))
+
+        def raw_room(raw, part):
+            return raw.rearrange("p i r -> p (i r)")[:, part * PASS:(part + 1) * PASS]
 
         gates = {}
 
@@ -193,13 +202,13 @@ def tile_list_memory_kv_swiglu_kernel(tc, tab_words, tab_scales, tab2_words, tab
         def cast_wd(b, c, engine):
             wd_bf[b, c] = stage.tile([P, WD_COLS, PACK], BF16, name="wd_bf", bufs=6, align_bytes=64)
             copy_on(engine, wd_bf[b, c][:].rearrange("p (m e) i -> p m i e", e=4),
-                    wd_raw[b, c][:].rearrange("p i (m e) -> p m i e", e=4))
+                    wd_raw[b, c].rearrange("p i (m e) -> p m i e", e=4))
 
         def quantize_wd(b, c):
             wd_codes[b, c], wd_planes[b, c] = quantize(
                 wd_bf[b, c][:].rearrange("p n i -> p (n i)"), WD_COLS, "wd%d%d" % (b, c))
 
-        def project(c, jp, engine):
+        def project(c, jp, engine, room=None):
             bank = psum.tile([P, 2, PAIR], F32, name="side_bank", bufs=3)
             for v in range(2):
                 for b in range(2):
@@ -208,10 +217,12 @@ def tile_list_memory_kv_swiglu_kernel(tc, tab_words, tab_scales, tab2_words, tab
                                         lhsT_scale=wd_planes[b, c][:, v * P:(v + 1) * P],
                                         rhs=h_codes[b, jp][:].bitcast(FP8X4), rhs_scale=h_planes[b, jp][:],
                                         start=(b == 0), stop=(b == 1))
-            result = stage.tile([P, 2, PAIR], F32, name="result", bufs=6)
-            copy_on(engine, result[:], bank[:])
+            if room is None:
+                room = stage.tile([P, 2 * PAIR], F32, name="result", bufs=6)[:]
+            result = room.rearrange("p (v j) -> p v j", v=2)
+            copy_on(engine, result, bank[:])
             rows = out[c * WD_COLS:(c + 1) * WD_COLS, jp * PAIR:(jp + 1) * PAIR]
-            nc.sync.dma_start(out=rows.rearrange("(v p) j -> p v j", p=P), in_=result[:])
+            nc.sync.dma_start(out=rows.rearrange("(v p) j -> p v j", p=P), in_=result)
 
         def project_chunk(g, jc, engine):
             jp, e = divmod(jc, 2)
@@ -229,76 +240,83 @@ def tile_list_memory_kv_swiglu_kernel(tc, tab_words, tab_scales, tab2_words, tab
             rows = out[3 * g * P:3 * (g + 1) * P, jc * CHUNK:(jc + 1) * CHUNK]
             nc.sync.dma_start(out=rows.rearrange("(w p) j -> p w j", p=P), in_=result[:])
 
-        key_codes = [gather(key_tab, key_list, U32, "key_codes", u) for u in range(2)]
-        val_planes = [gather(val_scale_tab, val_list, U8, "val_plane", u) for u in range(2)]
-        val_codes = [[gather(val_tab[0], val_list, U32, "val_codes0", u) for u in range(2)]]
-        cast_wv(0, 0, 0, 256, "scalar")
-        cast_wv(0, 0, 256, 256, "vector")
+        key_codes = [gather(key_tab, key_list, U32, "key_codes", 0)]
+        key_codes.append(gather(key_tab, key_list, U32, "key_codes", 1, "wk_scale_raw"))
+        val_codes = [gather_all(val_tab[0], val_list, U32, "val_codes0")]
+        val_planes = gather_all(val_scale_tab, val_list, U8, "val_plane")
+        cast_wv(0, 0, 0, PASS, "vector")
         cast_wv(1, 0, 0, PASS, "vector")
         quantize_wv(0, 0)
         quantize_wv(1, 0)
         val_codes.append([gather(val_tab[1], val_list, U32, "val_codes1", u) for u in range(2)])
-        for jc in range(8):
-            gate(0, jc)
         cast_wv(0, 1, 0, PASS, "scalar")
-        cast_wv(1, 1, 0, 256, "scalar")
-        cast_wv(1, 1, 256, 256, "vector")
-        for jc in range(4):
-            gate(1, jc)
-        raw_room = wv_raw[1, 1, 0][:].rearrange("p i r -> p (i r)")
-        for jc in range(4, 6):
-            gate(1, jc, raw_room[:, (jc - 4) * CHUNK * PACK:(jc - 3) * CHUNK * PACK])
-        raw_room = wv_raw[1, 1, 256][:].rearrange("p i r -> p (i r)")
-        for jc in range(6, 8):
-            gate(1, jc, raw_room[:, (jc - 6) * CHUNK * PACK:(jc - 5) * CHUNK * PACK])
+        cast_wv(1, 1, 0, PASS, "scalar")
+        gate(0, 0)
+        gate(0, 1)
+        gate(0, 2)
+        gate(0, 3)
+        gate(0, 4)
+        gate(0, 5)
+        gate(0, 6)
+        gate(0, 7)
+        gate(1, 0)
+        gate(1, 1)
+        gate(1, 2)
+        gate(1, 3)
+        gate(1, 4)
+        gate(1, 5)
+        gate(1, 6)
+        gate(1, 7)
         quantize_wv(0, 1)
         quantize_wv(1, 1)
-        wv_room = wv_bf[1, 1][:].rearrange("p t q i -> p (t q i)")
-        for b in range(2):
-            cast_wd(b, 0, "scalar")
-            quantize_wd(b, 0)
+        cast_wd(0, 0, "scalar")
+        cast_wd(0, 1, "scalar")
+        cast_wd(0, 2, "scalar")
+        cast_wd(1, 0, "scalar")
+        cast_wd(1, 1, "scalar")
+        cast_wd(1, 2, "scalar")
         hidden(0, 0)
         hidden(0, 1)
-        hidden(0, 2, wv_room[:, :PAIR * PACK])
+        hidden(0, 2)
         quantize_h(0, 0)
         hidden(0, 3)
-        hidden(1, 0)
+        hidden(0, 4, wv_bf[1, 1][:].rearrange("p t q i -> p (t q i)")[:, 0 * PAIR * PACK:1 * PAIR * PACK])
         quantize_h(0, 1)
-        hidden(1, 1)
-        for b in range(2):
-            cast_wd(b, 1, "scalar")
-            quantize_wd(b, 1)
-        hidden(1, 2)
-        quantize_h(1, 0)
-        project(0, 0, "scalar")
-        hidden(1, 3)
-        hidden(0, 4, wv_room[:, PAIR * PACK:])
-        quantize_h(1, 1)
-        project(1, 0, "scalar")
         hidden(0, 5)
-        for b in range(2):
-            cast_wd(b, 2, "scalar")
-            quantize_wd(b, 2)
-        hidden(1, 4, wd_bf[1, 1][:].rearrange("p n i -> p (n i)"))
+        hidden(1, 0)
         quantize_h(0, 2)
-        project(0, 1, "scalar")
+        hidden(1, 1)
+        quantize_wd(0, 0)
+        quantize_wd(0, 1)
+        quantize_wd(0, 2)
+        quantize_h(1, 0)
+        quantize_wd(1, 0)
+        hidden(1, 2, wd_bf[1, 0][:].rearrange("p n i -> p (n i)"))
+        quantize_wd(1, 1)
+        hidden(1, 3)
+        quantize_wd(1, 2)
+        quantize_h(1, 1)
+        hidden(1, 4, wd_bf[1, 1][:].rearrange("p n i -> p (n i)"))
         hidden(1, 5)
-        project(1, 1, "scalar")
-        hidden(0, 6, wd_bf[0, 1][:].rearrange("p n i -> p (n i)"))
+        hidden(0, 6, wd_bf[1, 2][:].rearrange("p n i -> p (n i)"))
         quantize_h(1, 2)
-        project(2, 0, "scalar")
-        project(2, 1, "scalar")
-        hidden(1, 6, wd_bf[1, 2][:].rearrange("p n i -> p (n i)"))
+        hidden(1, 6)
         quantize_h_chunk(0, 6)
-        project(0, 2, "scalar")
         hidden(0, 7)
         quantize_h_chunk(1, 6)
-        project(1, 2, "scalar")
         hidden(1, 7)
         quantize_h_chunk(0, 7)
         quantize_h_chunk(1, 7)
+        project(0, 0, "scalar")
+        project(1, 0, "scalar")
+        project(2, 0, "scalar")
+        project(0, 1, "scalar")
+        project(1, 1, "scalar")
+        project(2, 1, "scalar")
+        project(0, 2, "scalar")
+        project(1, 2, "scalar")
         project(2, 2, "scalar")
         project_chunk(0, 6, "scalar")
-        project_chunk(1, 6, "vector")
+        project_chunk(1, 6, "scalar")
         project_chunk(0, 7, "vector")
         project_chunk(1, 7, "scalar")

@@ -22,15 +22,18 @@ PASS = P * PACK
 HALF = S // 2
 CHUNK = 128
 PAIR = 2 * CHUNK
+VAL_ROW = 8
 WD_COLS = 256
+SIDE_BANKS = 3
+H_BUFS = 4
+RESULT_BUFS = 6
 
 
 def tile_list_memory_kv_swiglu_kernel(tc, tab_words, tab_scales, tab2_words, tab2_scales, offs, offs2,
-                                               wk_words, wk_scales, wv, wd, out):
+                                                   wk_words, wk_scales, wv, wd, out):
     nc = tc.nc
     with ExitStack() as ctx:
         keep = ctx.enter_context(tc.tile_pool(name="keep", bufs=1))
-        stage = ctx.enter_context(tc.tile_pool(name="stage", bufs=3))
         psum = ctx.enter_context(tc.psum_pool(name="psum", bufs=1))
 
         def held(shape, dtype, name):
@@ -46,18 +49,12 @@ def tile_list_memory_kv_swiglu_kernel(tc, tab_words, tab_scales, tab2_words, tab
         val_tab = [held([P, T2], U32, "val_tab%d" % a) for a in range(2)]
         wv_raw = {}
         wd_raw = {}
+        wd_tiles = {}
 
-        nc.vector.memset(key_scale_tab[:, :T // 2].bitcast(I32), 0)
-        nc.gpsimd.memset(key_scale_tab[:, T // 2:].bitcast(I32), 0)
-        nc.vector.memset(wk_scale_raw[:].bitcast(I32), 0)
-        nc.gpsimd.memset(val_scale_tab[:, :T2 // 2].bitcast(I32), 0)
-        nc.vector.memset(val_scale_tab[:, T2 // 2:].bitcast(I32), 0)
-
-        def load_wv(a, b, c0, width):
-            raw = held([P, PACK, width], F32, "wv_raw%d%d%d" % (a, b, c0))
-            rows = wv[a * PASS:(a + 1) * PASS, b * PASS + c0:b * PASS + c0 + width]
-            nc.sync.dma_start(out=raw[:], in_=rows.rearrange("(p i) r -> p i r", i=PACK))
-            wv_raw[a, b, c0] = raw
+        def load_wv(a, b):
+            wv_raw[a, b] = held([P, PACK, PASS], F32, "wv_raw%d%d" % (a, b))
+            rows = wv[a * PASS:(a + 1) * PASS, b * PASS:(b + 1) * PASS]
+            nc.sync.dma_start(out=wv_raw[a, b][:], in_=rows.rearrange("(p i) r -> p i r", i=PACK))
 
         def load_wd(b, c0, chunks):
             raw = held([P, PACK, chunks * WD_COLS], F32, "wd_raw%d%d" % (b, c0))
@@ -65,48 +62,32 @@ def tile_list_memory_kv_swiglu_kernel(tc, tab_words, tab_scales, tab2_words, tab
             rows = rows.rearrange("(m t e) n -> t m e n", t=PACK, e=4)
             for t in range(PACK):
                 nc.sync.dma_start(out=raw[:, t, :], in_=rows[t])
+            wd_tiles[b, c0] = raw
             for c in range(chunks):
                 wd_raw[b, c0 + c] = raw[:, :, c * WD_COLS:(c + 1) * WD_COLS]
 
-        def words_of(table, a):
-            return table[a].rearrange("p t i -> p (t i)").bitcast(I32)
+        def load_words(tile, table, a):
+            nc.sync.dma_start(out=tile[:].bitcast(I32), in_=table[a].rearrange("p t i -> p (t i)").bitcast(I32))
 
-        def load_planes(queue, plane, scales):
-            passes = scales.shape[0]
+        def load_plane(queue, plane, scales):
+            for r in range(4):
+                queue.dma_start(out=plane[r:P:32, :].bitcast(I32), in_=scales[0, r:16:4, :].bitcast(I32))
+
+        def load_val_planes(queue):
             for q in range(4):
-                queue.dma_start(out=plane[32 * q:32 * q + 4 * passes, :].bitcast(I32),
-                                in_=scales[:, 4 * q:4 * q + 4, :].bitcast(I32))
+                queue.dma_start(out=val_scale_tab[32 * q + VAL_ROW:32 * q + VAL_ROW + 8, :].bitcast(I32),
+                                in_=tab2_scales[:, 4 * q:4 * q + 4, :].bitcast(I32))
 
-        nc.sync.dma_start(key_list[:], offs)
-        nc.sync.dma_start(out=wk_raw[:], in_=wk_words[0].bitcast(I32))
-        load_planes(nc.sync, key_scale_tab, tab_scales)
-        nc.sync.dma_start(out=key_tab[:].bitcast(I32), in_=words_of(tab_words, 0))
-        nc.sync.dma_start(val_list[:], offs2)
-        load_planes(nc.sync, wk_scale_raw, wk_scales)
-        nc.sync.dma_start(out=val_tab[0][:].bitcast(I32), in_=words_of(tab2_words, 0))
-        load_planes(nc.sync, val_scale_tab, tab2_scales)
-        load_wv(0, 0, 0, PASS)
-        load_wv(1, 0, 0, PASS)
-        nc.sync.dma_start(out=val_tab[1][:].bitcast(I32), in_=words_of(tab2_words, 1))
-        load_wv(0, 1, 0, PASS)
-        load_wv(1, 1, 0, PASS)
-        for c0, chunks in ((0, 3),):
-            for b in range(2):
-                load_wd(b, c0, chunks)
-
-        def gather(window, lst, dtype, name, u, tag=None):
-            picked = keep.tile([P, HALF], dtype, name="%s%d" % (name, u), tag=tag or "%s%d" % (name, u), align_bytes=64)
-            nc.vector.tensor_copy(out=picked[:], in_=window[:].indirect(lst[:, u * HALF // 16:(u + 1) * HALF // 16]))
-            return picked[:]
-
-        def gather_all(window, lst, dtype, name):
-            picked = held([P, S], dtype, name)
-            nc.vector.tensor_copy(out=picked[:], in_=window[:].indirect(lst[:]))
-            return [picked[:, :HALF], picked[:, HALF:]]
+        def gather(window, lst, dtype, name, u0, u1, tag=None):
+            picked = keep.tile([P, (u1 - u0) * HALF], dtype, name=name, tag=tag or name, align_bytes=64)
+            nc.vector.tensor_copy(out=picked[:], in_=window[:].indirect(lst[:, u0 * HALF // 16:u1 * HALF // 16]))
+            return [picked[:, w * HALF:(w + 1) * HALF] for w in range(u1 - u0)]
 
         def copy_on(engine, dst, src):
             if engine == "scalar":
                 nc.scalar.copy(out=dst, in_=src)
+            elif engine == "gpsimd":
+                nc.gpsimd.tensor_scalar(out=dst, in0=src, scalar1=1.0, scalar2=0.0, op0=MULT, op1=mybir.AluOpType.add)
             else:
                 nc.vector.tensor_copy(out=dst, in_=src)
 
@@ -114,48 +95,54 @@ def tile_list_memory_kv_swiglu_kernel(tc, tab_words, tab_scales, tab2_words, tab
         wv_codes = {}
         wv_planes = {}
 
-        def cast_wv(a, b, c0, width, engine):
-            if (a, b) not in wv_bf:
-                wv_bf[a, b] = stage.tile([P, PACK, P, PACK], BF16, name="wv_bf", bufs=4, align_bytes=64)
-            q0 = c0 // PACK
-            dst = wv_bf[a, b][:, :, q0:q0 + width // PACK, :].rearrange("p t (m e) i -> p m t i e", e=4)
-            copy_on(engine, dst, wv_raw[a, b, c0][:].rearrange("p i (m t e) -> p m t i e", t=PACK, e=4))
+        def cast_wv(a, b, engine, t0=0, t1=PACK):
+            if t0 == 0:
+                wv_bf[a, b] = held([P, PACK, P, PACK], BF16, "wv_bf%d%d" % (a, b))
+            dst = wv_bf[a, b][:, t0:t1, :, :].rearrange("p t (m e) i -> p m t i e", e=4)
+            src = wv_raw[a, b][:].rearrange("p i (m t e) -> p m t i e", t=PACK, e=4)[:, :, t0:t1, :, :]
+            copy_on(engine, dst, src)
 
-        def quantize(src, width, name):
-            codes = held([P, width], U32, name + "_codes")
-            plane = held([P, width], U8, name + "_plane")
-            nc.vector.quantize_mx(out=codes[:].bitcast(FP8X4), scales=plane[:], in_=src)
-            return codes, plane
+        def quantize(codes, plane, src):
+            nc.vector.quantize_mx(out=codes.bitcast(FP8X4), scales=plane, in_=src)
 
-        def quantize_wv(a, b):
-            wv_codes[a, b], wv_planes[a, b] = quantize(
-                wv_bf[a, b][:].rearrange("p t q i -> p (t q i)"), PASS, "wv%d%d" % (a, b))
+        def quantize_wv(a, b, t0=0, t1=PACK):
+            if t0 == 0:
+                wv_codes[a, b] = held([P, PASS], U32, "wv_codes%d%d" % (a, b))
+                wv_planes[a, b] = held([P, PASS], U8, "wv_plane%d%d" % (a, b))
+            quantize(wv_codes[a, b][:, t0 * P:t1 * P], wv_planes[a, b][:, t0 * P:t1 * P],
+                     wv_bf[a, b][:, t0:t1, :, :].rearrange("p t q i -> p (t q i)"))
 
-        key_planes = gather_all(key_scale_tab, key_list, U8, "key_plane")
         wk_codes = held([P, 2 * H], U8, "wk_codes")
         wk_plane = held([P, H], U8, "wk_plane")
-        nc.vector.tensor_copy(
-            out=wk_codes[:].bitcast(I32).rearrange("p (b t m w) -> p b t m w", b=2, t=PACK, w=2),
-            in_=wk_raw[:].rearrange("p (b m t w) -> p b t m w", b=2, t=PACK, w=2))
-        nc.vector.tensor_copy(
-            out=wk_plane[:].bitcast(I32).rearrange("p (b t m) -> p b t m", b=2, t=PACK),
-            in_=wk_scale_raw[:].bitcast(I32).rearrange("p (b m t) -> p b t m", b=2, t=PACK))
 
-        def raw_room(raw, part):
-            return raw.rearrange("p i r -> p (i r)")[:, part * PASS:(part + 1) * PASS]
+        def deal_wk_words(engine):
+            engine.tensor_copy(
+                out=wk_codes[:].bitcast(I32).rearrange("p (b t m w) -> p b t m w", b=2, t=PACK, w=2),
+                in_=wk_raw[:].rearrange("p (b m t w) -> p b t m w", b=2, t=PACK, w=2))
+
+        def deal_wk_scales(engine):
+            engine.tensor_copy(
+                out=wk_plane[:].bitcast(I32).rearrange("p (b t m) -> p b t m", b=2, t=PACK),
+                in_=wk_scale_raw[:].bitcast(I32).rearrange("p (b m t) -> p b t m", b=2, t=PACK))
+
+        def side_bank(shape):
+            return psum.tile(shape, F32, name="side_bank", bufs=SIDE_BANKS)
+
+        def val_bank(shape):
+            return psum.tile(shape, F32, name="val_bank", bufs=8 - SIDE_BANKS)
 
         gates = {}
 
         def gate(b, jc, room=None):
-            u, cols = divmod(jc * CHUNK, HALF)
-            cols = slice(cols, cols + CHUNK)
-            bank = psum.tile([P, PACK, CHUNK], F32, name="side_bank", bufs=3)
+            u, c0 = divmod(jc * CHUNK, HALF)
+            bank = side_bank([P, PACK, CHUNK])
             for t in range(PACK):
                 r0 = b * PASS + t * P
                 nc.tensor.matmul_mx(out=bank[:, t, :],
                                     lhsT=wk_codes[:, 2 * r0:2 * (r0 + P)].bitcast(FP4X4),
                                     lhsT_scale=wk_plane[:, r0:r0 + P],
-                                    rhs=key_codes[u][:, cols].bitcast(FP8X4), rhs_scale=key_planes[u][:, cols],
+                                    rhs=key_codes[u][:, c0:c0 + CHUNK].bitcast(FP8X4),
+                                    rhs_scale=key_planes[u][:, c0:c0 + CHUNK],
                                     start=True, stop=True)
             if room is None:
                 room = held([P, CHUNK * PACK], F32, "gate%d%d" % (b, jc))[:]
@@ -163,160 +150,148 @@ def tile_list_memory_kv_swiglu_kernel(tc, tab_words, tab_scales, tab2_words, tab
             nc.scalar.activation(out=gates[b, jc], in_=bank[:].rearrange("p t j -> p j t"), func=SILU)
 
         h_bf = {}
-        h_codes = {}
-        h_planes = {}
+        h_codes = {(b, u): held([P, HALF], U32, "h_codes%d%d" % (b, u)) for b in range(2) for u in range(2)}
+        h_planes = {(b, u): held([P, HALF], U8, "h_plane%d%d" % (b, u)) for b in range(2) for u in range(2)}
+        val_banks = {}
+
+        def values(b, jc, a):
+            u, c0 = divmod(jc * CHUNK, HALF)
+            if a == 0:
+                val_banks[b, jc] = val_bank([P, PACK, CHUNK])
+            for t in range(PACK):
+                nc.tensor.matmul_mx(out=val_banks[b, jc][:, t, :],
+                                    lhsT=wv_codes[a, b][:, t * P:(t + 1) * P].bitcast(FP8X4),
+                                    lhsT_scale=wv_planes[a, b][:, t * P:(t + 1) * P],
+                                    rhs=val_codes[a][u][:, c0:c0 + CHUNK].bitcast(FP8X4),
+                                    rhs_scale=val_planes[u][VAL_ROW + 4 * a:, c0:c0 + CHUNK],
+                                    start=(a == 0 and t == 0), stop=(a == 1 and t == PACK - 1))
 
         def hidden(b, jc, room=None):
-            u, cols = divmod(jc * CHUNK, HALF)
-            cols = slice(cols, cols + CHUNK)
-            bank = psum.tile([P, PACK, CHUNK], F32, name="val_bank", bufs=5)
-            for t in range(PACK):
-                for a in range(2):
-                    nc.tensor.matmul_mx(out=bank[:, t, :],
-                                        lhsT=wv_codes[a, b][:, t * P:(t + 1) * P].bitcast(FP8X4),
-                                        lhsT_scale=wv_planes[a, b][:, t * P:(t + 1) * P],
-                                        rhs=val_codes[a][u][:, cols].bitcast(FP8X4),
-                                        rhs_scale=val_planes[u][4 * a:, cols],
-                                        start=(a == 0), stop=(a == 1))
-            jp, e = divmod(jc, 2)
-            if e == 0:
-                if room is None:
-                    room = stage.tile([P, PAIR * PACK], BF16, name="h_bf", bufs=4, align_bytes=64)[:]
-                h_bf[b, jp] = room
-            nc.vector.tensor_tensor(out=h_bf[b, jp].rearrange("p (e j t) -> p e j t", e=2, t=PACK)[:, e, :, :], in0=bank[:].rearrange("p t j -> p j t"),
-                                    in1=gates[b, jc], op=MULT)
+            values(b, jc, 0)
+            values(b, jc, 1)
+            if room is None:
+                room = keep.tile([P, CHUNK * PACK], BF16, name="h_bf", bufs=H_BUFS, align_bytes=64)[:]
+            h_bf[b, jc] = room
+            nc.vector.tensor_tensor(out=room.rearrange("p (j t) -> p j t", t=PACK),
+                                    in0=val_banks[b, jc][:].rearrange("p t j -> p j t"), in1=gates[b, jc], op=MULT)
 
-        def quantize_h(b, jp):
-            h_codes[b, jp], h_planes[b, jp] = quantize(
-                h_bf[b, jp], PAIR, "h%d%d" % (b, jp))
+        def quantize_h(b, jc):
+            u, c0 = divmod(jc * CHUNK, HALF)
+            quantize(h_codes[b, u][:, c0:c0 + CHUNK], h_planes[b, u][:, c0:c0 + CHUNK], h_bf[b, jc])
 
-        def quantize_h_chunk(b, jc):
-            jp, e = divmod(jc, 2)
-            h_codes[b, jp, e], h_planes[b, jp, e] = quantize(
-                h_bf[b, jp][:, e * CHUNK * PACK:(e + 1) * CHUNK * PACK], CHUNK, "hc%d%d" % (b, jc))
+        def room_in(raw, k):
+            return raw[:].rearrange("p i n -> p (i n)").bitcast(BF16)[:, k * PASS:(k + 1) * PASS]
 
+        wd_bf = {}
         wd_codes = {}
         wd_planes = {}
-        wd_bf = {}
 
-        def cast_wd(b, c, engine):
-            wd_bf[b, c] = stage.tile([P, WD_COLS, PACK], BF16, name="wd_bf", bufs=6, align_bytes=64)
-            copy_on(engine, wd_bf[b, c][:].rearrange("p (m e) i -> p m i e", e=4),
+        def cast_wd(b, c, engine, room=None):
+            if room is None:
+                room = held([P, WD_COLS * PACK], BF16, "wd_bf%d%d" % (b, c))[:]
+            wd_bf[b, c] = room
+            copy_on(engine, room.rearrange("p (m e i) -> p m i e", e=4, i=PACK),
                     wd_raw[b, c].rearrange("p i (m e) -> p m i e", e=4))
 
         def quantize_wd(b, c):
-            wd_codes[b, c], wd_planes[b, c] = quantize(
-                wd_bf[b, c][:].rearrange("p n i -> p (n i)"), WD_COLS, "wd%d%d" % (b, c))
+            wd_codes[b, c] = held([P, WD_COLS], U32, "wd_codes%d%d" % (b, c))
+            wd_planes[b, c] = held([P, WD_COLS], U8, "wd_plane%d%d" % (b, c))
+            quantize(wd_codes[b, c][:], wd_planes[b, c][:], wd_bf[b, c])
 
-        def project(c, jp, engine, room=None):
-            bank = psum.tile([P, 2, PAIR], F32, name="side_bank", bufs=3)
-            for v in range(2):
-                for b in range(2):
-                    nc.tensor.matmul_mx(out=bank[:, v, :],
-                                        lhsT=wd_codes[b, c][:, v * P:(v + 1) * P].bitcast(FP8X4),
-                                        lhsT_scale=wd_planes[b, c][:, v * P:(v + 1) * P],
-                                        rhs=h_codes[b, jp][:].bitcast(FP8X4), rhs_scale=h_planes[b, jp][:],
-                                        start=(b == 0), stop=(b == 1))
+        def project(v0, nv, j0, width, engine, bank_of, room=None):
+            u, c0 = divmod(j0, HALF)
+            bank = bank_of([P, nv, width])
+            for b in range(2):
+                for w in range(nv):
+                    c, n0 = divmod((v0 + w) * P, WD_COLS)
+                    nc.tensor.matmul_mx(out=bank[:, w, :],
+                                        lhsT=wd_codes[b, c][:, n0:n0 + P].bitcast(FP8X4),
+                                        lhsT_scale=wd_planes[b, c][:, n0:n0 + P],
+                                        rhs=h_codes[b, u][:, c0:c0 + width].bitcast(FP8X4),
+                                        rhs_scale=h_planes[b, u][:, c0:c0 + width],
+                                        start=(b == 0 and w == 0), stop=(b == 1 and w == nv - 1))
             if room is None:
-                room = stage.tile([P, 2 * PAIR], F32, name="result", bufs=6)[:]
-            result = room.rearrange("p (v j) -> p v j", v=2)
+                room = keep.tile([P, nv * width], F32, name="result", bufs=RESULT_BUFS)[:]
+            result = room.rearrange("p (v j) -> p v j", v=nv)
             copy_on(engine, result, bank[:])
-            rows = out[c * WD_COLS:(c + 1) * WD_COLS, jp * PAIR:(jp + 1) * PAIR]
+            rows = out[v0 * P:(v0 + nv) * P, j0:j0 + width]
             nc.sync.dma_start(out=rows.rearrange("(v p) j -> p v j", p=P), in_=result)
 
-        def project_chunk(g, jc, engine):
-            jp, e = divmod(jc, 2)
-            bank = psum.tile([P, 3, CHUNK], F32, name="side_bank", bufs=3)
-            for w in range(3):
-                c, v = divmod(3 * g + w, 2)
-                for b in range(2):
-                    nc.tensor.matmul_mx(out=bank[:, w, :],
-                                        lhsT=wd_codes[b, c][:, v * P:(v + 1) * P].bitcast(FP8X4),
-                                        lhsT_scale=wd_planes[b, c][:, v * P:(v + 1) * P],
-                                        rhs=h_codes[b, jp, e][:].bitcast(FP8X4), rhs_scale=h_planes[b, jp, e][:],
-                                        start=(b == 0), stop=(b == 1))
-            result = stage.tile([P, 3, CHUNK], F32, name="result", bufs=6)
-            copy_on(engine, result[:], bank[:])
-            rows = out[3 * g * P:3 * (g + 1) * P, jc * CHUNK:(jc + 1) * CHUNK]
-            nc.sync.dma_start(out=rows.rearrange("(w p) j -> p w j", p=P), in_=result[:])
-
-        key_codes = [gather(key_tab, key_list, U32, "key_codes", 0)]
-        key_codes.append(gather(key_tab, key_list, U32, "key_codes", 1, "wk_scale_raw"))
-        val_codes = [gather_all(val_tab[0], val_list, U32, "val_codes0")]
-        val_planes = gather_all(val_scale_tab, val_list, U8, "val_plane")
-        cast_wv(0, 0, 0, PASS, "vector")
-        cast_wv(1, 0, 0, PASS, "vector")
-        quantize_wv(0, 0)
-        quantize_wv(1, 0)
-        val_codes.append([gather(val_tab[1], val_list, U32, "val_codes1", u) for u in range(2)])
-        cast_wv(0, 1, 0, PASS, "scalar")
-        cast_wv(1, 1, 0, PASS, "scalar")
-        gate(0, 0)
-        gate(0, 1)
-        gate(0, 2)
-        gate(0, 3)
-        gate(0, 4)
-        gate(0, 5)
-        gate(0, 6)
-        gate(0, 7)
-        gate(1, 0)
-        gate(1, 1)
-        gate(1, 2)
-        gate(1, 3)
-        gate(1, 4)
-        gate(1, 5)
-        gate(1, 6)
-        gate(1, 7)
+        nc.vector.memset(key_scale_tab[:, :T // 2].bitcast(I32), 0)
+        nc.gpsimd.memset(key_scale_tab[:, T // 2:].bitcast(I32), 0)
+        nc.vector.memset(val_scale_tab[:, :T2 // 2].bitcast(I32), 0)
+        nc.gpsimd.memset(val_scale_tab[:, T2 // 2:].bitcast(I32), 0)
+        nc.vector.memset(wk_scale_raw[:].bitcast(I32), 0)
+        nc.sync.dma_start(key_list[:], offs)
+        load_words(key_tab, tab_words, 0)
+        load_plane(nc.sync, key_scale_tab, tab_scales)
+        nc.sync.dma_start(out=wk_raw[:], in_=wk_words[0].bitcast(I32))
+        nc.sync.dma_start(val_list[:], offs2)
+        load_plane(nc.sync, wk_scale_raw, wk_scales)
+        load_words(val_tab[0], tab2_words, 0)
+        load_val_planes(nc.sync)
+        load_wv(0, 0)
+        load_wv(1, 0)
+        load_words(val_tab[1], tab2_words, 1)
+        load_wv(0, 1)
+        load_wv(1, 1)
+        for c0, chunks in ((0, 1), (1, 2)):
+            for b in range(2):
+                load_wd(b, c0, chunks)
+        key_codes = gather(key_tab, key_list, U32, "key_codes", 0, 2)
+        key_planes = gather(key_scale_tab, key_list, U8, "key_plane0", 0, 1)
+        deal_wk_words(nc.vector)
+        deal_wk_scales(nc.vector)
+        key_planes += gather(key_scale_tab, key_list, U8, "key_plane1", 1, 2, "wk_scale_raw")
+        for jc in range(8):
+            gate(0, jc)
+        val_codes = [gather(val_tab[0], val_list, U32, "val_codes0", 0, 2)]
+        val_planes = gather(val_scale_tab, val_list, U8, "val_plane", 0, 2)
+        for a in range(2):
+            for t0 in (0, 2):
+                cast_wv(a, 0, "vector", t0, t0 + 2)
+            for t0 in (0, 2):
+                quantize_wv(a, 0, t0, t0 + 2)
+        for jc in range(8):
+            gate(1, jc)
+        val_codes.append(gather(val_tab[1], val_list, U32, "val_codes10", 0, 1) + gather(val_tab[1], val_list, U32, "val_codes11", 1, 2))
+        cast_wv(0, 1, "scalar")
+        cast_wv(1, 1, "scalar")
+        def step(b, jc, room=None):
+            hidden(b, jc, room)
+            if (b, jc) != (0, 0):
+                quantize_h(*divmod(8 * b + jc - 1, 8))
+        for jc in range(4):
+            step(0, jc)
         quantize_wv(0, 1)
+        for jc in (4, 5):
+            step(0, jc, room_in(wv_raw[0, 1], jc))
         quantize_wv(1, 1)
-        cast_wd(0, 0, "scalar")
-        cast_wd(0, 1, "scalar")
-        cast_wd(0, 2, "scalar")
-        cast_wd(1, 0, "scalar")
-        cast_wd(1, 1, "scalar")
-        cast_wd(1, 2, "scalar")
-        hidden(0, 0)
-        hidden(0, 1)
-        hidden(0, 2)
-        quantize_h(0, 0)
-        hidden(0, 3)
-        hidden(0, 4, wv_bf[1, 1][:].rearrange("p t q i -> p (t q i)")[:, 0 * PAIR * PACK:1 * PAIR * PACK])
-        quantize_h(0, 1)
-        hidden(0, 5)
-        hidden(1, 0)
-        quantize_h(0, 2)
-        hidden(1, 1)
+        for jc in (6, 7):
+            step(0, jc, room_in(wv_raw[1, 1], jc))
+        for c0, chunks in ((0, 1), (1, 2)):
+            for b in range(2):
+                for c in range(c0, c0 + chunks):
+                    cast_wd(b, c, "scalar")
         quantize_wd(0, 0)
+        quantize_wd(1, 0)
+        for jc in (0, 1):
+            step(1, jc, room_in(wd_tiles[1, 0], jc))
         quantize_wd(0, 1)
         quantize_wd(0, 2)
-        quantize_h(1, 0)
-        quantize_wd(1, 0)
-        hidden(1, 2, wd_bf[1, 0][:].rearrange("p n i -> p (n i)"))
+        for jc in (2, 3, 4):
+            step(1, jc, room_in(wd_tiles[0, 1], jc))
         quantize_wd(1, 1)
-        hidden(1, 3)
         quantize_wd(1, 2)
-        quantize_h(1, 1)
-        hidden(1, 4, wd_bf[1, 1][:].rearrange("p n i -> p (n i)"))
-        hidden(1, 5)
-        hidden(0, 6, wd_bf[1, 2][:].rearrange("p n i -> p (n i)"))
-        quantize_h(1, 2)
-        hidden(1, 6)
-        quantize_h_chunk(0, 6)
-        hidden(0, 7)
-        quantize_h_chunk(1, 6)
-        hidden(1, 7)
-        quantize_h_chunk(0, 7)
-        quantize_h_chunk(1, 7)
-        project(0, 0, "scalar")
-        project(1, 0, "scalar")
-        project(2, 0, "scalar")
-        project(0, 1, "scalar")
-        project(1, 1, "scalar")
-        project(2, 1, "scalar")
-        project(0, 2, "scalar")
-        project(1, 2, "scalar")
-        project(2, 2, "scalar")
-        project_chunk(0, 6, "scalar")
-        project_chunk(1, 6, "scalar")
-        project_chunk(0, 7, "vector")
-        project_chunk(1, 7, "scalar")
+        for jc in (5, 6, 7):
+            step(1, jc, room_in(wd_tiles[1, 1], jc))
+        quantize_h(1, 7)
+        def result_room(k):
+            raw = wd_tiles[1, 1] if k < 2 else wv_raw[(k - 2) // 4, (k - 2) // 2 % 2]
+            k = k if k < 2 else k % 2
+            return raw[:].rearrange("p i n -> p (i n)")[:, k * HALF:(k + 1) * HALF]
+        for v in range(6):
+            project(v, 1, 0, HALF, "scalar", side_bank if v % 2 == 0 else val_bank, result_room(v))
+        for jp in (2, 3):
+            for c in range(3):
+                project(2 * c, 2, jp * PAIR, PAIR, "scalar" if (c + jp) % 2 == 0 else "vector", val_bank if c != 1 else side_bank)

@@ -26,7 +26,7 @@ VAL_ROW = 8
 WD_COLS = 256
 SIDE_BANKS = 3
 H_BUFS = 4
-RESULT_BUFS = 6
+RESULT_BUFS = 8
 
 
 def tile_list_memory_kv_swiglu_kernel(tc, tab_words, tab_scales, tab2_words, tab2_scales, offs, offs2,
@@ -49,22 +49,38 @@ def tile_list_memory_kv_swiglu_kernel(tc, tab_words, tab_scales, tab2_words, tab
         val_tab = [held([P, T2], U32, "val_tab%d" % a) for a in range(2)]
         wv_raw = {}
         wd_raw = {}
-        wd_tiles = {}
+
+        KW = 256
+        chain = [held([P, n * KW], F32, "chain%d" % k) for k, n in enumerate((1 + 8, 4 + 8, 4 + 4, 4 + 4, 4 + 8))]
+        raw_place = {("wv", 0, 1): chain[0][:, KW:], ("wv", 1, 1): chain[1][:, 4 * KW:], ("wd", 1, 0): chain[2][:, 4 * KW:],
+                     ("wd", 1, 1): chain[3][:, 4 * KW:], ("wd", 1, 2): chain[4][:, 4 * KW:8 * KW], ("wd", 0, 2): chain[4][:, 8 * KW:]}
+        bf_place = {("wv", 0, 1): chain[1], ("wv", 1, 1): chain[2], ("wd", 0): chain[3], ("wd", 1): chain[4]}
+
+        def raw_tile(key, width):
+            if key not in raw_place:
+                raw_place[key] = held([P, PACK * width], F32, "raw_%s%d%d" % key)[:]
+            return raw_place[key].rearrange("p (i r) -> p i r", i=PACK)
+
+        def bf_tile(key):
+            if key in bf_place:
+                return bf_place[key][:, :4 * KW].bitcast(BF16)
+            return held([P, PACK * PASS], BF16, "bf_" + "".join(str(x) for x in key))[:]
+
+        def chain_room(k):
+            first = 0 if k == 0 else 3 * KW
+            return chain[k][:, first:first + 2 * KW].bitcast(BF16)
 
         def load_wv(a, b):
-            wv_raw[a, b] = held([P, PACK, PASS], F32, "wv_raw%d%d" % (a, b))
+            wv_raw[a, b] = raw_tile(("wv", a, b), PASS)
             rows = wv[a * PASS:(a + 1) * PASS, b * PASS:(b + 1) * PASS]
-            nc.sync.dma_start(out=wv_raw[a, b][:], in_=rows.rearrange("(p i) r -> p i r", i=PACK))
+            nc.sync.dma_start(out=wv_raw[a, b], in_=rows.rearrange("(p i) r -> p i r", i=PACK))
 
-        def load_wd(b, c0, chunks):
-            raw = held([P, PACK, chunks * WD_COLS], F32, "wd_raw%d%d" % (b, c0))
-            rows = wd[b * PASS:(b + 1) * PASS, c0 * WD_COLS:(c0 + chunks) * WD_COLS]
+        def load_wd(b, c):
+            wd_raw[b, c] = raw_tile(("wd", b, c), WD_COLS)
+            rows = wd[b * PASS:(b + 1) * PASS, c * WD_COLS:(c + 1) * WD_COLS]
             rows = rows.rearrange("(m t e) n -> t m e n", t=PACK, e=4)
             for t in range(PACK):
-                nc.sync.dma_start(out=raw[:, t, :], in_=rows[t])
-            wd_tiles[b, c0] = raw
-            for c in range(chunks):
-                wd_raw[b, c0 + c] = raw[:, :, c * WD_COLS:(c + 1) * WD_COLS]
+                nc.sync.dma_start(out=wd_raw[b, c][:, t, :], in_=rows[t])
 
         def load_words(tile, table, a):
             nc.sync.dma_start(out=tile[:].bitcast(I32), in_=table[a].rearrange("p t i -> p (t i)").bitcast(I32))
@@ -96,10 +112,10 @@ def tile_list_memory_kv_swiglu_kernel(tc, tab_words, tab_scales, tab2_words, tab
         wv_planes = {}
 
         def cast_wv(a, b, engine, t0=0, t1=PACK):
-            if t0 == 0:
-                wv_bf[a, b] = held([P, PACK, P, PACK], BF16, "wv_bf%d%d" % (a, b))
+            if (a, b) not in wv_bf:
+                wv_bf[a, b] = bf_tile(("wv", a, b)).rearrange("p (t q i) -> p t q i", t=PACK, i=PACK)
             dst = wv_bf[a, b][:, t0:t1, :, :].rearrange("p t (m e) i -> p m t i e", e=4)
-            src = wv_raw[a, b][:].rearrange("p i (m t e) -> p m t i e", t=PACK, e=4)[:, :, t0:t1, :, :]
+            src = wv_raw[a, b].rearrange("p i (m t e) -> p m t i e", t=PACK, e=4)[:, :, t0:t1, :, :]
             copy_on(engine, dst, src)
 
         def quantize(codes, plane, src):
@@ -169,34 +185,25 @@ def tile_list_memory_kv_swiglu_kernel(tc, tab_words, tab_scales, tab2_words, tab
         def hidden(b, jc, room=None):
             values(b, jc, 0)
             values(b, jc, 1)
-            if room is None:
-                room = keep.tile([P, CHUNK * PACK], BF16, name="h_bf", bufs=H_BUFS, align_bytes=64)[:]
             h_bf[b, jc] = room
             nc.vector.tensor_tensor(out=room.rearrange("p (j t) -> p j t", t=PACK),
                                     in0=val_banks[b, jc][:].rearrange("p t j -> p j t"), in1=gates[b, jc], op=MULT)
 
-        def quantize_h(b, jc):
+        def quantize_h(b, jc, room):
             u, c0 = divmod(jc * CHUNK, HALF)
-            quantize(h_codes[b, u][:, c0:c0 + CHUNK], h_planes[b, u][:, c0:c0 + CHUNK], h_bf[b, jc])
+            width = room.shape[1] // PACK
+            quantize(h_codes[b, u][:, c0:c0 + width], h_planes[b, u][:, c0:c0 + width], room)
 
-        def room_in(raw, k):
-            return raw[:].rearrange("p i n -> p (i n)").bitcast(BF16)[:, k * PASS:(k + 1) * PASS]
+        wd_bf = [bf_tile(("wd", c)).rearrange("p (b n) -> p b n", b=2) for c in range(3)]
+        wd_codes = [held([P, 2 * WD_COLS], U32, "wd_codes%d" % c) for c in range(3)]
+        wd_planes = [held([P, 2 * WD_COLS], U8, "wd_plane%d" % c) for c in range(3)]
 
-        wd_bf = {}
-        wd_codes = {}
-        wd_planes = {}
-
-        def cast_wd(b, c, engine, room=None):
-            if room is None:
-                room = held([P, WD_COLS * PACK], BF16, "wd_bf%d%d" % (b, c))[:]
-            wd_bf[b, c] = room
-            copy_on(engine, room.rearrange("p (m e i) -> p m i e", e=4, i=PACK),
+        def cast_wd(b, c, engine):
+            copy_on(engine, wd_bf[c][:, b, :].rearrange("p (m e i) -> p m i e", e=4, i=PACK),
                     wd_raw[b, c].rearrange("p i (m e) -> p m i e", e=4))
 
-        def quantize_wd(b, c):
-            wd_codes[b, c] = held([P, WD_COLS], U32, "wd_codes%d%d" % (b, c))
-            wd_planes[b, c] = held([P, WD_COLS], U8, "wd_plane%d%d" % (b, c))
-            quantize(wd_codes[b, c][:], wd_planes[b, c][:], wd_bf[b, c])
+        def quantize_wd(c):
+            quantize(wd_codes[c][:], wd_planes[c][:], wd_bf[c].rearrange("p b n -> p (b n)"))
 
         def project(v0, nv, j0, width, engine, bank_of, room=None):
             u, c0 = divmod(j0, HALF)
@@ -204,15 +211,16 @@ def tile_list_memory_kv_swiglu_kernel(tc, tab_words, tab_scales, tab2_words, tab
             for b in range(2):
                 for w in range(nv):
                     c, n0 = divmod((v0 + w) * P, WD_COLS)
+                    n0 = n0 + b * WD_COLS
                     nc.tensor.matmul_mx(out=bank[:, w, :],
-                                        lhsT=wd_codes[b, c][:, n0:n0 + P].bitcast(FP8X4),
-                                        lhsT_scale=wd_planes[b, c][:, n0:n0 + P],
+                                        lhsT=wd_codes[c][:, n0:n0 + P].bitcast(FP8X4),
+                                        lhsT_scale=wd_planes[c][:, n0:n0 + P],
                                         rhs=h_codes[b, u][:, c0:c0 + width].bitcast(FP8X4),
                                         rhs_scale=h_planes[b, u][:, c0:c0 + width],
                                         start=(b == 0 and w == 0), stop=(b == 1 and w == nv - 1))
             if room is None:
-                room = keep.tile([P, nv * width], F32, name="result", bufs=RESULT_BUFS)[:]
-            result = room.rearrange("p (v j) -> p v j", v=nv)
+                room = keep.tile([P, nv, width], F32, name="result", bufs=RESULT_BUFS)[:]
+            result = room
             copy_on(engine, result, bank[:])
             rows = out[v0 * P:(v0 + nv) * P, j0:j0 + width]
             nc.sync.dma_start(out=rows.rearrange("(v p) j -> p v j", p=P), in_=result)
@@ -235,9 +243,9 @@ def tile_list_memory_kv_swiglu_kernel(tc, tab_words, tab_scales, tab2_words, tab
         load_words(val_tab[1], tab2_words, 1)
         load_wv(0, 1)
         load_wv(1, 1)
-        for c0, chunks in ((0, 1), (1, 2)):
+        for c in range(3):
             for b in range(2):
-                load_wd(b, c0, chunks)
+                load_wd(b, c)
         key_codes = gather(key_tab, key_list, U32, "key_codes", 0, 2)
         key_planes = gather(key_scale_tab, key_list, U8, "key_plane0", 0, 1)
         deal_wk_words(nc.vector)
@@ -247,51 +255,52 @@ def tile_list_memory_kv_swiglu_kernel(tc, tab_words, tab_scales, tab2_words, tab
             gate(0, jc)
         val_codes = [gather(val_tab[0], val_list, U32, "val_codes0", 0, 2)]
         val_planes = gather(val_scale_tab, val_list, U8, "val_plane", 0, 2)
-        for a in range(2):
-            for t0 in (0, 2):
-                cast_wv(a, 0, "vector", t0, t0 + 2)
-            for t0 in (0, 2):
-                quantize_wv(a, 0, t0, t0 + 2)
+        cast_wv(0, 0, "scalar", 0, 2)
+        cast_wv(0, 0, "vector", 2, 4)
+        quantize_wv(0, 0)
+        cast_wv(1, 0, "vector")
+        quantize_wv(1, 0)
         for jc in range(8):
-            gate(1, jc)
+            gate(1, jc, raw_place["wv", 0, 0][:, jc * HALF:(jc + 1) * HALF] if jc < 4 else None)
         val_codes.append(gather(val_tab[1], val_list, U32, "val_codes10", 0, 1) + gather(val_tab[1], val_list, U32, "val_codes11", 1, 2))
         cast_wv(0, 1, "scalar")
         cast_wv(1, 1, "scalar")
-        def step(b, jc, room=None):
-            hidden(b, jc, room)
-            if (b, jc) != (0, 0):
-                quantize_h(*divmod(8 * b + jc - 1, 8))
-        for jc in range(4):
-            step(0, jc)
-        quantize_wv(0, 1)
-        for jc in (4, 5):
-            step(0, jc, room_in(wv_raw[0, 1], jc))
-        quantize_wv(1, 1)
-        for jc in (6, 7):
-            step(0, jc, room_in(wv_raw[1, 1], jc))
-        for c0, chunks in ((0, 1), (1, 2)):
+        pending = []
+        def pair(b, jp, room, between=None):
+            hidden(b, 2 * jp, room[:, :PASS])
+            for args in pending:
+                quantize_h(*args)
+            pending.clear()
+            if between is not None:
+                between()
+            hidden(b, 2 * jp + 1, room[:, PASS:])
+            pending.append((b, 2 * jp, room))
+        def cast_group(c):
             for b in range(2):
-                for c in range(c0, c0 + chunks):
-                    cast_wd(b, c, "scalar")
-        quantize_wd(0, 0)
-        quantize_wd(1, 0)
-        for jc in (0, 1):
-            step(1, jc, room_in(wd_tiles[1, 0], jc))
-        quantize_wd(0, 1)
-        quantize_wd(0, 2)
-        for jc in (2, 3, 4):
-            step(1, jc, room_in(wd_tiles[0, 1], jc))
-        quantize_wd(1, 1)
-        quantize_wd(1, 2)
-        for jc in (5, 6, 7):
-            step(1, jc, room_in(wd_tiles[1, 1], jc))
-        quantize_h(1, 7)
-        def result_room(k):
-            raw = wd_tiles[1, 1] if k < 2 else wv_raw[(k - 2) // 4, (k - 2) // 2 % 2]
-            k = k if k < 2 else k % 2
-            return raw[:].rearrange("p i n -> p (i n)")[:, k * HALF:(k + 1) * HALF]
-        for v in range(6):
-            project(v, 1, 0, HALF, "scalar", side_bank if v % 2 == 0 else val_bank, result_room(v))
-        for jp in (2, 3):
-            for c in range(3):
-                project(2 * c, 2, jp * PAIR, PAIR, "scalar" if (c + jp) % 2 == 0 else "vector", val_bank if c != 1 else side_bank)
+                cast_wd(b, c, "scalar")
+        def late_room(k):
+            return chain[4][:, 4 * KW:].rearrange("p (v j) -> p v j", v=2)[:, :, (k + 1) * KW:(k + 2) * KW]
+        pair(0, 0, held([P, 2 * PASS], BF16, "h_first")[:])
+        pair(0, 1, chain_room(0), lambda: quantize_wv(0, 1))
+        pair(0, 2, chain_room(1), lambda: quantize_wv(1, 1))
+        for c in range(3):
+            cast_group(c)
+        pair(1, 0, chain_room(2), lambda: quantize_wd(0))
+        pair(1, 1, chain_room(3), lambda: quantize_wd(1))
+        pair(0, 3, chain_room(4), lambda: quantize_wd(2))
+        tail = wd_bf[2].rearrange("p b n -> p (b n)")
+        pair(1, 2, tail[:, :2 * PASS])
+        last = tail[:, 2 * PASS:]
+        hidden(1, 6, last[:, :PASS])
+        quantize_h(*pending[0])
+        hidden(1, 7, last[:, PASS:])
+        quantize_h(1, 6, last[:, :PASS])
+        quantize_h(1, 7, last[:, PASS:])
+        order = [(0, 0), (1, 0), (0, 1), (1, 1), (2, 0), (2, 1)]
+        for k, (c, jp) in enumerate(order):
+            project(2 * c, 2, jp * PAIR, PAIR, "scalar", side_bank, late_room(k) if k < 3 else None)
+        for c in range(3):
+            project(2 * c, 2, 2 * PAIR, PAIR, "vector" if c == 2 else "scalar", val_bank)
+        for jc in (6, 7):
+            for g in range(2):
+                project(3 * g, 3, jc * CHUNK, CHUNK, "vector" if g == 0 else "scalar", val_bank if jc == 6 else side_bank)

@@ -78,9 +78,7 @@ def tile_list_memory_kv_swiglu_kernel(tc, tab_words, tab_scales, tab2_words, tab
         def load_wd(b, c):
             wd_raw[b, c] = raw_tile(("wd", b, c), WD_COLS)
             rows = wd[b * PASS:(b + 1) * PASS, c * WD_COLS:(c + 1) * WD_COLS]
-            rows = rows.rearrange("(m t e) n -> t m e n", t=PACK, e=4)
-            for t in range(PACK):
-                nc.sync.dma_start(out=wd_raw[b, c][:, t, :], in_=rows[t])
+            nc.sync.dma_start(out=wd_raw[b, c], in_=rows.rearrange("(p t) n -> p t n", t=PACK))
 
         def load_words(tile, table, a):
             nc.sync.dma_start(out=tile[:].bitcast(I32), in_=table[a].rearrange("p t i -> p (t i)").bitcast(I32))
@@ -111,11 +109,11 @@ def tile_list_memory_kv_swiglu_kernel(tc, tab_words, tab_scales, tab2_words, tab
         wv_codes = {}
         wv_planes = {}
 
-        def cast_wv(a, b, engine, t0=0, t1=PACK):
+        def cast_wv(a, b, engine, m0=0, m1=P):
             if (a, b) not in wv_bf:
                 wv_bf[a, b] = bf_tile(("wv", a, b)).rearrange("p (t q i) -> p t q i", t=PACK, i=PACK)
-            dst = wv_bf[a, b][:, t0:t1, :, :].rearrange("p t (m e) i -> p m t i e", e=4)
-            src = wv_raw[a, b].rearrange("p i (m t e) -> p m t i e", t=PACK, e=4)[:, :, t0:t1, :, :]
+            dst = wv_bf[a, b][:, :, m0:m1, :].rearrange("p t m i -> p m i t")
+            src = wv_raw[a, b].rearrange("p i (m t) -> p m i t", t=PACK)[:, m0:m1, :, :]
             copy_on(engine, dst, src)
 
         def quantize(codes, plane, src):
@@ -133,13 +131,13 @@ def tile_list_memory_kv_swiglu_kernel(tc, tab_words, tab_scales, tab2_words, tab
 
         def deal_wk_words(engine):
             engine.tensor_copy(
-                out=wk_codes[:].bitcast(I32).rearrange("p (b t m w) -> p b t m w", b=2, t=PACK, w=2),
-                in_=wk_raw[:].rearrange("p (b m t w) -> p b t m w", b=2, t=PACK, w=2))
+                out=wk_codes[:].bitcast(U16).rearrange("p (b t m) -> p b t m", b=2, t=PACK),
+                in_=wk_raw[:].bitcast(U16).rearrange("p (b m t) -> p b t m", b=2, t=PACK))
 
         def deal_wk_scales(engine):
             engine.tensor_copy(
-                out=wk_plane[:].bitcast(I32).rearrange("p (b t m) -> p b t m", b=2, t=PACK),
-                in_=wk_scale_raw[:].bitcast(I32).rearrange("p (b m t) -> p b t m", b=2, t=PACK))
+                out=wk_plane[:].rearrange("p (b t m) -> p b t m", b=2, t=PACK),
+                in_=wk_scale_raw[:].rearrange("p (b m t) -> p b t m", b=2, t=PACK))
 
         def side_bank(shape):
             return psum.tile(shape, F32, name="side_bank", bufs=SIDE_BANKS)
@@ -198,9 +196,9 @@ def tile_list_memory_kv_swiglu_kernel(tc, tab_words, tab_scales, tab2_words, tab
         wd_codes = [held([P, 2 * WD_COLS], U32, "wd_codes%d" % c) for c in range(3)]
         wd_planes = [held([P, 2 * WD_COLS], U8, "wd_plane%d" % c) for c in range(3)]
 
-        def cast_wd(b, c, engine):
-            copy_on(engine, wd_bf[c][:, b, :].rearrange("p (m e i) -> p m i e", e=4, i=PACK),
-                    wd_raw[b, c].rearrange("p i (m e) -> p m i e", e=4))
+        def cast_wd(b, c, engine, n0=0, n1=WD_COLS):
+            copy_on(engine, wd_bf[c][:, b, n0 * PACK:n1 * PACK].rearrange("p (m e i) -> p m i e", e=4, i=PACK),
+                    wd_raw[b, c][:, :, n0:n1].rearrange("p i (m e) -> p m i e", e=4))
 
         def quantize_wd(c):
             quantize(wd_codes[c][:], wd_planes[c][:], wd_bf[c].rearrange("p b n -> p (b n)"))
@@ -255,8 +253,8 @@ def tile_list_memory_kv_swiglu_kernel(tc, tab_words, tab_scales, tab2_words, tab
             gate(0, jc)
         val_codes = [gather(val_tab[0], val_list, U32, "val_codes0", 0, 2)]
         val_planes = gather(val_scale_tab, val_list, U8, "val_plane", 0, 2)
-        cast_wv(0, 0, "scalar", 0, 2)
-        cast_wv(0, 0, "vector", 2, 4)
+        cast_wv(0, 0, "scalar", 0, P // 2)
+        cast_wv(0, 0, "vector", P // 2, P)
         quantize_wv(0, 0)
         cast_wv(1, 0, "vector")
         quantize_wv(1, 0)

@@ -97,6 +97,13 @@ def tile_list_memory_kv_swiglu_kernel(tc, tab_words, tab_scales, tab2_words, tab
             nc.vector.tensor_copy(out=picked[:], in_=window[:].indirect(lst[:, u0 * HALF // 16:u1 * HALF // 16]))
             return [picked[:, w * HALF:(w + 1) * HALF] for w in range(u1 - u0)]
 
+        def gather_halves(window, lst, dtype, name, tag=None):
+            picked = keep.tile([P, S], dtype, name=name, tag=tag or name, align_bytes=64)
+            for u in range(2):
+                nc.vector.tensor_copy(out=picked[:, u * HALF:(u + 1) * HALF],
+                                      in_=window[:].indirect(lst[:, u * HALF // 16:(u + 1) * HALF // 16]))
+            return [picked[:, u * HALF:(u + 1) * HALF] for u in range(2)]
+
         def copy_on(engine, dst, src):
             if engine == "scalar":
                 nc.scalar.copy(out=dst, in_=src)
@@ -119,9 +126,10 @@ def tile_list_memory_kv_swiglu_kernel(tc, tab_words, tab_scales, tab2_words, tab
         def quantize(codes, plane, src):
             nc.vector.quantize_mx(out=codes.bitcast(FP8X4), scales=plane, in_=src)
 
-        def quantize_wv(a, b, t0=0, t1=PACK):
+        def quantize_wv(a, b, t0=0, t1=PACK, tag=None):
             if t0 == 0:
-                wv_codes[a, b] = held([P, PASS], U32, "wv_codes%d%d" % (a, b))
+                name = "wv_codes%d%d" % (a, b)
+                wv_codes[a, b] = keep.tile([P, PASS], U32, name=name, tag=tag or name, align_bytes=64)
                 wv_planes[a, b] = held([P, PASS], U8, "wv_plane%d%d" % (a, b))
             quantize(wv_codes[a, b][:, t0 * P:t1 * P], wv_planes[a, b][:, t0 * P:t1 * P],
                      wv_bf[a, b][:, t0:t1, :, :].rearrange("p t q i -> p (t q i)"))
@@ -255,8 +263,8 @@ def tile_list_memory_kv_swiglu_kernel(tc, tab_words, tab_scales, tab2_words, tab
         val_planes = gather(val_scale_tab, val_list, U8, "val_plane", 0, 2)
         cast_wv(0, 0, "scalar", 0, P // 2)
         cast_wv(0, 0, "vector", P // 2, P)
-        quantize_wv(0, 0)
         cast_wv(1, 0, "vector")
+        quantize_wv(0, 0, tag="raw_wv10")
         quantize_wv(1, 0)
         for jc in range(8):
             gate(1, jc, raw_place["wv", 0, 0][:, jc * HALF:(jc + 1) * HALF] if jc < 4 else None)
@@ -284,21 +292,20 @@ def tile_list_memory_kv_swiglu_kernel(tc, tab_words, tab_scales, tab2_words, tab
         for c in range(3):
             cast_group(c)
         pair(1, 0, chain_room(2), lambda: quantize_wd(0))
-        pair(1, 1, chain_room(3), lambda: quantize_wd(1))
-        pair(0, 3, chain_room(4), lambda: quantize_wd(2))
+        pair(1, 1, chain[3][:, :2 * KW].bitcast(BF16))
+        pair(1, 2, chain_room(3), lambda: quantize_wd(1))
         tail = wd_bf[2].rearrange("p b n -> p (b n)")
-        pair(1, 2, tail[:, :2 * PASS])
-        last = tail[:, 2 * PASS:]
-        hidden(1, 6, last[:, :PASS])
-        quantize_h(*pending[0])
-        hidden(1, 7, last[:, PASS:])
-        quantize_h(1, 6, last[:, :PASS])
-        quantize_h(1, 7, last[:, PASS:])
-        order = [(0, 0), (1, 0), (0, 1), (1, 1), (2, 0), (2, 1)]
+        late = chain_room(4)
+        for k, (b, jc, room) in enumerate(((0, 6, late[:, :PASS]), (1, 6, late[:, PASS:]), (0, 7, tail[:, :PASS]), (1, 7, tail[:, PASS:2 * PASS]))):
+            if k == 1:
+                quantize_wd(2)
+            hidden(b, jc, room)
+            quantize_h(*pending.pop())
+            pending.append((b, jc, room))
+        quantize_h(*pending.pop())
+        order = [(0, 0), (0, 1), (1, 0), (1, 1), (0, 2), (1, 2), (2, 0), (2, 1), (2, 2)]
         for k, (c, jp) in enumerate(order):
-            project(2 * c, 2, jp * PAIR, PAIR, "scalar", side_bank, late_room(k) if k < 3 else None)
-        for c in range(3):
-            project(2 * c, 2, 2 * PAIR, PAIR, "vector" if c == 2 else "scalar", val_bank)
+            project(2 * c, 2, jp * PAIR, PAIR, "vector" if k == 8 else "scalar", side_bank if k < 6 else val_bank, late_room(k - 1) if 1 <= k < 1 + 3 else None)
         for jc in (6, 7):
             for g in range(2):
                 project(3 * g, 3, jc * CHUNK, CHUNK, "vector" if g == 0 else "scalar", val_bank if jc == 6 else side_bank)

@@ -270,7 +270,8 @@ def tile_list_memory_kv_swiglu_kernel(tc, tab_words, tab_scales, tab2_words, tab
             gate(1, jc, raw_place["wv", 0, 0][:, jc * HALF:(jc + 1) * HALF] if jc < 4 else None)
         val_codes.append(gather(val_tab[1], val_list, U32, "val_codes10", 0, 1) + gather(val_tab[1], val_list, U32, "val_codes11", 1, 2))
         cast_wv(0, 1, "scalar")
-        cast_wv(1, 1, "scalar")
+        cast_wv(1, 1, "scalar", 0, P // 2)
+        cast_wv(1, 1, "vector", P // 2, P)
         pending = []
         def pair(b, jp, room, between=None):
             hidden(b, 2 * jp, room[:, :PASS])
@@ -281,31 +282,39 @@ def tile_list_memory_kv_swiglu_kernel(tc, tab_words, tab_scales, tab2_words, tab
                 between()
             hidden(b, 2 * jp + 1, room[:, PASS:])
             pending.append((b, 2 * jp, room))
-        def cast_group(c):
-            for b in range(2):
-                cast_wd(b, c, "scalar")
-        def late_room(k):
-            return chain[4][:, 4 * KW:].rearrange("p (v j) -> p v j", v=2)[:, :, (k + 1) * KW:(k + 2) * KW]
+        def single(b, jc, room):
+            hidden(b, jc, room)
+            for args in pending:
+                quantize_h(*args)
+            pending.clear()
+            pending.append((b, jc, room))
         pair(0, 0, held([P, 2 * PASS], BF16, "h_first")[:])
         pair(0, 1, chain_room(0), lambda: quantize_wv(0, 1))
-        pair(0, 2, chain_room(1), lambda: quantize_wv(1, 1))
+        quantize_wv(1, 1)
+        single(0, 4, chain_room(1)[:, PASS:])
         for c in range(3):
-            cast_group(c)
+            for b in range(2):
+                cast_wd(b, c, "vector" if (b, c) in () else "scalar")
         pair(1, 0, chain_room(2), lambda: quantize_wd(0))
         pair(1, 1, chain[3][:, :2 * KW].bitcast(BF16))
-        pair(1, 2, chain_room(3), lambda: quantize_wd(1))
-        tail = wd_bf[2].rearrange("p b n -> p (b n)")
-        late = chain_room(4)
-        for k, (b, jc, room) in enumerate(((0, 6, late[:, :PASS]), (1, 6, late[:, PASS:]), (0, 7, tail[:, :PASS]), (1, 7, tail[:, PASS:2 * PASS]))):
-            if k == 1:
-                quantize_wd(2)
-            hidden(b, jc, room)
-            quantize_h(*pending.pop())
-            pending.append((b, jc, room))
+        quantize_wd(1)
         quantize_h(*pending.pop())
-        order = [(0, 0), (0, 1), (1, 0), (1, 1), (0, 2), (1, 2), (2, 0), (2, 1), (2, 2)]
-        for k, (c, jp) in enumerate(order):
-            project(2 * c, 2, jp * PAIR, PAIR, "vector" if k == 8 else "scalar", side_bank if k < 6 else val_bank, late_room(k - 1) if 1 <= k < 1 + 3 else None)
-        for jc in (6, 7):
-            for g in range(2):
-                project(3 * g, 3, jc * CHUNK, CHUNK, "vector" if g == 0 else "scalar", val_bank if jc == 6 else side_bank)
+        single(0, 5, chain_room(3)[:, PASS:])
+        pair(1, 2, chain[4][:, :2 * KW].bitcast(BF16))
+        pair(0, 3, chain_room(4), lambda: quantize_wd(2))
+        pair(1, 3, wd_bf[2][:, 0, :])
+        quantize_h(*pending.pop())
+        early_room = chain[3][:, 5 * KW:7 * KW].rearrange("p (v j) -> p v j", v=2)
+        def wide_room(k):
+            return chain[4][:, (5 + 2 * k) * KW:(7 + 2 * k) * KW].rearrange("p (v j) -> p v j", v=1)
+        project(0, 2, 0, PAIR, "scalar", side_bank, early_room)
+        project(0, 2, PAIR, PAIR, "scalar", side_bank)
+        for v in (2, 3):
+            project(v, 1, 0, HALF, "scalar", side_bank, wide_room(v - 2))
+        for c in range(2):
+            project(2 * c, 2, 2 * PAIR, PAIR, "scalar", side_bank)
+        for v in (4, 5):
+            project(v, 1, 0, HALF, "scalar", val_bank)
+        project(4, 2, 2 * PAIR, PAIR, "scalar", val_bank)
+        for c in range(3):
+            project(2 * c, 2, 3 * PAIR, PAIR, "scalar" if c == 1 else "vector", val_bank if c < 2 else side_bank)

@@ -15,6 +15,7 @@ FP8X4 = mybir.dt.float8_e4m3fn_x4
 FP4X4 = mybir.dt.float4_e2m1fn_x4
 SILU = mybir.ActivationFunctionType.Silu
 MULT = mybir.AluOpType.mult
+ADD = mybir.AluOpType.add
 
 P = 128
 PACK = 4
@@ -24,9 +25,12 @@ CHUNK = 128
 PAIR = 2 * CHUNK
 VAL_ROW = 8
 WD_COLS = 256
-SIDE_BANKS = 3
+GATE_BANKS = (0, 1, 2)
+FIRST_BANKS = (3, 4, 5)
+SECOND_BANKS = (6, 7, 0, 1, 2)
 H_BUFS = 4
 RESULT_BUFS = 8
+LEAD = 256
 
 
 def tile_list_memory_kv_swiglu_kernel(tc, tab_words, tab_scales, tab2_words, tab2_scales, offs, offs2,
@@ -36,8 +40,8 @@ def tile_list_memory_kv_swiglu_kernel(tc, tab_words, tab_scales, tab2_words, tab
         keep = ctx.enter_context(tc.tile_pool(name="keep", bufs=1))
         psum = ctx.enter_context(tc.psum_pool(name="psum", bufs=1))
 
-        def held(shape, dtype, name):
-            return keep.tile(shape, dtype, name=name, align_bytes=64)
+        def held(shape, dtype, name, tag=None):
+            return keep.tile(shape, dtype, name=name, tag=tag or name, align_bytes=64)
 
         key_list = keep.tile([P, S // 16], U16, name="key_list")
         val_list = keep.tile([P, S // 16], U16, name="val_list")
@@ -50,157 +54,162 @@ def tile_list_memory_kv_swiglu_kernel(tc, tab_words, tab_scales, tab2_words, tab
         wv_raw = {}
         wd_raw = {}
 
-        KW = 256
-        chain = [held([P, n * KW], F32, "chain%d" % k) for k, n in enumerate((1 + 8, 4 + 8, 4 + 4, 4 + 4, 4 + 8))]
-        raw_place = {("wv", 0, 1): chain[0][:, KW:], ("wv", 1, 1): chain[1][:, 4 * KW:], ("wd", 1, 0): chain[2][:, 4 * KW:],
-                     ("wd", 1, 1): chain[3][:, 4 * KW:], ("wd", 1, 2): chain[4][:, 4 * KW:8 * KW], ("wd", 0, 2): chain[4][:, 8 * KW:]}
-        bf_place = {("wv", 0, 1): chain[1], ("wv", 1, 1): chain[2], ("wd", 0): chain[3], ("wd", 1): chain[4]}
+        raw_rooms = {}
 
-        def raw_tile(key, width):
-            if key not in raw_place:
-                raw_place[key] = held([P, PACK * width], F32, "raw_%s%d%d" % key)[:]
-            return raw_place[key].rearrange("p (i r) -> p i r", i=PACK)
-
-        def bf_tile(key):
-            if key in bf_place:
-                return bf_place[key][:, :4 * KW].bitcast(BF16)
-            return held([P, PACK * PASS], BF16, "bf_" + "".join(str(x) for x in key))[:]
-
-        def chain_room(k):
-            first = 0 if k == 0 else 3 * KW
-            return chain[k][:, first:first + 2 * KW].bitcast(BF16)
+        def raw_tile(name, words):
+            raw_rooms[name] = held([P, LEAD + words], F32, name)
+            return raw_rooms[name][:, LEAD:]
 
         def load_wv(a, b):
-            wv_raw[a, b] = raw_tile(("wv", a, b), PASS)
+            wv_raw[a, b] = raw_tile("wv_raw%d%d" % (a, b), PACK * PASS).rearrange("p (i r) -> p i r", i=PACK)
             rows = wv[a * PASS:(a + 1) * PASS, b * PASS:(b + 1) * PASS]
             nc.sync.dma_start(out=wv_raw[a, b], in_=rows.rearrange("(p i) r -> p i r", i=PACK))
 
-        def load_wd(b, c):
-            wd_raw[b, c] = raw_tile(("wd", b, c), WD_COLS)
-            rows = wd[b * PASS:(b + 1) * PASS, c * WD_COLS:(c + 1) * WD_COLS]
-            nc.sync.dma_start(out=wd_raw[b, c], in_=rows.rearrange("(p t) n -> p t n", t=PACK))
+        def load_wd(b, c0, c1):
+            width = (c1 - c0) * WD_COLS
+            raw = raw_tile("wd_raw%d%d" % (b, c0), PACK * width).rearrange("p (t n) -> p t n", t=PACK)
+            rows = wd[b * PASS:(b + 1) * PASS, c0 * WD_COLS:c1 * WD_COLS]
+            nc.sync.dma_start(out=raw, in_=rows.rearrange("(p t) n -> p t n", t=PACK))
+            for c in range(c0, c1):
+                wd_raw[b, c] = raw[:, :, (c - c0) * WD_COLS:(c - c0 + 1) * WD_COLS]
 
         def load_words(tile, table, a):
             nc.sync.dma_start(out=tile[:].bitcast(I32), in_=table[a].rearrange("p t i -> p (t i)").bitcast(I32))
 
-        def load_plane(queue, plane, scales):
+        def load_plane(plane, scales):
             for r in range(4):
-                queue.dma_start(out=plane[r:P:32, :].bitcast(I32), in_=scales[0, r:16:4, :].bitcast(I32))
+                nc.sync.dma_start(out=plane[r:P:32, :].bitcast(I32), in_=scales[0, r:16:4, :].bitcast(I32))
 
-        def load_val_planes(queue):
-            for q in range(4):
-                queue.dma_start(out=val_scale_tab[32 * q + VAL_ROW:32 * q + VAL_ROW + 8, :].bitcast(I32),
-                                in_=tab2_scales[:, 4 * q:4 * q + 4, :].bitcast(I32))
+        def load_key_rows():
+            nc.sync.dma_start(out=key_scale_tab[0:P:8, :].bitcast(I32), in_=tab_scales[0].bitcast(I32))
 
-        def gather(window, lst, dtype, name, u0, u1, tag=None):
-            picked = keep.tile([P, (u1 - u0) * HALF], dtype, name=name, tag=tag or name, align_bytes=64)
-            nc.vector.tensor_copy(out=picked[:], in_=window[:].indirect(lst[:, u0 * HALF // 16:u1 * HALF // 16]))
-            return [picked[:, w * HALF:(w + 1) * HALF] for w in range(u1 - u0)]
+        def load_val_rows():
+            nc.sync.dma_start(out=val_scale_tab[0:P:4, :].bitcast(I32),
+                              in_=tab2_scales.rearrange("a q t -> (a q) t").bitcast(I32))
 
-        def gather_halves(window, lst, dtype, name, tag=None):
-            picked = keep.tile([P, S], dtype, name=name, tag=tag or name, align_bytes=64)
-            for u in range(2):
-                nc.vector.tensor_copy(out=picked[:, u * HALF:(u + 1) * HALF],
-                                      in_=window[:].indirect(lst[:, u * HALF // 16:(u + 1) * HALF // 16]))
-            return [picked[:, u * HALF:(u + 1) * HALF] for u in range(2)]
+        def place_key_rows():
+            for r in range(4):
+                nc.sync.dma_start(out=key_plane[r:P:32, :].bitcast(I32), in_=key_rows[8 * r:P:32, :].bitcast(I32))
+
+        def place_val_rows(a):
+            for r in range(4):
+                nc.sync.dma_start(out=val_plane[VAL_ROW + 4 * a + r:P:32, :].bitcast(I32),
+                                  in_=val_rows[64 * a + 4 * r:64 * (a + 1):16, :].bitcast(I32))
+
+        def gather(picked, window, lst, j0, j1):
+            nc.vector.tensor_copy(out=picked[:, j0:j1], in_=window[:].indirect(lst[:, j0 // 16:j1 // 16]))
 
         def copy_on(engine, dst, src):
             if engine == "scalar":
                 nc.scalar.copy(out=dst, in_=src)
             elif engine == "gpsimd":
-                nc.gpsimd.tensor_scalar(out=dst, in0=src, scalar1=1.0, scalar2=0.0, op0=MULT, op1=mybir.AluOpType.add)
+                nc.gpsimd.tensor_scalar(out=dst, in0=src, scalar1=1.0, scalar2=0.0, op0=MULT, op1=ADD)
             else:
                 nc.vector.tensor_copy(out=dst, in_=src)
 
+        def quantize(codes, plane, src):
+            nc.vector.quantize_mx(out=codes.bitcast(FP8X4), scales=plane, in_=src)
+
+        key_codes = held([P, S], U32, "key_codes")
+        key_plane = held([P, S], U8, "key_plane")
+        val_codes = [held([P, S], U32, "val_codes%d" % a) for a in range(2)]
+        val_plane = held([P, S], U8, "val_plane")
+        key_rows = held([P, S], U8, "key_rows")
+        val_rows = held([P, S], U8, "val_rows")
         wv_bf = {}
         wv_codes = {}
         wv_planes = {}
 
         def cast_wv(a, b, engine, m0=0, m1=P):
             if (a, b) not in wv_bf:
-                wv_bf[a, b] = bf_tile(("wv", a, b)).rearrange("p (t q i) -> p t q i", t=PACK, i=PACK)
+                wv_bf[a, b] = held([P, PACK * PASS], BF16, "wv_bf%d%d" % (a, b))[:].rearrange("p (t q i) -> p t q i", t=PACK, i=PACK)
             dst = wv_bf[a, b][:, :, m0:m1, :].rearrange("p t m i -> p m i t")
             src = wv_raw[a, b].rearrange("p i (m t) -> p m i t", t=PACK)[:, m0:m1, :, :]
             copy_on(engine, dst, src)
 
-        def quantize(codes, plane, src):
-            nc.vector.quantize_mx(out=codes.bitcast(FP8X4), scales=plane, in_=src)
-
-        def quantize_wv(a, b, t0=0, t1=PACK, tag=None):
-            if t0 == 0:
-                name = "wv_codes%d%d" % (a, b)
-                wv_codes[a, b] = keep.tile([P, PASS], U32, name=name, tag=tag or name, align_bytes=64)
-                wv_planes[a, b] = held([P, PASS], U8, "wv_plane%d%d" % (a, b))
-            quantize(wv_codes[a, b][:, t0 * P:t1 * P], wv_planes[a, b][:, t0 * P:t1 * P],
-                     wv_bf[a, b][:, t0:t1, :, :].rearrange("p t q i -> p (t q i)"))
+        def quantize_wv(a, b, tag=None):
+            wv_codes[a, b] = held([P, PASS], U32, "wv_codes%d%d" % (a, b), tag)
+            wv_planes[a, b] = held([P, PASS], U8, "wv_plane%d%d" % (a, b))
+            quantize(wv_codes[a, b][:], wv_planes[a, b][:], wv_bf[a, b].rearrange("p t q i -> p (t q i)"))
 
         wk_codes = held([P, 2 * H], U8, "wk_codes")
         wk_plane = held([P, H], U8, "wk_plane")
 
-        def deal_wk_words(engine):
-            engine.tensor_copy(
+        def deal_wk_words():
+            nc.vector.tensor_copy(
                 out=wk_codes[:].bitcast(U16).rearrange("p (b t m) -> p b t m", b=2, t=PACK),
                 in_=wk_raw[:].bitcast(U16).rearrange("p (b m t) -> p b t m", b=2, t=PACK))
 
-        def deal_wk_scales(engine):
-            engine.tensor_copy(
+        def deal_wk_scales():
+            nc.vector.tensor_copy(
                 out=wk_plane[:].rearrange("p (b t m) -> p b t m", b=2, t=PACK),
                 in_=wk_scale_raw[:].rearrange("p (b m t) -> p b t m", b=2, t=PACK))
 
-        def side_bank(shape):
-            return psum.tile(shape, F32, name="side_bank", bufs=SIDE_BANKS)
+        turns = {}
 
-        def val_bank(shape):
-            return psum.tile(shape, F32, name="val_bank", bufs=8 - SIDE_BANKS)
+        def bank_from(banks, shape):
+            k = turns.get(banks, 0)
+            turns[banks] = k + 1
+            return psum.tile(shape, F32, name="bank%d" % banks[k % len(banks)])
 
         gates = {}
 
         def gate(b, jc, room=None):
-            u, c0 = divmod(jc * CHUNK, HALF)
-            bank = side_bank([P, PACK, CHUNK])
+            c0 = jc * CHUNK
+            bank = bank_from(GATE_BANKS, [P, PACK, CHUNK])
             for t in range(PACK):
                 r0 = b * PASS + t * P
                 nc.tensor.matmul_mx(out=bank[:, t, :],
                                     lhsT=wk_codes[:, 2 * r0:2 * (r0 + P)].bitcast(FP4X4),
                                     lhsT_scale=wk_plane[:, r0:r0 + P],
-                                    rhs=key_codes[u][:, c0:c0 + CHUNK].bitcast(FP8X4),
-                                    rhs_scale=key_planes[u][:, c0:c0 + CHUNK],
+                                    rhs=key_codes[:, c0:c0 + CHUNK].bitcast(FP8X4),
+                                    rhs_scale=key_plane[:, c0:c0 + CHUNK],
                                     start=True, stop=True)
             if room is None:
                 room = held([P, CHUNK * PACK], F32, "gate%d%d" % (b, jc))[:]
             gates[b, jc] = room.rearrange("p (j t) -> p j t", t=PACK)
             nc.scalar.activation(out=gates[b, jc], in_=bank[:].rearrange("p t j -> p j t"), func=SILU)
 
-        h_bf = {}
-        h_codes = {(b, u): held([P, HALF], U32, "h_codes%d%d" % (b, u)) for b in range(2) for u in range(2)}
-        h_planes = {(b, u): held([P, HALF], U8, "h_plane%d%d" % (b, u)) for b in range(2) for u in range(2)}
+        h_codes = [held([P, S], U32, "h_codes%d" % b) for b in range(2)]
+        h_planes = [held([P, S], U8, "h_plane%d" % b) for b in range(2)]
         val_banks = {}
+        h_bf = {}
 
-        def values(b, jc, a):
-            u, c0 = divmod(jc * CHUNK, HALF)
+        def values(b, jc, a, banks):
+            c0 = jc * CHUNK
             if a == 0:
-                val_banks[b, jc] = val_bank([P, PACK, CHUNK])
+                val_banks[b, jc] = bank_from(banks, [P, PACK, CHUNK])
             for t in range(PACK):
                 nc.tensor.matmul_mx(out=val_banks[b, jc][:, t, :],
                                     lhsT=wv_codes[a, b][:, t * P:(t + 1) * P].bitcast(FP8X4),
                                     lhsT_scale=wv_planes[a, b][:, t * P:(t + 1) * P],
-                                    rhs=val_codes[a][u][:, c0:c0 + CHUNK].bitcast(FP8X4),
-                                    rhs_scale=val_planes[u][VAL_ROW + 4 * a:, c0:c0 + CHUNK],
+                                    rhs=val_codes[a][:, c0:c0 + CHUNK].bitcast(FP8X4),
+                                    rhs_scale=val_plane[VAL_ROW + 4 * a:, c0:c0 + CHUNK],
                                     start=(a == 0 and t == 0), stop=(a == 1 and t == PACK - 1))
 
         def hidden(b, jc, room=None):
-            values(b, jc, 0)
-            values(b, jc, 1)
-            h_bf[b, jc] = room
-            nc.vector.tensor_tensor(out=room.rearrange("p (j t) -> p j t", t=PACK),
+            banks = FIRST_BANKS if b == 0 and jc < 7 else SECOND_BANKS
+            values(b, jc, 0, banks)
+            values(b, jc, 1, banks)
+            jp, w = divmod(jc, 2)
+            if w == 0:
+                if room is None:
+                    room = keep.tile([P, 2 * PASS], BF16, name="h_bf", bufs=H_BUFS, align_bytes=64)[:]
+                h_bf[b, jp] = room
+            nc.vector.tensor_tensor(out=h_bf[b, jp][:, w * PASS:(w + 1) * PASS].rearrange("p (j t) -> p j t", t=PACK),
                                     in0=val_banks[b, jc][:].rearrange("p t j -> p j t"), in1=gates[b, jc], op=MULT)
 
-        def quantize_h(b, jc, room):
-            u, c0 = divmod(jc * CHUNK, HALF)
-            width = room.shape[1] // PACK
-            quantize(h_codes[b, u][:, c0:c0 + width], h_planes[b, u][:, c0:c0 + width], room)
+        def second_behind(name):
+            return raw_rooms[name][:, :2 * LEAD].bitcast(BF16)
 
-        wd_bf = [bf_tile(("wd", c)).rearrange("p (b n) -> p b n", b=2) for c in range(3)]
+        def both_behind(name):
+            return raw_rooms[name][:, LEAD:3 * LEAD].bitcast(BF16)
+
+        def quantize_h(b, jp):
+            c0 = jp * PAIR
+            quantize(h_codes[b][:, c0:c0 + PAIR], h_planes[b][:, c0:c0 + PAIR], h_bf[b, jp])
+
+        wd_bf = [held([P, 2 * WD_COLS * PACK], BF16, "wd_bf%d" % c)[:].rearrange("p (b n) -> p b n", b=2) for c in range(3)]
         wd_codes = [held([P, 2 * WD_COLS], U32, "wd_codes%d" % c) for c in range(3)]
         wd_planes = [held([P, 2 * WD_COLS], U8, "wd_plane%d" % c) for c in range(3)]
 
@@ -211,9 +220,8 @@ def tile_list_memory_kv_swiglu_kernel(tc, tab_words, tab_scales, tab2_words, tab
         def quantize_wd(c):
             quantize(wd_codes[c][:], wd_planes[c][:], wd_bf[c].rearrange("p b n -> p (b n)"))
 
-        def project(v0, nv, j0, width, engine, bank_of, room=None):
-            u, c0 = divmod(j0, HALF)
-            bank = bank_of([P, nv, width])
+        def project(v0, nv, j0, width, engine, banks):
+            bank = bank_from(banks, [P, nv, width])
             for b in range(2):
                 for w in range(nv):
                     c, n0 = divmod((v0 + w) * P, WD_COLS)
@@ -221,100 +229,100 @@ def tile_list_memory_kv_swiglu_kernel(tc, tab_words, tab_scales, tab2_words, tab
                     nc.tensor.matmul_mx(out=bank[:, w, :],
                                         lhsT=wd_codes[c][:, n0:n0 + P].bitcast(FP8X4),
                                         lhsT_scale=wd_planes[c][:, n0:n0 + P],
-                                        rhs=h_codes[b, u][:, c0:c0 + width].bitcast(FP8X4),
-                                        rhs_scale=h_planes[b, u][:, c0:c0 + width],
+                                        rhs=h_codes[b][:, j0:j0 + width].bitcast(FP8X4),
+                                        rhs_scale=h_planes[b][:, j0:j0 + width],
                                         start=(b == 0 and w == 0), stop=(b == 1 and w == nv - 1))
-            if room is None:
-                room = keep.tile([P, nv, width], F32, name="result", bufs=RESULT_BUFS)[:]
-            result = room
+            result = keep.tile([P, nv, width], F32, name="result", bufs=RESULT_BUFS)[:]
             copy_on(engine, result, bank[:])
             rows = out[v0 * P:(v0 + nv) * P, j0:j0 + width]
             nc.sync.dma_start(out=rows.rearrange("(v p) j -> p v j", p=P), in_=result)
 
-        nc.vector.memset(key_scale_tab[:, :T // 2].bitcast(I32), 0)
-        nc.gpsimd.memset(key_scale_tab[:, T // 2:].bitcast(I32), 0)
-        nc.vector.memset(val_scale_tab[:, :T2 // 2].bitcast(I32), 0)
-        nc.gpsimd.memset(val_scale_tab[:, T2 // 2:].bitcast(I32), 0)
+        nc.vector.memset(key_scale_tab[:].bitcast(I32), 0)
+        nc.vector.memset(val_scale_tab[:].bitcast(I32), 0)
         nc.vector.memset(wk_scale_raw[:].bitcast(I32), 0)
+        nc.vector.memset(key_plane[:].bitcast(I32), 0)
+        nc.vector.memset(val_plane[:].bitcast(I32), 0)
         nc.sync.dma_start(key_list[:], offs)
-        load_words(key_tab, tab_words, 0)
-        load_plane(nc.sync, key_scale_tab, tab_scales)
-        nc.sync.dma_start(out=wk_raw[:], in_=wk_words[0].bitcast(I32))
         nc.sync.dma_start(val_list[:], offs2)
-        load_plane(nc.sync, wk_scale_raw, wk_scales)
+        nc.sync.dma_start(out=wk_raw[:], in_=wk_words[0].bitcast(I32))
+        load_key_rows()
+        load_val_rows()
+        load_plane(wk_scale_raw, wk_scales)
+        load_words(key_tab, tab_words, 0)
+        deal_wk_words()
+        gather(key_rows, key_scale_tab, key_list, 0, S)
+        place_key_rows()
         load_words(val_tab[0], tab2_words, 0)
-        load_val_planes(nc.sync)
+        gather(val_rows, val_scale_tab, val_list, 0, S)
+        deal_wk_scales()
+        place_val_rows(0)
         load_wv(0, 0)
+        place_val_rows(1)
         load_wv(1, 0)
         load_words(val_tab[1], tab2_words, 1)
         load_wv(0, 1)
         load_wv(1, 1)
         for c in range(3):
             for b in range(2):
-                load_wd(b, c)
-        key_codes = gather(key_tab, key_list, U32, "key_codes", 0, 2)
-        key_planes = gather(key_scale_tab, key_list, U8, "key_plane0", 0, 1)
-        deal_wk_words(nc.vector)
-        deal_wk_scales(nc.vector)
-        key_planes += gather(key_scale_tab, key_list, U8, "key_plane1", 1, 2, "wk_scale_raw")
+                load_wd(b, c, c + 1)
+        for u in range(2):
+            gather(key_codes, key_tab, key_list, u * HALF, (u + 1) * HALF)
+        gather(val_codes[0], val_tab[0], val_list, 0, S)
         for jc in range(8):
             gate(0, jc)
-        val_codes = [gather(val_tab[0], val_list, U32, "val_codes0", 0, 2)]
-        val_planes = gather(val_scale_tab, val_list, U8, "val_plane", 0, 2)
-        cast_wv(0, 0, "scalar", 0, P // 2)
-        cast_wv(0, 0, "vector", P // 2, P)
-        cast_wv(1, 0, "vector")
-        quantize_wv(0, 0, tag="raw_wv10")
-        quantize_wv(1, 0)
+        cast_wv(0, 0, "vector")
         for jc in range(8):
-            gate(1, jc, raw_place["wv", 0, 0][:, jc * HALF:(jc + 1) * HALF] if jc < 4 else None)
-        val_codes.append(gather(val_tab[1], val_list, U32, "val_codes10", 0, 1) + gather(val_tab[1], val_list, U32, "val_codes11", 1, 2))
+            gate(1, jc, raw_rooms["wv_raw00"][:, LEAD + jc * PASS:LEAD + (jc + 1) * PASS] if jc < 4 else None)
+        quantize_wv(0, 0)
+        cast_wv(1, 0, "vector")
+        quantize_wv(1, 0)
+        for u in range(2):
+            gather(val_codes[1], val_tab[1], val_list, u * HALF, (u + 1) * HALF)
         cast_wv(0, 1, "scalar")
         cast_wv(1, 1, "scalar", 0, P // 2)
+        hidden(0, 0)
+        hidden(0, 1)
+        hidden(0, 2)
+        quantize_h(0, 0)
+        hidden(0, 3)
+        hidden(0, 4)
+        hidden(0, 5)
+        quantize_wv(0, 1)
         cast_wv(1, 1, "vector", P // 2, P)
-        pending = []
-        def pair(b, jp, room, between=None):
-            hidden(b, 2 * jp, room[:, :PASS])
-            for args in pending:
-                quantize_h(*args)
-            pending.clear()
-            if between is not None:
-                between()
-            hidden(b, 2 * jp + 1, room[:, PASS:])
-            pending.append((b, 2 * jp, room))
-        def single(b, jc, room):
-            hidden(b, jc, room)
-            for args in pending:
-                quantize_h(*args)
-            pending.clear()
-            pending.append((b, jc, room))
-        pair(0, 0, held([P, 2 * PASS], BF16, "h_first")[:])
-        pair(0, 1, chain_room(0), lambda: quantize_wv(0, 1))
+        quantize_h(0, 1)
         quantize_wv(1, 1)
-        single(0, 4, chain_room(1)[:, PASS:])
-        for c in range(3):
-            for b in range(2):
-                cast_wd(b, c, "vector" if (b, c) in () else "scalar")
-        pair(1, 0, chain_room(2), lambda: quantize_wd(0))
-        pair(1, 1, chain[3][:, :2 * KW].bitcast(BF16))
-        quantize_wd(1)
-        quantize_h(*pending.pop())
-        single(0, 5, chain_room(3)[:, PASS:])
-        pair(1, 2, chain[4][:, :2 * KW].bitcast(BF16))
-        pair(0, 3, chain_room(4), lambda: quantize_wd(2))
-        pair(1, 3, wd_bf[2][:, 0, :])
-        quantize_h(*pending.pop())
-        early_room = chain[3][:, 5 * KW:7 * KW].rearrange("p (v j) -> p v j", v=2)
-        def wide_room(k):
-            return chain[4][:, (5 + 2 * k) * KW:(7 + 2 * k) * KW].rearrange("p (v j) -> p v j", v=1)
-        project(0, 2, 0, PAIR, "scalar", side_bank, early_room)
-        project(0, 2, PAIR, PAIR, "scalar", side_bank)
-        for v in (2, 3):
-            project(v, 1, 0, HALF, "scalar", side_bank, wide_room(v - 2))
+        hidden(0, 6, both_behind("wv_raw11"))
+        quantize_h(0, 2)
         for c in range(2):
-            project(2 * c, 2, 2 * PAIR, PAIR, "scalar", side_bank)
+            for b in range(2):
+                cast_wd(b, c, "scalar")
+        cast_wd(0, 2, "scalar")
+        hidden(1, 0)
+        hidden(1, 1)
+        quantize_wd(0)
+        quantize_h(1, 0)
+        hidden(1, 2)
+        project(0, 2, 0, PAIR, "scalar", FIRST_BANKS)
+        hidden(1, 3)
+        quantize_wd(1)
+        quantize_h(1, 1)
+        hidden(1, 4)
+        project(0, 2, PAIR, PAIR, "scalar", FIRST_BANKS)
+        for v in (2, 3):
+            project(v, 1, 0, HALF, "scalar", FIRST_BANKS)
+        hidden(1, 5)
+        cast_wd(1, 2, "vector")
+        quantize_h(1, 2)
+        quantize_wd(2)
+        hidden(0, 7)
+        for c in range(2):
+            project(2 * c, 2, 2 * PAIR, PAIR, "scalar", FIRST_BANKS)
+        hidden(1, 6)
+        quantize_h(0, 3)
         for v in (4, 5):
-            project(v, 1, 0, HALF, "scalar", val_bank)
-        project(4, 2, 2 * PAIR, PAIR, "scalar", val_bank)
+            project(v, 1, 0, HALF, "scalar", FIRST_BANKS)
+        hidden(1, 7)
+        quantize_h(1, 3)
+        project(4, 2, 2 * PAIR, PAIR, "scalar", FIRST_BANKS)
         for c in range(3):
-            project(2 * c, 2, 3 * PAIR, PAIR, "scalar" if c == 1 else "vector", val_bank if c < 2 else side_bank)
+            project(2 * c, 2, 3 * PAIR, PAIR, "scalar" if c == 1 else "vector", SECOND_BANKS)

@@ -91,8 +91,8 @@ def tile_list_memory_kv_swiglu_kernel(tc, tab_words, tab_scales, tab2_words, tab
             for r in range(4):
                 nc.sync.dma_start(out=key_plane[r:P:32, :].bitcast(I32), in_=key_rows[8 * r:P:32, :].bitcast(I32))
 
-        def place_val_rows(a):
-            for r in range(4):
+        def place_val_rows(a, r0, r1):
+            for r in range(r0, r1):
                 nc.sync.dma_start(out=val_plane[VAL_ROW + 4 * a + r:P:32, :].bitcast(I32),
                                   in_=val_rows[64 * a + 4 * r:64 * (a + 1):16, :].bitcast(I32))
 
@@ -170,8 +170,8 @@ def tile_list_memory_kv_swiglu_kernel(tc, tab_words, tab_scales, tab2_words, tab
             gates[b, jc] = room.rearrange("p (j t) -> p j t", t=PACK)
             nc.scalar.activation(out=gates[b, jc], in_=bank[:].rearrange("p t j -> p j t"), func=SILU)
 
-        h_codes = [held([P, S], U32, "h_codes%d" % b) for b in range(2)]
-        h_planes = [held([P, S], U8, "h_plane%d" % b) for b in range(2)]
+        h_codes = {}
+        h_planes = {}
         val_banks = {}
         h_bf = {}
 
@@ -187,8 +187,7 @@ def tile_list_memory_kv_swiglu_kernel(tc, tab_words, tab_scales, tab2_words, tab
                                     rhs_scale=val_plane[VAL_ROW + 4 * a:, c0:c0 + CHUNK],
                                     start=(a == 0 and t == 0), stop=(a == 1 and t == PACK - 1))
 
-        def hidden(b, jc, room=None):
-            banks = FIRST_BANKS if b == 0 and jc < 7 else SECOND_BANKS
+        def hidden(b, jc, banks, room=None):
             values(b, jc, 0, banks)
             values(b, jc, 1, banks)
             jp, w = divmod(jc, 2)
@@ -205,9 +204,12 @@ def tile_list_memory_kv_swiglu_kernel(tc, tab_words, tab_scales, tab2_words, tab
         def both_behind(name):
             return raw_rooms[name][:, LEAD:3 * LEAD].bitcast(BF16)
 
-        def quantize_h(b, jp):
-            c0 = jp * PAIR
-            quantize(h_codes[b][:, c0:c0 + PAIR], h_planes[b][:, c0:c0 + PAIR], h_bf[b, jp])
+        def quantize_h(b, jp, w0=0, w1=2, tag=None):
+            if w0 == 0:
+                h_codes[b, jp] = held([P, PAIR], U32, "h_codes%d%d" % (b, jp), tag)
+                h_planes[b, jp] = held([P, PAIR], U8, "h_plane%d%d" % (b, jp))
+            cols = slice(w0 * CHUNK, w1 * CHUNK)
+            quantize(h_codes[b, jp][:, cols], h_planes[b, jp][:, cols], h_bf[b, jp][:, w0 * PASS:w1 * PASS])
 
         wd_bf = [held([P, 2 * WD_COLS * PACK], BF16, "wd_bf%d" % c)[:].rearrange("p (b n) -> p b n", b=2) for c in range(3)]
         wd_codes = [held([P, 2 * WD_COLS], U32, "wd_codes%d" % c) for c in range(3)]
@@ -222,16 +224,18 @@ def tile_list_memory_kv_swiglu_kernel(tc, tab_words, tab_scales, tab2_words, tab
 
         def project(v0, nv, j0, width, engine, banks):
             bank = bank_from(banks, [P, nv, width])
-            for b in range(2):
-                for w in range(nv):
-                    c, n0 = divmod((v0 + w) * P, WD_COLS)
-                    n0 = n0 + b * WD_COLS
-                    nc.tensor.matmul_mx(out=bank[:, w, :],
-                                        lhsT=wd_codes[c][:, n0:n0 + P].bitcast(FP8X4),
-                                        lhsT_scale=wd_planes[c][:, n0:n0 + P],
-                                        rhs=h_codes[b][:, j0:j0 + width].bitcast(FP8X4),
-                                        rhs_scale=h_planes[b][:, j0:j0 + width],
-                                        start=(b == 0 and w == 0), stop=(b == 1 and w == nv - 1))
+            step = min(width, PAIR)
+            passes = [(b, w, j) for b in range(2) for w in range(nv) for j in range(j0, j0 + width, step)]
+            for b, w, j in passes:
+                c, n0 = divmod((v0 + w) * P, WD_COLS)
+                n0 = n0 + b * WD_COLS
+                jp, c0 = divmod(j, PAIR)
+                nc.tensor.matmul_mx(out=bank[:, w, j - j0:j - j0 + step],
+                                    lhsT=wd_codes[c][:, n0:n0 + P].bitcast(FP8X4),
+                                    lhsT_scale=wd_planes[c][:, n0:n0 + P],
+                                    rhs=h_codes[b, jp][:, c0:c0 + step].bitcast(FP8X4),
+                                    rhs_scale=h_planes[b, jp][:, c0:c0 + step],
+                                    start=(b, w, j) == passes[0], stop=(b, w, j) == passes[-1])
             result = keep.tile([P, nv, width], F32, name="result", bufs=RESULT_BUFS)[:]
             copy_on(engine, result, bank[:])
             rows = out[v0 * P:(v0 + nv) * P, j0:j0 + width]
@@ -255,11 +259,12 @@ def tile_list_memory_kv_swiglu_kernel(tc, tab_words, tab_scales, tab2_words, tab
         load_words(val_tab[0], tab2_words, 0)
         gather(val_rows, val_scale_tab, val_list, 0, S)
         deal_wk_scales()
-        place_val_rows(0)
         load_wv(0, 0)
-        place_val_rows(1)
+        place_val_rows(0, 0, 2)
         load_wv(1, 0)
         load_words(val_tab[1], tab2_words, 1)
+        place_val_rows(0, 2, 4)
+        place_val_rows(1, 0, 4)
         load_wv(0, 1)
         load_wv(1, 1)
         for c in range(3):
@@ -280,49 +285,49 @@ def tile_list_memory_kv_swiglu_kernel(tc, tab_words, tab_scales, tab2_words, tab
             gather(val_codes[1], val_tab[1], val_list, u * HALF, (u + 1) * HALF)
         cast_wv(0, 1, "scalar")
         cast_wv(1, 1, "scalar", 0, P // 2)
-        hidden(0, 0)
-        hidden(0, 1)
-        hidden(0, 2)
+        hidden(0, 0, FIRST_BANKS)
+        hidden(0, 1, FIRST_BANKS)
+        hidden(0, 2, FIRST_BANKS)
         quantize_h(0, 0)
-        hidden(0, 3)
-        hidden(0, 4)
-        hidden(0, 5)
-        quantize_wv(0, 1)
+        hidden(0, 3, FIRST_BANKS)
+        hidden(0, 4, FIRST_BANKS)
+        hidden(0, 5, FIRST_BANKS)
         cast_wv(1, 1, "vector", P // 2, P)
-        quantize_h(0, 1)
+        quantize_wv(0, 1)
         quantize_wv(1, 1)
-        hidden(0, 6, both_behind("wv_raw11"))
-        quantize_h(0, 2)
+        hidden(0, 6, FIRST_BANKS, both_behind("wv_raw11"))
+        quantize_h(0, 1, tag="wv_bf11")
         for c in range(2):
             for b in range(2):
                 cast_wd(b, c, "scalar")
-        cast_wd(0, 2, "scalar")
-        hidden(1, 0)
-        hidden(1, 1)
+        hidden(1, 0, SECOND_BANKS)
+        hidden(1, 1, SECOND_BANKS)
         quantize_wd(0)
         quantize_h(1, 0)
-        hidden(1, 2)
-        project(0, 2, 0, PAIR, "scalar", FIRST_BANKS)
-        hidden(1, 3)
-        quantize_wd(1)
+        hidden(1, 2, SECOND_BANKS)
+        project(0, 2, 0, PAIR, "scalar", (4,))
+        cast_wd(0, 2, "scalar")
+        hidden(1, 3, SECOND_BANKS)
+        quantize_h(0, 2, tag="wd_bf0")
         quantize_h(1, 1)
-        hidden(1, 4)
-        project(0, 2, PAIR, PAIR, "scalar", FIRST_BANKS)
+        quantize_wd(1)
+        project(0, 2, PAIR, PAIR, "scalar", (5,))
         for v in (2, 3):
-            project(v, 1, 0, HALF, "scalar", FIRST_BANKS)
-        hidden(1, 5)
+            project(v, 1, 0, HALF, "scalar", ((3,), (4,))[v - 2])
+        hidden(1, 4, SECOND_BANKS)
+        hidden(1, 5, SECOND_BANKS)
         cast_wd(1, 2, "vector")
         quantize_h(1, 2)
         quantize_wd(2)
-        hidden(0, 7)
         for c in range(2):
-            project(2 * c, 2, 2 * PAIR, PAIR, "scalar", FIRST_BANKS)
-        hidden(1, 6)
+            project(2 * c, 2, 2 * PAIR, PAIR, "scalar", ((2,), (5,))[c])
+        hidden(0, 7, SECOND_BANKS)
+        hidden(1, 6, SECOND_BANKS)
         quantize_h(0, 3)
+        hidden(1, 7, SECOND_BANKS)
         for v in (4, 5):
-            project(v, 1, 0, HALF, "scalar", FIRST_BANKS)
-        hidden(1, 7)
+            project(v, 1, 0, HALF, "scalar", ((6,), (3,))[v - 4])
+        project(4, 2, 2 * PAIR, PAIR, "scalar", (4,))
         quantize_h(1, 3)
-        project(4, 2, 2 * PAIR, PAIR, "scalar", FIRST_BANKS)
         for c in range(3):
-            project(2 * c, 2, 3 * PAIR, PAIR, "scalar" if c == 1 else "vector", SECOND_BANKS)
+            project(2 * c, 2, 3 * PAIR, PAIR, "scalar" if c == 1 else "vector", ((7,), (0,), (2,))[c])

@@ -23,7 +23,6 @@ PASS = P * PACK
 HALF = S // 2
 CHUNK = 128
 PAIR = 2 * CHUNK
-VAL_ROW = 8
 WD_COLS = 256
 GATE_BANKS = (0, 1, 2)
 FIRST_BANKS = (3, 4, 5)
@@ -31,6 +30,7 @@ SECOND_BANKS = (6, 7, 0, 1, 2)
 H_BUFS = 4
 RESULT_BUFS = 8
 LEAD = 256
+RESULT_LEAD = 384
 
 
 def tile_list_memory_kv_swiglu_kernel(tc, tab_words, tab_scales, tab2_words, tab2_scales, offs, offs2,
@@ -57,8 +57,9 @@ def tile_list_memory_kv_swiglu_kernel(tc, tab_words, tab_scales, tab2_words, tab
         raw_rooms = {}
 
         def raw_tile(name, words):
-            raw_rooms[name] = held([P, LEAD + words], F32, name)
-            return raw_rooms[name][:, LEAD:]
+            lead = RESULT_LEAD if name == "wd_raw02" else LEAD
+            raw_rooms[name] = held([P, lead + words], F32, name)
+            return raw_rooms[name][:, lead:]
 
         def load_wv(a, b):
             wv_raw[a, b] = raw_tile("wv_raw%d%d" % (a, b), PACK * PASS).rearrange("p (i r) -> p i r", i=PACK)
@@ -73,27 +74,20 @@ def tile_list_memory_kv_swiglu_kernel(tc, tab_words, tab_scales, tab2_words, tab
             for c in range(c0, c1):
                 wd_raw[b, c] = raw[:, :, (c - c0) * WD_COLS:(c - c0 + 1) * WD_COLS]
 
-        def load_words(tile, table, a):
-            nc.sync.dma_start(out=tile[:].bitcast(I32), in_=table[a].rearrange("p t i -> p (t i)").bitcast(I32))
+        def load_words(tile, table, a, t0=0, t1=None):
+            words = table[a].rearrange("p t i -> p (t i)").bitcast(I32)
+            nc.sync.dma_start(out=tile[:, t0:t1].bitcast(I32), in_=words[:, t0:t1])
 
-        def load_plane(plane, scales):
-            for r in range(4):
-                nc.sync.dma_start(out=plane[r:P:32, :].bitcast(I32), in_=scales[0, r:16:4, :].bitcast(I32))
+        def load_rows(tile, step, rows):
+            nc.sync.dma_start(out=tile[0:P:step, :].bitcast(I32), in_=rows.bitcast(I32))
 
-        def load_key_rows():
-            nc.sync.dma_start(out=key_scale_tab[0:P:8, :].bitcast(I32), in_=tab_scales[0].bitcast(I32))
-
-        def load_val_rows():
-            nc.sync.dma_start(out=val_scale_tab[0:P:4, :].bitcast(I32),
-                              in_=tab2_scales.rearrange("a q t -> (a q) t").bitcast(I32))
-
-        def place_key_rows():
-            for r in range(4):
-                nc.sync.dma_start(out=key_plane[r:P:32, :].bitcast(I32), in_=key_rows[8 * r:P:32, :].bitcast(I32))
+        def place_gate_rows():
+            for r in range(1, 4):
+                nc.sync.dma_start(out=gate_planes[r:P:32, :].bitcast(I32), in_=gate_planes[8 * r:P:32, :].bitcast(I32))
 
         def place_val_rows(a, r0, r1):
             for r in range(r0, r1):
-                nc.sync.dma_start(out=val_plane[VAL_ROW + 4 * a + r:P:32, :].bitcast(I32),
+                nc.sync.dma_start(out=val_plane[4 * a + r:P:32, :].bitcast(I32),
                                   in_=val_rows[64 * a + 4 * r:64 * (a + 1):16, :].bitcast(I32))
 
         def gather(picked, window, lst, j0, j1):
@@ -111,7 +105,8 @@ def tile_list_memory_kv_swiglu_kernel(tc, tab_words, tab_scales, tab2_words, tab
             nc.vector.quantize_mx(out=codes.bitcast(FP8X4), scales=plane, in_=src)
 
         key_codes = held([P, S], U32, "key_codes")
-        key_plane = held([P, S], U8, "key_plane")
+        gate_planes = held([P, S + H], U8, "gate_planes")
+        key_plane = gate_planes[:, :S]
         val_codes = [held([P, S], U32, "val_codes%d" % a) for a in range(2)]
         val_plane = held([P, S], U8, "val_plane")
         key_rows = held([P, S], U8, "key_rows")
@@ -133,7 +128,7 @@ def tile_list_memory_kv_swiglu_kernel(tc, tab_words, tab_scales, tab2_words, tab
             quantize(wv_codes[a, b][:], wv_planes[a, b][:], wv_bf[a, b].rearrange("p t q i -> p (t q i)"))
 
         wk_codes = held([P, 2 * H], U8, "wk_codes")
-        wk_plane = held([P, H], U8, "wk_plane")
+        wk_plane = gate_planes[:, S:]
 
         def deal_wk_words():
             nc.vector.tensor_copy(
@@ -142,7 +137,7 @@ def tile_list_memory_kv_swiglu_kernel(tc, tab_words, tab_scales, tab2_words, tab
 
         def deal_wk_scales():
             nc.vector.tensor_copy(
-                out=wk_plane[:].rearrange("p (b t m) -> p b t m", b=2, t=PACK),
+                out=wk_plane.rearrange("p (b t m) -> p b t m", b=2, t=PACK),
                 in_=wk_scale_raw[:].rearrange("p (b m t) -> p b t m", b=2, t=PACK))
 
         turns = {}
@@ -175,21 +170,20 @@ def tile_list_memory_kv_swiglu_kernel(tc, tab_words, tab_scales, tab2_words, tab
         val_banks = {}
         h_bf = {}
 
-        def values(b, jc, a, banks):
+        def values(b, jc, bank):
             c0 = jc * CHUNK
-            if a == 0:
-                val_banks[b, jc] = bank_from(banks, [P, PACK, CHUNK])
-            for t in range(PACK):
+            val_banks[b, jc] = psum.tile([P, PACK, CHUNK], F32, name="bank%d" % bank)
+            for a, t in [(a, t) for a in range(2) for t in range(PACK)]:
                 nc.tensor.matmul_mx(out=val_banks[b, jc][:, t, :],
                                     lhsT=wv_codes[a, b][:, t * P:(t + 1) * P].bitcast(FP8X4),
                                     lhsT_scale=wv_planes[a, b][:, t * P:(t + 1) * P],
                                     rhs=val_codes[a][:, c0:c0 + CHUNK].bitcast(FP8X4),
-                                    rhs_scale=val_plane[VAL_ROW + 4 * a:, c0:c0 + CHUNK],
+                                    rhs_scale=val_plane[4 * a:, c0:c0 + CHUNK],
                                     start=(a == 0 and t == 0), stop=(a == 1 and t == PACK - 1))
 
-        def hidden(b, jc, banks, room=None):
-            values(b, jc, 0, banks)
-            values(b, jc, 1, banks)
+        def hidden(b, jc, bank, room=None):
+            if (b, jc) not in val_banks:
+                values(b, jc, bank)
             jp, w = divmod(jc, 2)
             if w == 0:
                 if room is None:
@@ -211,19 +205,28 @@ def tile_list_memory_kv_swiglu_kernel(tc, tab_words, tab_scales, tab2_words, tab
             cols = slice(w0 * CHUNK, w1 * CHUNK)
             quantize(h_codes[b, jp][:, cols], h_planes[b, jp][:, cols], h_bf[b, jp][:, w0 * PASS:w1 * PASS])
 
-        wd_bf = [held([P, 2 * WD_COLS * PACK], BF16, "wd_bf%d" % c)[:].rearrange("p (b n) -> p b n", b=2) for c in range(3)]
+        wd_bf = {}
+        for c in range(3):
+            both = held([P, 2 * WD_COLS * PACK], BF16, "wd_bf%d" % c)
+            for b in range(2):
+                wd_bf[b, c] = both[:, b * WD_COLS * PACK:(b + 1) * WD_COLS * PACK]
+            wd_bf[c] = both[:]
         wd_codes = [held([P, 2 * WD_COLS], U32, "wd_codes%d" % c) for c in range(3)]
         wd_planes = [held([P, 2 * WD_COLS], U8, "wd_plane%d" % c) for c in range(3)]
 
         def cast_wd(b, c, engine, n0=0, n1=WD_COLS):
-            copy_on(engine, wd_bf[c][:, b, n0 * PACK:n1 * PACK].rearrange("p (m e i) -> p m i e", e=4, i=PACK),
+            copy_on(engine, wd_bf[b, c][:, n0 * PACK:n1 * PACK].rearrange("p (m e i) -> p m i e", e=4, i=PACK),
                     wd_raw[b, c][:, :, n0:n1].rearrange("p i (m e) -> p m i e", e=4))
 
         def quantize_wd(c):
-            quantize(wd_codes[c][:], wd_planes[c][:], wd_bf[c].rearrange("p b n -> p (b n)"))
+            quantize(wd_codes[c][:], wd_planes[c][:], wd_bf[c])
 
-        def project(v0, nv, j0, width, engine, banks):
-            bank = bank_from(banks, [P, nv, width])
+        def quantize_wd_piece(b, c):
+            cols = slice(b * WD_COLS, (b + 1) * WD_COLS)
+            quantize(wd_codes[c][:, cols], wd_planes[c][:, cols], wd_bf[b, c])
+
+        def project(v0, nv, j0, width, engine, bank_index, room=None):
+            bank = psum.tile([P, nv, width], F32, name="bank%d" % bank_index)
             step = min(width, PAIR)
             passes = [(b, w, j) for b in range(2) for w in range(nv) for j in range(j0, j0 + width, step)]
             for b, w, j in passes:
@@ -236,32 +239,36 @@ def tile_list_memory_kv_swiglu_kernel(tc, tab_words, tab_scales, tab2_words, tab
                                     rhs=h_codes[b, jp][:, c0:c0 + step].bitcast(FP8X4),
                                     rhs_scale=h_planes[b, jp][:, c0:c0 + step],
                                     start=(b, w, j) == passes[0], stop=(b, w, j) == passes[-1])
-            result = keep.tile([P, nv, width], F32, name="result", bufs=RESULT_BUFS)[:]
+            if room is None:
+                result = keep.tile([P, nv, width], F32, name="result", bufs=RESULT_BUFS)[:]
+            else:
+                result = room.rearrange("p (v j) -> p v j", v=nv)
             copy_on(engine, result, bank[:])
             rows = out[v0 * P:(v0 + nv) * P, j0:j0 + width]
             nc.sync.dma_start(out=rows.rearrange("(v p) j -> p v j", p=P), in_=result)
 
         nc.vector.memset(key_scale_tab[:].bitcast(I32), 0)
-        nc.vector.memset(val_scale_tab[:].bitcast(I32), 0)
         nc.vector.memset(wk_scale_raw[:].bitcast(I32), 0)
-        nc.vector.memset(key_plane[:].bitcast(I32), 0)
+        nc.vector.memset(val_scale_tab[:].bitcast(I32), 0)
         nc.vector.memset(val_plane[:].bitcast(I32), 0)
         nc.sync.dma_start(key_list[:], offs)
-        nc.sync.dma_start(val_list[:], offs2)
         nc.sync.dma_start(out=wk_raw[:], in_=wk_words[0].bitcast(I32))
-        load_key_rows()
-        load_val_rows()
-        load_plane(wk_scale_raw, wk_scales)
+        load_rows(key_scale_tab, 8, tab_scales[0])
+        load_rows(wk_scale_raw, 8, wk_scales[0])
+        nc.sync.dma_start(val_list[:], offs2)
+        load_rows(val_scale_tab, 4, tab2_scales.rearrange("a q t -> (a q) t"))
         load_words(key_tab, tab_words, 0)
+        load_words(val_tab[0], tab2_words, 0, 0, 1024)
         deal_wk_words()
         gather(key_rows, key_scale_tab, key_list, 0, S)
-        place_key_rows()
-        load_words(val_tab[0], tab2_words, 0)
-        gather(val_rows, val_scale_tab, val_list, 0, S)
         deal_wk_scales()
+        nc.vector.tensor_copy(out=key_plane.bitcast(I32), in_=key_rows[:].bitcast(I32))
+        place_gate_rows()
+        load_words(val_tab[0], tab2_words, 0, 1024, T2)
+        gather(val_rows, val_scale_tab, val_list, 0, S)
         load_wv(0, 0)
-        place_val_rows(0, 0, 2)
         load_wv(1, 0)
+        place_val_rows(0, 0, 2)
         load_words(val_tab[1], tab2_words, 1)
         place_val_rows(0, 2, 4)
         place_val_rows(1, 0, 4)
@@ -278,56 +285,58 @@ def tile_list_memory_kv_swiglu_kernel(tc, tab_words, tab_scales, tab2_words, tab
         cast_wv(0, 0, "vector")
         for jc in range(8):
             gate(1, jc, raw_rooms["wv_raw00"][:, LEAD + jc * PASS:LEAD + (jc + 1) * PASS] if jc < 4 else None)
-        quantize_wv(0, 0)
         cast_wv(1, 0, "vector")
+        quantize_wv(0, 0, tag="wv_raw10")
         quantize_wv(1, 0)
         for u in range(2):
             gather(val_codes[1], val_tab[1], val_list, u * HALF, (u + 1) * HALF)
         cast_wv(0, 1, "scalar")
         cast_wv(1, 1, "scalar", 0, P // 2)
-        hidden(0, 0, FIRST_BANKS)
-        hidden(0, 1, FIRST_BANKS)
-        hidden(0, 2, FIRST_BANKS)
+        hidden(0, 0, 3)
+        hidden(0, 1, 4)
+        hidden(0, 2, 5)
         quantize_h(0, 0)
-        hidden(0, 3, FIRST_BANKS)
-        hidden(0, 4, FIRST_BANKS)
-        hidden(0, 5, FIRST_BANKS)
-        cast_wv(1, 1, "vector", P // 2, P)
+        hidden(0, 3, 3)
+        hidden(0, 4, 4)
+        hidden(0, 5, 5)
         quantize_wv(0, 1)
+        cast_wv(1, 1, "vector", P // 2, P)
+        quantize_h(0, 2, tag="wv_raw01")
         quantize_wv(1, 1)
-        hidden(0, 6, FIRST_BANKS, both_behind("wv_raw11"))
+        hidden(0, 6, 3, both_behind("wv_raw11"))
+        values(0, 7, 4)
         quantize_h(0, 1, tag="wv_bf11")
         for c in range(2):
             for b in range(2):
                 cast_wd(b, c, "scalar")
-        hidden(1, 0, SECOND_BANKS)
-        hidden(1, 1, SECOND_BANKS)
+        hidden(1, 0, 6)
+        hidden(1, 1, 7)
         quantize_wd(0)
         quantize_h(1, 0)
-        hidden(1, 2, SECOND_BANKS)
-        project(0, 2, 0, PAIR, "scalar", (4,))
-        cast_wd(0, 2, "scalar")
-        hidden(1, 3, SECOND_BANKS)
-        quantize_h(0, 2, tag="wd_bf0")
-        quantize_h(1, 1)
+        hidden(1, 2, 0)
+        for n0 in (0, WD_COLS // 2):
+            cast_wd(0, 2, "scalar", n0, n0 + WD_COLS // 2)
+        project(0, 2, 0, PAIR, "scalar", 3, raw_rooms["wd_raw02"][:, :PASS])
+        hidden(1, 3, 1)
         quantize_wd(1)
-        project(0, 2, PAIR, PAIR, "scalar", (5,))
-        for v in (2, 3):
-            project(v, 1, 0, HALF, "scalar", ((3,), (4,))[v - 2])
-        hidden(1, 4, SECOND_BANKS)
-        hidden(1, 5, SECOND_BANKS)
+        quantize_h(1, 1)
+        project(2, 2, 0, PAIR, "scalar", 0)
+        for c in range(2):
+            project(2 * c, 2, PAIR, PAIR, "scalar", (1, 3)[c])
+        hidden(1, 4, 2)
+        hidden(1, 5, 5)
         cast_wd(1, 2, "vector")
         quantize_h(1, 2)
         quantize_wd(2)
         for c in range(2):
-            project(2 * c, 2, 2 * PAIR, PAIR, "scalar", ((2,), (5,))[c])
-        hidden(0, 7, SECOND_BANKS)
-        hidden(1, 6, SECOND_BANKS)
-        quantize_h(0, 3)
-        hidden(1, 7, SECOND_BANKS)
+            project(2 * c, 2, 2 * PAIR, PAIR, "scalar", (2, 5)[c])
         for v in (4, 5):
-            project(v, 1, 0, HALF, "scalar", ((6,), (3,))[v - 4])
-        project(4, 2, 2 * PAIR, PAIR, "scalar", (4,))
+            project(v, 1, 0, HALF, "scalar", (0, 1)[v - 4])
+        project(4, 2, 2 * PAIR, PAIR, "scalar", 3)
+        hidden(0, 7, 4)
+        hidden(1, 6, 6)
+        hidden(1, 7, 7)
+        quantize_h(0, 3)
         quantize_h(1, 3)
         for c in range(3):
-            project(2 * c, 2, 3 * PAIR, PAIR, "scalar" if c == 1 else "vector", ((7,), (0,), (2,))[c])
+            project(2 * c, 2, 3 * PAIR, PAIR, "scalar" if c == 1 else "vector", (4, 6, 7)[c])

@@ -24,13 +24,10 @@ HALF = S // 2
 CHUNK = 128
 PAIR = 2 * CHUNK
 WD_COLS = 256
-GATE_BANKS = (0, 1, 2)
-FIRST_BANKS = (3, 4, 5)
-SECOND_BANKS = (6, 7, 0, 1, 2)
+GATE_BANKS = 3
 H_BUFS = 4
-RESULT_BUFS = 8
 LEAD = 256
-RESULT_LEAD = 384
+RESULT_ROOMS = ("key_tab", "val_tab0", "val_tab1", "key_scale_tab", None, None)
 
 
 def tile_list_memory_kv_swiglu_kernel(tc, tab_words, tab_scales, tab2_words, tab2_scales, offs, offs2,
@@ -57,9 +54,8 @@ def tile_list_memory_kv_swiglu_kernel(tc, tab_words, tab_scales, tab2_words, tab
         raw_rooms = {}
 
         def raw_tile(name, words):
-            lead = RESULT_LEAD if name == "wd_raw02" else LEAD
-            raw_rooms[name] = held([P, lead + words], F32, name)
-            return raw_rooms[name][:, lead:]
+            raw_rooms[name] = held([P, LEAD + words], F32, name)
+            return raw_rooms[name][:, LEAD:]
 
         def load_wv(a, b):
             wv_raw[a, b] = raw_tile("wv_raw%d%d" % (a, b), PACK * PASS).rearrange("p (i r) -> p i r", i=PACK)
@@ -140,18 +136,11 @@ def tile_list_memory_kv_swiglu_kernel(tc, tab_words, tab_scales, tab2_words, tab
                 out=wk_plane.rearrange("p (b t m) -> p b t m", b=2, t=PACK),
                 in_=wk_scale_raw[:].rearrange("p (b m t) -> p b t m", b=2, t=PACK))
 
-        turns = {}
-
-        def bank_from(banks, shape):
-            k = turns.get(banks, 0)
-            turns[banks] = k + 1
-            return psum.tile(shape, F32, name="bank%d" % banks[k % len(banks)])
-
         gates = {}
 
         def gate(b, jc, room=None):
             c0 = jc * CHUNK
-            bank = bank_from(GATE_BANKS, [P, PACK, CHUNK])
+            bank = psum.tile([P, PACK, CHUNK], F32, name="bank%d" % ((8 * b + jc) % GATE_BANKS))
             for t in range(PACK):
                 r0 = b * PASS + t * P
                 nc.tensor.matmul_mx(out=bank[:, t, :],
@@ -225,7 +214,9 @@ def tile_list_memory_kv_swiglu_kernel(tc, tab_words, tab_scales, tab2_words, tab
             cols = slice(b * WD_COLS, (b + 1) * WD_COLS)
             quantize(wd_codes[c][:, cols], wd_planes[c][:, cols], wd_bf[b, c])
 
-        def project(v0, nv, j0, width, engine, bank_index, room=None):
+        results = {}
+
+        def project(v0, nv, j0, width, engine, bank_index):
             bank = psum.tile([P, nv, width], F32, name="bank%d" % bank_index)
             step = min(width, PAIR)
             passes = [(b, w, j) for b in range(2) for w in range(nv) for j in range(j0, j0 + width, step)]
@@ -239,13 +230,16 @@ def tile_list_memory_kv_swiglu_kernel(tc, tab_words, tab_scales, tab2_words, tab
                                     rhs=h_codes[b, jp][:, c0:c0 + step].bitcast(FP8X4),
                                     rhs_scale=h_planes[b, jp][:, c0:c0 + step],
                                     start=(b, w, j) == passes[0], stop=(b, w, j) == passes[-1])
-            if room is None:
-                result = keep.tile([P, nv, width], F32, name="result", bufs=RESULT_BUFS)[:]
-            else:
-                result = room.rearrange("p (v j) -> p v j", v=nv)
-            copy_on(engine, result, bank[:])
-            rows = out[v0 * P:(v0 + nv) * P, j0:j0 + width]
-            nc.sync.dma_start(out=rows.rearrange("(v p) j -> p v j", p=P), in_=result)
+            u, c0 = divmod(j0, HALF)
+            c, w0 = divmod(v0, 2)
+            if (c, u) not in results:
+                results[c, u] = held([P, 2, HALF], F32, "result%d%d" % (c, u), RESULT_ROOMS[3 * u + c])
+            copy_on(engine, results[c, u][:, w0:w0 + nv, c0:c0 + width], bank[:])
+
+        def store(v0, nv, u):
+            c, w0 = divmod(v0, 2)
+            rows = out[v0 * P:(v0 + nv) * P, u * HALF:(u + 1) * HALF]
+            nc.sync.dma_start(out=rows.rearrange("(v p) j -> p v j", p=P), in_=results[c, u][:, w0:w0 + nv, :])
 
         nc.vector.memset(key_scale_tab[:].bitcast(I32), 0)
         nc.vector.memset(wk_scale_raw[:].bitcast(I32), 0)
@@ -314,25 +308,25 @@ def tile_list_memory_kv_swiglu_kernel(tc, tab_words, tab_scales, tab2_words, tab
         quantize_wd(0)
         quantize_h(1, 0)
         hidden(1, 2, 0)
-        for n0 in (0, WD_COLS // 2):
-            cast_wd(0, 2, "scalar", n0, n0 + WD_COLS // 2)
-        project(0, 2, 0, PAIR, "scalar", 3, raw_rooms["wd_raw02"][:, :PASS])
+        cast_wd(0, 2, "scalar")
+
         hidden(1, 3, 1)
         quantize_wd(1)
         quantize_h(1, 1)
-        project(2, 2, 0, PAIR, "scalar", 0)
-        for c in range(2):
-            project(2 * c, 2, PAIR, PAIR, "scalar", (1, 3)[c])
+        for v in range(4):
+            project(v, 1, 0, HALF, "scalar", (3, 0, 1, 3)[v])
+            store(v, 1, 0)
         hidden(1, 4, 2)
         hidden(1, 5, 5)
         cast_wd(1, 2, "vector")
         quantize_h(1, 2)
+
         quantize_wd(2)
-        for c in range(2):
-            project(2 * c, 2, 2 * PAIR, PAIR, "scalar", (2, 5)[c])
         for v in (4, 5):
             project(v, 1, 0, HALF, "scalar", (0, 1)[v - 4])
-        project(4, 2, 2 * PAIR, PAIR, "scalar", 3)
+            store(v, 1, 0)
+        for c in range(3):
+            project(2 * c, 2, 2 * PAIR, PAIR, "scalar", (2, 5, 3)[c])
         hidden(0, 7, 4)
         hidden(1, 6, 6)
         hidden(1, 7, 7)
@@ -340,3 +334,4 @@ def tile_list_memory_kv_swiglu_kernel(tc, tab_words, tab_scales, tab2_words, tab
         quantize_h(1, 3)
         for c in range(3):
             project(2 * c, 2, 3 * PAIR, PAIR, "scalar" if c == 1 else "vector", (4, 6, 7)[c])
+            store(2 * c, 2, 1)

@@ -77,6 +77,14 @@ def tile_list_memory_kv_swiglu_kernel(tc, tab_words, tab_scales, tab2_words, tab
         def load_rows(tile, step, rows):
             nc.sync.dma_start(out=tile[0:P:step, :].bitcast(I32), in_=rows.bitcast(I32))
 
+        def load_plane(plane, scales):
+            for r in range(4):
+                nc.sync.dma_start(out=plane[r:P:32, :].bitcast(I32), in_=scales[0, r:16:4, :].bitcast(I32))
+
+        def place_key_rows():
+            for r in range(4):
+                nc.sync.dma_start(out=key_plane[r:P:32, :].bitcast(I32), in_=key_rows[8 * r:P:32, :].bitcast(I32))
+
         def place_gate_rows():
             for r in range(1, 4):
                 nc.sync.dma_start(out=gate_planes[r:P:32, :].bitcast(I32), in_=gate_planes[8 * r:P:32, :].bitcast(I32))
@@ -236,33 +244,33 @@ def tile_list_memory_kv_swiglu_kernel(tc, tab_words, tab_scales, tab2_words, tab
                 results[c, u] = held([P, 2, HALF], F32, "result%d%d" % (c, u), RESULT_ROOMS[3 * u + c])
             copy_on(engine, results[c, u][:, w0:w0 + nv, c0:c0 + width], bank[:])
 
-        def store(v0, nv, u):
+        def store(v0, nv, j0, width):
+            u, c0 = divmod(j0, HALF)
             c, w0 = divmod(v0, 2)
-            rows = out[v0 * P:(v0 + nv) * P, u * HALF:(u + 1) * HALF]
-            nc.sync.dma_start(out=rows.rearrange("(v p) j -> p v j", p=P), in_=results[c, u][:, w0:w0 + nv, :])
+            rows = out[v0 * P:(v0 + nv) * P, j0:j0 + width]
+            nc.sync.dma_start(out=rows.rearrange("(v p) j -> p v j", p=P), in_=results[c, u][:, w0:w0 + nv, c0:c0 + width])
 
         nc.vector.memset(key_scale_tab[:].bitcast(I32), 0)
-        nc.vector.memset(wk_scale_raw[:].bitcast(I32), 0)
         nc.vector.memset(val_scale_tab[:].bitcast(I32), 0)
+        nc.vector.memset(wk_scale_raw[:].bitcast(I32), 0)
+        nc.vector.memset(key_plane.bitcast(I32), 0)
         nc.vector.memset(val_plane[:].bitcast(I32), 0)
         nc.sync.dma_start(key_list[:], offs)
+        nc.sync.dma_start(val_list[:], offs2)
         nc.sync.dma_start(out=wk_raw[:], in_=wk_words[0].bitcast(I32))
         load_rows(key_scale_tab, 8, tab_scales[0])
-        load_rows(wk_scale_raw, 8, wk_scales[0])
-        nc.sync.dma_start(val_list[:], offs2)
         load_rows(val_scale_tab, 4, tab2_scales.rearrange("a q t -> (a q) t"))
+        load_plane(wk_scale_raw, wk_scales)
         load_words(key_tab, tab_words, 0)
-        load_words(val_tab[0], tab2_words, 0, 0, 1024)
         deal_wk_words()
         gather(key_rows, key_scale_tab, key_list, 0, S)
-        deal_wk_scales()
-        nc.vector.tensor_copy(out=key_plane.bitcast(I32), in_=key_rows[:].bitcast(I32))
-        place_gate_rows()
-        load_words(val_tab[0], tab2_words, 0, 1024, T2)
+        place_key_rows()
+        load_words(val_tab[0], tab2_words, 0)
         gather(val_rows, val_scale_tab, val_list, 0, S)
+        deal_wk_scales()
         load_wv(0, 0)
-        load_wv(1, 0)
         place_val_rows(0, 0, 2)
+        load_wv(1, 0)
         load_words(val_tab[1], tab2_words, 1)
         place_val_rows(0, 2, 4)
         place_val_rows(1, 0, 4)
@@ -279,8 +287,8 @@ def tile_list_memory_kv_swiglu_kernel(tc, tab_words, tab_scales, tab2_words, tab
         cast_wv(0, 0, "vector")
         for jc in range(8):
             gate(1, jc, raw_rooms["wv_raw00"][:, LEAD + jc * PASS:LEAD + (jc + 1) * PASS] if jc < 4 else None)
+        quantize_wv(0, 0)
         cast_wv(1, 0, "vector")
-        quantize_wv(0, 0, tag="wv_raw10")
         quantize_wv(1, 0)
         for u in range(2):
             gather(val_codes[1], val_tab[1], val_list, u * HALF, (u + 1) * HALF)
@@ -308,24 +316,29 @@ def tile_list_memory_kv_swiglu_kernel(tc, tab_words, tab_scales, tab2_words, tab
         quantize_wd(0)
         quantize_h(1, 0)
         hidden(1, 2, 0)
+        project(0, 2, 0, PAIR, "scalar", 3)
+        store(0, 2, 0, PAIR)
         cast_wd(0, 2, "scalar")
-
         hidden(1, 3, 1)
         quantize_wd(1)
         quantize_h(1, 1)
-        for v in range(4):
-            project(v, 1, 0, HALF, "scalar", (3, 0, 1, 3)[v])
-            store(v, 1, 0)
+        project(0, 2, PAIR, PAIR, "scalar", 1)
+        store(0, 2, PAIR, PAIR)
+        for v in (2, 3):
+            project(v, 1, 0, HALF, "scalar", (0, 3)[v - 2])
+            store(v, 1, 0, HALF)
         hidden(1, 4, 2)
         hidden(1, 5, 5)
         cast_wd(1, 2, "vector")
         quantize_h(1, 2)
-
         quantize_wd(2)
+        for c in range(1):
+            project(2 * c, 2, 2 * PAIR, PAIR, "scalar", (2, 5)[c])
+            store(2 * c, 2, 2 * PAIR, PAIR)
         for v in (4, 5):
             project(v, 1, 0, HALF, "scalar", (0, 1)[v - 4])
-            store(v, 1, 0)
-        for c in range(3):
+            store(v, 1, 0, HALF)
+        for c in range(1, 3):
             project(2 * c, 2, 2 * PAIR, PAIR, "scalar", (2, 5, 3)[c])
         hidden(0, 7, 4)
         hidden(1, 6, 6)
@@ -334,4 +347,7 @@ def tile_list_memory_kv_swiglu_kernel(tc, tab_words, tab_scales, tab2_words, tab
         quantize_h(1, 3)
         for c in range(3):
             project(2 * c, 2, 3 * PAIR, PAIR, "scalar" if c == 1 else "vector", (4, 6, 7)[c])
-            store(2 * c, 2, 1)
+            if c < 1:
+                store(2 * c, 2, 3 * PAIR, PAIR)
+            else:
+                store(2 * c, 2, HALF, HALF)

@@ -85,10 +85,6 @@ def tile_list_memory_kv_swiglu_kernel(tc, tab_words, tab_scales, tab2_words, tab
             for r in range(4):
                 nc.sync.dma_start(out=key_plane[r:P:32, :].bitcast(I32), in_=key_rows[8 * r:P:32, :].bitcast(I32))
 
-        def place_gate_rows():
-            for r in range(1, 4):
-                nc.sync.dma_start(out=gate_planes[r:P:32, :].bitcast(I32), in_=gate_planes[8 * r:P:32, :].bitcast(I32))
-
         def place_val_rows(a, r0, r1):
             for r in range(r0, r1):
                 nc.sync.dma_start(out=val_plane[4 * a + r:P:32, :].bitcast(I32),
@@ -109,8 +105,7 @@ def tile_list_memory_kv_swiglu_kernel(tc, tab_words, tab_scales, tab2_words, tab
             nc.vector.quantize_mx(out=codes.bitcast(FP8X4), scales=plane, in_=src)
 
         key_codes = held([P, S], U32, "key_codes")
-        gate_planes = held([P, S + H], U8, "gate_planes")
-        key_plane = gate_planes[:, :S]
+        key_plane = held([P, S], U8, "key_plane")[:]
         val_codes = [held([P, S], U32, "val_codes%d" % a) for a in range(2)]
         val_plane = held([P, S], U8, "val_plane")
         key_rows = held([P, S], U8, "key_rows")
@@ -132,7 +127,7 @@ def tile_list_memory_kv_swiglu_kernel(tc, tab_words, tab_scales, tab2_words, tab
             quantize(wv_codes[a, b][:], wv_planes[a, b][:], wv_bf[a, b].rearrange("p t q i -> p (t q i)"))
 
         wk_codes = held([P, 2 * H], U8, "wk_codes")
-        wk_plane = gate_planes[:, S:]
+        wk_plane = held([P, H], U8, "wk_plane")[:]
 
         def deal_wk_words():
             nc.vector.tensor_copy(
@@ -332,22 +327,22 @@ def tile_list_memory_kv_swiglu_kernel(tc, tab_words, tab_scales, tab2_words, tab
         cast_wd(1, 2, "vector")
         quantize_h(1, 2)
         quantize_wd(2)
-        for c in range(1):
+        for c in range(2):
             project(2 * c, 2, 2 * PAIR, PAIR, "scalar", (2, 5)[c])
             store(2 * c, 2, 2 * PAIR, PAIR)
         for v in (4, 5):
             project(v, 1, 0, HALF, "scalar", (0, 1)[v - 4])
             store(v, 1, 0, HALF)
-        for c in range(1, 3):
+        for c in range(2, 3):
             project(2 * c, 2, 2 * PAIR, PAIR, "scalar", (2, 5, 3)[c])
         hidden(0, 7, 4)
         hidden(1, 6, 6)
         hidden(1, 7, 7)
         quantize_h(0, 3)
         quantize_h(1, 3)
-        for c in range(3):
-            project(2 * c, 2, 3 * PAIR, PAIR, "scalar" if c == 1 else "vector", (4, 6, 7)[c])
-            if c < 1:
-                store(2 * c, 2, 3 * PAIR, PAIR)
-            else:
-                store(2 * c, 2, HALF, HALF)
+        for v in range(2):
+            project(v, 1, 3 * PAIR, PAIR, ("vector", "scalar")[v], (4, 2)[v])
+        store(0, 2, 3 * PAIR, PAIR)
+        for c in (1, 2):
+            project(2 * c, 2, 3 * PAIR, PAIR, ("vector", "scalar")[c - 1], (6, 7)[c - 1])
+            store(2 * c, 2, 3 * PAIR if c == 1 else HALF, PAIR if c == 1 else HALF)

@@ -306,21 +306,17 @@ def tile_list_memory_kv_swiglu_kernel(tc, tab_words, tab_scales, tab2_words, tab
         for c in range(2):
             for b in range(2):
                 cast_wd(b, c, "scalar")
+        cast_wd(0, 2, "scalar")
         hidden(1, 0, 6)
         hidden(1, 1, 7)
-        quantize_wd(0)
-        quantize_h(1, 0)
         hidden(1, 2, 0)
-        project(0, 2, 0, PAIR, "scalar", 3)
-        store(0, 2, 0, PAIR)
-        cast_wd(0, 2, "scalar")
+        quantize_h(1, 0)
         hidden(1, 3, 1)
-        quantize_wd(1)
+        quantize_wd(0)
         quantize_h(1, 1)
-        project(0, 2, PAIR, PAIR, "scalar", 1)
-        store(0, 2, PAIR, PAIR)
-        for v in (2, 3):
-            project(v, 1, 0, HALF, "scalar", (0, 3)[v - 2])
+        quantize_wd(1)
+        for v in range(4):
+            project(v, 1, 0, HALF, "scalar", (3, 0, 1, 3)[v])
             store(v, 1, 0, HALF)
         hidden(1, 4, 2)
         hidden(1, 5, 5)
@@ -340,9 +336,9 @@ def tile_list_memory_kv_swiglu_kernel(tc, tab_words, tab_scales, tab2_words, tab
         hidden(1, 7, 7)
         quantize_h(0, 3)
         quantize_h(1, 3)
-        for v in range(2):
-            project(v, 1, 3 * PAIR, PAIR, ("vector", "scalar")[v], (4, 2)[v])
-        store(0, 2, 3 * PAIR, PAIR)
-        for c in (1, 2):
-            project(2 * c, 2, 3 * PAIR, PAIR, ("vector", "scalar")[c - 1], (6, 7)[c - 1])
-            store(2 * c, 2, 3 * PAIR if c == 1 else HALF, PAIR if c == 1 else HALF)
+        for v in (4, 5):
+            project(v, 1, 3 * PAIR, PAIR, ("vector", "scalar")[v - 4], (4, 2)[v - 4])
+        store(4, 2, HALF, HALF)
+        for c in range(2):
+            project(2 * c, 2, 3 * PAIR, PAIR, ("vector", "scalar")[c], (6, 7)[c])
+            store(2 * c, 2, 3 * PAIR, PAIR)

@@ -15,19 +15,13 @@ FP8X4 = mybir.dt.float8_e4m3fn_x4
 FP4X4 = mybir.dt.float4_e2m1fn_x4
 SILU = mybir.ActivationFunctionType.Silu
 MULT = mybir.AluOpType.mult
-ADD = mybir.AluOpType.add
 
 P = 128
 PACK = 4
 PASS = P * PACK
-HALF = S // 2
 CHUNK = 128
-PAIR = 2 * CHUNK
 WD_COLS = 256
 GATE_BANKS = 3
-H_BUFS = 4
-LEAD = 256
-RESULT_ROOMS = ("key_tab", "val_tab0", "val_tab1", "key_scale_tab", None, None)
 
 
 def tile_list_memory_kv_swiglu_kernel(tc, tab_words, tab_scales, tab2_words, tab2_scales, offs, offs2,
@@ -40,6 +34,9 @@ def tile_list_memory_kv_swiglu_kernel(tc, tab_words, tab_scales, tab2_words, tab
         def held(shape, dtype, name, tag=None):
             return keep.tile(shape, dtype, name=name, tag=tag or name, align_bytes=64)
 
+        def bank_tile(index, shape):
+            return psum.tile(shape, F32, name="bank%d" % index)
+
         key_list = keep.tile([P, S // 16], U16, name="key_list")
         val_list = keep.tile([P, S // 16], U16, name="val_list")
         key_scale_tab = held([P, T], U8, "key_scale_tab")
@@ -48,86 +45,52 @@ def tile_list_memory_kv_swiglu_kernel(tc, tab_words, tab_scales, tab2_words, tab
         wk_raw = held([P, H // 2], I32, "wk_raw")
         key_tab = held([P, T], U32, "key_tab")
         val_tab = [held([P, T2], U32, "val_tab%d" % a) for a in range(2)]
-        wv_raw = {}
-        wd_raw = {}
-
-        raw_rooms = {}
-
-        def raw_tile(name, words):
-            raw_rooms[name] = held([P, LEAD + words], F32, name)
-            return raw_rooms[name][:, LEAD:]
-
-        def load_wv(a, b):
-            wv_raw[a, b] = raw_tile("wv_raw%d%d" % (a, b), PACK * PASS).rearrange("p (i r) -> p i r", i=PACK)
-            rows = wv[a * PASS:(a + 1) * PASS, b * PASS:(b + 1) * PASS]
-            nc.sync.dma_start(out=wv_raw[a, b], in_=rows.rearrange("(p i) r -> p i r", i=PACK))
-
-        def load_wd(b, c0, c1):
-            width = (c1 - c0) * WD_COLS
-            raw = raw_tile("wd_raw%d%d" % (b, c0), PACK * width).rearrange("p (t n) -> p t n", t=PACK)
-            rows = wd[b * PASS:(b + 1) * PASS, c0 * WD_COLS:c1 * WD_COLS]
-            nc.sync.dma_start(out=raw, in_=rows.rearrange("(p t) n -> p t n", t=PACK))
-            for c in range(c0, c1):
-                wd_raw[b, c] = raw[:, :, (c - c0) * WD_COLS:(c - c0 + 1) * WD_COLS]
-
-        def load_words(tile, table, a, t0=0, t1=None):
-            words = table[a].rearrange("p t i -> p (t i)").bitcast(I32)
-            nc.sync.dma_start(out=tile[:, t0:t1].bitcast(I32), in_=words[:, t0:t1])
-
-        def load_rows(tile, step, rows):
-            nc.sync.dma_start(out=tile[0:P:step, :].bitcast(I32), in_=rows.bitcast(I32))
-
-        def load_plane(plane, scales):
-            for r in range(4):
-                nc.sync.dma_start(out=plane[r:P:32, :].bitcast(I32), in_=scales[0, r:16:4, :].bitcast(I32))
-
-        def place_key_rows():
-            for r in range(4):
-                nc.sync.dma_start(out=key_plane[r:P:32, :].bitcast(I32), in_=key_rows[8 * r:P:32, :].bitcast(I32))
-
-        def place_val_rows(a, r0, r1):
-            for r in range(r0, r1):
-                nc.sync.dma_start(out=val_plane[4 * a + r:P:32, :].bitcast(I32),
-                                  in_=val_rows[64 * a + 4 * r:64 * (a + 1):16, :].bitcast(I32))
-
-        def gather(picked, window, lst, j0, j1):
-            nc.vector.tensor_copy(out=picked[:, j0:j1], in_=window[:].indirect(lst[:, j0 // 16:j1 // 16]))
+        key_codes = held([P, S], U32, "key_codes")
+        key_plane = held([P, S], U8, "key_plane")
+        val_codes = {}
+        val_plane = held([P, S], U8, "val_plane")
+        key_rows = held([P, S], U8, "key_rows")
+        val_rows = held([P, S], U8, "val_rows")
+        wk_codes = held([P, 2 * H], U8, "wk_codes")
+        wk_plane = held([P, H], U8, "wk_plane")
 
         def copy_on(engine, dst, src):
             if engine == "scalar":
                 nc.scalar.copy(out=dst, in_=src)
-            elif engine == "gpsimd":
-                nc.gpsimd.tensor_scalar(out=dst, in0=src, scalar1=1.0, scalar2=0.0, op0=MULT, op1=ADD)
             else:
                 nc.vector.tensor_copy(out=dst, in_=src)
 
         def quantize(codes, plane, src):
             nc.vector.quantize_mx(out=codes.bitcast(FP8X4), scales=plane, in_=src)
 
-        key_codes = held([P, S], U32, "key_codes")
-        key_plane = held([P, S], U8, "key_plane")[:]
-        val_codes = [held([P, S], U32, "val_codes%d" % a) for a in range(2)]
-        val_plane = held([P, S], U8, "val_plane")
-        key_rows = held([P, S], U8, "key_rows")
-        val_rows = held([P, S], U8, "val_rows")
-        wv_bf = {}
-        wv_codes = {}
-        wv_planes = {}
+        def load_words(tile, table, a):
+            words = table[a].rearrange("p t i -> p (t i)").bitcast(I32)
+            nc.sync.dma_start(out=tile[:].bitcast(I32), in_=words)
 
-        def cast_wv(a, b, engine, m0=0, m1=P):
-            if (a, b) not in wv_bf:
-                wv_bf[a, b] = held([P, PACK * PASS], BF16, "wv_bf%d%d" % (a, b))[:].rearrange("p (t q i) -> p t q i", t=PACK, i=PACK)
-            dst = wv_bf[a, b][:, :, m0:m1, :].rearrange("p t m i -> p m i t")
-            src = wv_raw[a, b].rearrange("p i (m t) -> p m i t", t=PACK)[:, m0:m1, :, :]
-            copy_on(engine, dst, src)
+        def load_rows(tile, step, rows):
+            nc.sync.dma_start(out=tile[0:P:step, :].bitcast(I32), in_=rows.bitcast(I32))
 
-        def quantize_wv(a, b, tag=None):
-            wv_codes[a, b] = held([P, PASS], U32, "wv_codes%d%d" % (a, b), tag)
-            wv_planes[a, b] = held([P, PASS], U8, "wv_plane%d%d" % (a, b))
-            quantize(wv_codes[a, b][:], wv_planes[a, b][:], wv_bf[a, b].rearrange("p t q i -> p (t q i)"))
+        def load_wk_scales():
+            for r in range(4):
+                nc.sync.dma_start(out=wk_scale_raw[r:P:32, :].bitcast(I32), in_=wk_scales[0, r:16:4, :].bitcast(I32))
 
-        wk_codes = held([P, 2 * H], U8, "wk_codes")
-        wk_plane = held([P, H], U8, "wk_plane")[:]
+        def place_key_rows():
+            for r in range(4):
+                nc.sync.dma_start(out=key_plane[r:P:32, :].bitcast(I32), in_=key_rows[8 * r:P:32, :].bitcast(I32))
+
+        def place_val_rows(first, last):
+            for a, r in [divmod(e, 4) for e in range(first, last)]:
+                nc.sync.dma_start(out=val_plane[4 * a + r:P:32, :].bitcast(I32),
+                                  in_=val_rows[64 * a + 4 * r:64 * (a + 1):16, :].bitcast(I32))
+
+        def gather(picked, window, lst, j0, j1):
+            nc.vector.tensor_copy(out=picked[:, j0:j1], in_=window[:].indirect(lst[:, j0 // 16:j1 // 16]))
+
+        def gather_values(a, jc0, jc1, room=None):
+            picked = held([P, (jc1 - jc0) * CHUNK], U32, "val_codes%d%d" % (a, jc0), room)
+            nc.vector.tensor_copy(out=picked[:], in_=val_tab[a][:].indirect(val_list[:, jc0 * CHUNK // 16:jc1 * CHUNK // 16]))
+            for jc in range(jc0, jc1):
+                val_codes[a, jc] = picked[:, (jc - jc0) * CHUNK:(jc - jc0 + 1) * CHUNK]
 
         def deal_wk_words():
             nc.vector.tensor_copy(
@@ -136,14 +99,58 @@ def tile_list_memory_kv_swiglu_kernel(tc, tab_words, tab_scales, tab2_words, tab
 
         def deal_wk_scales():
             nc.vector.tensor_copy(
-                out=wk_plane.rearrange("p (b t m) -> p b t m", b=2, t=PACK),
+                out=wk_plane[:].rearrange("p (b t m) -> p b t m", b=2, t=PACK),
                 in_=wk_scale_raw[:].rearrange("p (b m t) -> p b t m", b=2, t=PACK))
+
+        wv_raw = {}
+        wv_bf = {}
+        wv_codes = {}
+        wv_planes = {}
+
+        def load_wv(a, b, m0, m1):
+            width = (m1 - m0) * PACK
+            wv_raw[a, b, m0] = held([P, PACK * width], F32, "wv_raw%d%d_%d" % (a, b, m0))
+            rows = wv[a * PASS:(a + 1) * PASS, b * PASS + m0 * PACK:b * PASS + m1 * PACK]
+            nc.sync.dma_start(out=wv_raw[a, b, m0][:].rearrange("p (i r) -> p i r", i=PACK),
+                              in_=rows.rearrange("(p i) r -> p i r", i=PACK))
+
+        def cast_wv(a, b, piece, m0, m1, engine):
+            if (a, b) not in wv_bf:
+                wv_bf[a, b] = held([P, PACK * PASS], BF16, "wv_bf%d%d" % (a, b))
+            dst = wv_bf[a, b][:].rearrange("p (t m i) -> p m i t", t=PACK, i=PACK)[:, m0:m1, :, :]
+            src = wv_raw[a, b, piece][:].rearrange("p (i m t) -> p m i t", i=PACK, t=PACK)[:, m0 - piece:m1 - piece, :, :]
+            copy_on(engine, dst, src)
+
+        def quantize_wv(a, b, room=None):
+            wv_codes[a, b] = held([P, PASS], U32, "wv_codes%d%d" % (a, b), room)
+            wv_planes[a, b] = held([P, PASS], U8, "wv_plane%d%d" % (a, b))
+            quantize(wv_codes[a, b][:], wv_planes[a, b][:], wv_bf[a, b][:])
+
+        wd_raw = {}
+        wd_bf = [held([P, 2 * WD_COLS * PACK], BF16, "wd_bf%d" % c) for c in range(3)]
+        wd_codes = [held([P, 2 * WD_COLS], U32, "wd_codes%d" % c) for c in range(3)]
+        wd_planes = [held([P, 2 * WD_COLS], U8, "wd_plane%d" % c) for c in range(3)]
+
+        def load_wd(b, c):
+            wd_raw[b, c] = held([P, PACK * WD_COLS], F32, "wd_raw%d%d" % (b, c))
+            rows = wd[b * PASS:(b + 1) * PASS, c * WD_COLS:(c + 1) * WD_COLS]
+            nc.sync.dma_start(out=wd_raw[b, c][:].rearrange("p (i n) -> p i n", i=PACK),
+                              in_=rows.rearrange("(p i) n -> p i n", i=PACK))
+
+        def cast_wd(b, c, engine):
+            words = WD_COLS * PACK
+            copy_on(engine, wd_bf[c][:, b * words:(b + 1) * words].rearrange("p (m e i) -> p m i e", e=4, i=PACK),
+                    wd_raw[b, c][:].rearrange("p (i m e) -> p m i e", i=PACK, e=4))
+
+        def quantize_wd(c, b0=0, b1=2):
+            cols = slice(b0 * WD_COLS, b1 * WD_COLS)
+            quantize(wd_codes[c][:, cols], wd_planes[c][:, cols], wd_bf[c][:, b0 * WD_COLS * PACK:b1 * WD_COLS * PACK])
 
         gates = {}
 
         def gate(b, jc, room=None):
             c0 = jc * CHUNK
-            bank = psum.tile([P, PACK, CHUNK], F32, name="bank%d" % ((8 * b + jc) % GATE_BANKS))
+            bank = bank_tile((8 * b + jc) % GATE_BANKS, [P, PACK, CHUNK])
             for t in range(PACK):
                 r0 = b * PASS + t * P
                 nc.tensor.matmul_mx(out=bank[:, t, :],
@@ -157,105 +164,82 @@ def tile_list_memory_kv_swiglu_kernel(tc, tab_words, tab_scales, tab2_words, tab
             gates[b, jc] = room.rearrange("p (j t) -> p j t", t=PACK)
             nc.scalar.activation(out=gates[b, jc], in_=bank[:].rearrange("p t j -> p j t"), func=SILU)
 
-        h_codes = {}
-        h_planes = {}
         val_banks = {}
-        h_bf = {}
 
-        def values(b, jc, bank):
+        def values(b, jc, a, bank=None):
             c0 = jc * CHUNK
-            val_banks[b, jc] = psum.tile([P, PACK, CHUNK], F32, name="bank%d" % bank)
-            for a, t in [(a, t) for a in range(2) for t in range(PACK)]:
+            if a == 0:
+                val_banks[b, jc] = bank_tile(bank, [P, PACK, CHUNK])
+            for t in range(PACK):
                 nc.tensor.matmul_mx(out=val_banks[b, jc][:, t, :],
                                     lhsT=wv_codes[a, b][:, t * P:(t + 1) * P].bitcast(FP8X4),
                                     lhsT_scale=wv_planes[a, b][:, t * P:(t + 1) * P],
-                                    rhs=val_codes[a][:, c0:c0 + CHUNK].bitcast(FP8X4),
+                                    rhs=val_codes[a, jc].bitcast(FP8X4),
                                     rhs_scale=val_plane[4 * a:, c0:c0 + CHUNK],
                                     start=(a == 0 and t == 0), stop=(a == 1 and t == PACK - 1))
 
-        def hidden(b, jc, bank, room=None):
-            if (b, jc) not in val_banks:
-                values(b, jc, bank)
-            jp, w = divmod(jc, 2)
-            if w == 0:
-                if room is None:
-                    room = keep.tile([P, 2 * PASS], BF16, name="h_bf", bufs=H_BUFS, align_bytes=64)[:]
-                h_bf[b, jp] = room
-            nc.vector.tensor_tensor(out=h_bf[b, jp][:, w * PASS:(w + 1) * PASS].rearrange("p (j t) -> p j t", t=PACK),
+        def values_both(b, jc, bank):
+            values(b, jc, 0, bank)
+            values(b, jc, 1)
+
+        h_bf = {}
+        h_codes = {}
+        h_planes = {}
+        h_place = {}
+
+        def h_group(name, members, room=None, codes_room=None):
+            h_bf[name] = held([P, len(members) * PASS], BF16, "h_bf" + name, room)
+            h_codes[name] = held([P, len(members) * CHUNK], U32, "h_codes" + name, codes_room)
+            h_planes[name] = held([P, len(members) * CHUNK], U8, "h_plane" + name)
+            for w, member in enumerate(members):
+                h_place[member] = (name, w)
+
+        def hidden(b, jc):
+            name, w = h_place[b, jc]
+            nc.vector.tensor_tensor(out=h_bf[name][:, w * PASS:(w + 1) * PASS].rearrange("p (j t) -> p j t", t=PACK),
                                     in0=val_banks[b, jc][:].rearrange("p t j -> p j t"), in1=gates[b, jc], op=MULT)
 
-        def second_behind(name):
-            return raw_rooms[name][:, :2 * LEAD].bitcast(BF16)
-
-        def both_behind(name):
-            return raw_rooms[name][:, LEAD:3 * LEAD].bitcast(BF16)
-
-        def quantize_h(b, jp, w0=0, w1=2, tag=None):
-            if w0 == 0:
-                h_codes[b, jp] = held([P, PAIR], U32, "h_codes%d%d" % (b, jp), tag)
-                h_planes[b, jp] = held([P, PAIR], U8, "h_plane%d%d" % (b, jp))
-            cols = slice(w0 * CHUNK, w1 * CHUNK)
-            quantize(h_codes[b, jp][:, cols], h_planes[b, jp][:, cols], h_bf[b, jp][:, w0 * PASS:w1 * PASS])
-
-        wd_bf = {}
-        for c in range(3):
-            both = held([P, 2 * WD_COLS * PACK], BF16, "wd_bf%d" % c)
-            for b in range(2):
-                wd_bf[b, c] = both[:, b * WD_COLS * PACK:(b + 1) * WD_COLS * PACK]
-            wd_bf[c] = both[:]
-        wd_codes = [held([P, 2 * WD_COLS], U32, "wd_codes%d" % c) for c in range(3)]
-        wd_planes = [held([P, 2 * WD_COLS], U8, "wd_plane%d" % c) for c in range(3)]
-
-        def cast_wd(b, c, engine, n0=0, n1=WD_COLS):
-            copy_on(engine, wd_bf[b, c][:, n0 * PACK:n1 * PACK].rearrange("p (m e i) -> p m i e", e=4, i=PACK),
-                    wd_raw[b, c][:, :, n0:n1].rearrange("p i (m e) -> p m i e", e=4))
-
-        def quantize_wd(c):
-            quantize(wd_codes[c][:], wd_planes[c][:], wd_bf[c])
-
-        def quantize_wd_piece(b, c):
-            cols = slice(b * WD_COLS, (b + 1) * WD_COLS)
-            quantize(wd_codes[c][:, cols], wd_planes[c][:, cols], wd_bf[b, c])
+        def quantize_h(name):
+            quantize(h_codes[name][:], h_planes[name][:], h_bf[name][:])
 
         results = {}
 
-        def project(v0, nv, j0, width, engine, bank_index):
-            bank = psum.tile([P, nv, width], F32, name="bank%d" % bank_index)
-            step = min(width, PAIR)
-            passes = [(b, w, j) for b in range(2) for w in range(nv) for j in range(j0, j0 + width, step)]
-            for b, w, j in passes:
+        def result_room(jc, chunks, tag):
+            results[jc] = held([P, (N // P) * chunks * CHUNK], F32, "result%d" % jc, tag)[:].rearrange(
+                "p (v j) -> p v j", v=N // P)
+
+        def project(v0, nv, jc, chunks, bank_index, engine):
+            width = chunks * CHUNK
+            bank = bank_tile(bank_index, [P, nv, width])
+            passes = [(b, w) for b in range(2) for w in range(nv)]
+            for b, w in passes:
                 c, n0 = divmod((v0 + w) * P, WD_COLS)
                 n0 = n0 + b * WD_COLS
-                jp, c0 = divmod(j, PAIR)
-                nc.tensor.matmul_mx(out=bank[:, w, j - j0:j - j0 + step],
+                name, place = h_place[b, jc]
+                cols = slice(place * CHUNK, place * CHUNK + width)
+                nc.tensor.matmul_mx(out=bank[:, w, :],
                                     lhsT=wd_codes[c][:, n0:n0 + P].bitcast(FP8X4),
                                     lhsT_scale=wd_planes[c][:, n0:n0 + P],
-                                    rhs=h_codes[b, jp][:, c0:c0 + step].bitcast(FP8X4),
-                                    rhs_scale=h_planes[b, jp][:, c0:c0 + step],
-                                    start=(b, w, j) == passes[0], stop=(b, w, j) == passes[-1])
-            u, c0 = divmod(j0, HALF)
-            c, w0 = divmod(v0, 2)
-            if (c, u) not in results:
-                results[c, u] = held([P, 2, HALF], F32, "result%d%d" % (c, u), RESULT_ROOMS[3 * u + c])
-            copy_on(engine, results[c, u][:, w0:w0 + nv, c0:c0 + width], bank[:])
+                                    rhs=h_codes[name][:, cols].bitcast(FP8X4),
+                                    rhs_scale=h_planes[name][:, cols],
+                                    start=(b, w) == passes[0], stop=(b, w) == passes[-1])
+            copy_on(engine, results[jc][:, v0:v0 + nv, :], bank[:])
 
-        def store(v0, nv, j0, width):
-            u, c0 = divmod(j0, HALF)
-            c, w0 = divmod(v0, 2)
-            rows = out[v0 * P:(v0 + nv) * P, j0:j0 + width]
-            nc.sync.dma_start(out=rows.rearrange("(v p) j -> p v j", p=P), in_=results[c, u][:, w0:w0 + nv, c0:c0 + width])
+        def store(v0, nv, jc, chunks):
+            rows = out[v0 * P:(v0 + nv) * P, jc * CHUNK:(jc + chunks) * CHUNK]
+            nc.sync.dma_start(out=rows.rearrange("(v p) j -> p v j", p=P), in_=results[jc][:, v0:v0 + nv, :])
 
         nc.vector.memset(key_scale_tab[:].bitcast(I32), 0)
         nc.vector.memset(val_scale_tab[:].bitcast(I32), 0)
         nc.vector.memset(wk_scale_raw[:].bitcast(I32), 0)
-        nc.vector.memset(key_plane.bitcast(I32), 0)
+        nc.vector.memset(key_plane[:].bitcast(I32), 0)
         nc.vector.memset(val_plane[:].bitcast(I32), 0)
         nc.sync.dma_start(key_list[:], offs)
         nc.sync.dma_start(val_list[:], offs2)
         nc.sync.dma_start(out=wk_raw[:], in_=wk_words[0].bitcast(I32))
         load_rows(key_scale_tab, 8, tab_scales[0])
         load_rows(val_scale_tab, 4, tab2_scales.rearrange("a q t -> (a q) t"))
-        load_plane(wk_scale_raw, wk_scales)
+        load_wk_scales()
         load_words(key_tab, tab_words, 0)
         deal_wk_words()
         gather(key_rows, key_scale_tab, key_list, 0, S)
@@ -263,82 +247,93 @@ def tile_list_memory_kv_swiglu_kernel(tc, tab_words, tab_scales, tab2_words, tab
         load_words(val_tab[0], tab2_words, 0)
         gather(val_rows, val_scale_tab, val_list, 0, S)
         deal_wk_scales()
-        load_wv(0, 0)
-        place_val_rows(0, 0, 2)
-        load_wv(1, 0)
+        load_wv(0, 0, 0, P)
+        place_val_rows(0, 2)
+        load_wv(1, 0, 0, P)
         load_words(val_tab[1], tab2_words, 1)
-        place_val_rows(0, 2, 4)
-        place_val_rows(1, 0, 4)
-        load_wv(0, 1)
-        load_wv(1, 1)
+        place_val_rows(2, 8)
+        for a in range(2):
+            load_wv(a, 1, 0, P)
         for c in range(3):
             for b in range(2):
-                load_wd(b, c, c + 1)
-        for u in range(2):
-            gather(key_codes, key_tab, key_list, u * HALF, (u + 1) * HALF)
-        gather(val_codes[0], val_tab[0], val_list, 0, S)
-        for jc in range(8):
-            gate(0, jc)
-        cast_wv(0, 0, "vector")
-        for jc in range(8):
-            gate(1, jc, raw_rooms["wv_raw00"][:, LEAD + jc * PASS:LEAD + (jc + 1) * PASS] if jc < 4 else None)
-        quantize_wv(0, 0)
-        cast_wv(1, 0, "vector")
-        quantize_wv(1, 0)
-        for u in range(2):
-            gather(val_codes[1], val_tab[1], val_list, u * HALF, (u + 1) * HALF)
-        cast_wv(0, 1, "scalar")
-        cast_wv(1, 1, "scalar", 0, P // 2)
-        hidden(0, 0, 3)
-        hidden(0, 1, 4)
-        hidden(0, 2, 5)
-        quantize_h(0, 0)
-        hidden(0, 3, 3)
-        hidden(0, 4, 4)
-        hidden(0, 5, 5)
+                load_wd(b, c)
+
+        for j0, j1 in ((0, 256), (256, 512), (512, S)):
+            gather(key_codes, key_tab, key_list, j0, j1)
+        gather_values(0, 0, 8)
+        for b, jc in [divmod(e, 8) for e in range(8)]:
+            gate(b, jc)
+        for a in range(2):
+            cast_wv(a, 0, 0, 0, P, "vector")
+            quantize_wv(a, 0)
+        for e in range(8, 16):
+            w = e - 8
+            gate(1, e - 8, wv_raw[0, 0, 0][:, w * PASS:(w + 1) * PASS] if w < 4 else None)
+        gather_values(1, 0, 4)
+        gather_values(1, 4, 8)
+        cast_wv(0, 1, 0, 0, P, "scalar")
+        cast_wv(1, 1, 0, 0, 64, "scalar")
+        for b, c in ((0, 0), (1, 0), (0, 1), (1, 1)):
+            cast_wd(b, c, "scalar")
+
+        h_group("A0", [(0, jc) for jc in range(4)])
+        h_group("A1", [(1, jc) for jc in range(4)])
+        h_group("B0", [(0, 4), (0, 5)], None, "wv_raw01_0")
+        result_room(0, 4, "key_tab")
+        result_room(4, 2, "val_tab0")
+        result_room(6, 2, "val_tab1")
+
+        for jc in range(5):
+            values_both(0, jc, 3 + jc)
+            hidden(0, jc)
+        values_both(0, 5, 3)
+        quantize_h("A0")
+        hidden(0, 5)
+        values_both(0, 6, 6)
         quantize_wv(0, 1)
-        cast_wv(1, 1, "vector", P // 2, P)
-        quantize_h(0, 2, tag="wv_raw01")
+        cast_wv(1, 1, 0, 64, P, "vector")
+        quantize_h("B0")
         quantize_wv(1, 1)
-        hidden(0, 6, 3, both_behind("wv_raw11"))
-        values(0, 7, 4)
-        quantize_h(0, 1, tag="wv_bf11")
-        for c in range(2):
-            for b in range(2):
-                cast_wd(b, c, "scalar")
-        cast_wd(0, 2, "scalar")
-        hidden(1, 0, 6)
-        hidden(1, 1, 7)
-        hidden(1, 2, 0)
-        quantize_h(1, 0)
-        hidden(1, 3, 1)
-        quantize_wd(0)
-        quantize_h(1, 1)
-        quantize_wd(1)
+        h_group("C0", [(0, 6), (0, 7)], "wv_raw11_0")
+        hidden(0, 6)
+        quantize_wd(0, 0, 1)
+        for jc in range(4):
+            values_both(1, jc, jc)
+            hidden(1, jc)
+        values_both(1, 4, 4)
+        values_both(1, 5, 5)
+        quantize_wd(0, 1, 2)
+        quantize_h("A1")
+        h_group("B1", [(1, 4), (1, 5)])
+        quantize_wd(1, 0, 1)
+        hidden(1, 4)
+        quantize_wd(1, 1, 2)
         for v in range(4):
-            project(v, 1, 0, HALF, "scalar", (3, 0, 1, 3)[v])
-            store(v, 1, 0, HALF)
-        hidden(1, 4, 2)
-        hidden(1, 5, 5)
+            project(v, 1, 0, 4, v, "scalar")
+            store(v, 1, 0, 4)
+        values_both(0, 7, 4)
+        values_both(1, 6, 6)
+        values_both(1, 7, 7)
+        hidden(1, 5)
+        cast_wd(0, 2, "vector")
+        quantize_h("B1")
+        for c in range(2):
+            project(2 * c, 2, 4, 2, (5, 0)[c], "scalar")
+            store(2 * c, 2, 4, 2)
         cast_wd(1, 2, "vector")
-        quantize_h(1, 2)
-        quantize_wd(2)
-        for c in range(2):
-            project(2 * c, 2, 2 * PAIR, PAIR, "scalar", (2, 5)[c])
-            store(2 * c, 2, 2 * PAIR, PAIR)
+        h_group("C1", [(1, 6), (1, 7)], "wd_raw02")
+        quantize_wd(2, 0, 1)
+        quantize_wd(2, 1, 2)
         for v in (4, 5):
-            project(v, 1, 0, HALF, "scalar", (0, 1)[v - 4])
-            store(v, 1, 0, HALF)
-        for c in range(2, 3):
-            project(2 * c, 2, 2 * PAIR, PAIR, "scalar", (2, 5, 3)[c])
-        hidden(0, 7, 4)
-        hidden(1, 6, 6)
-        hidden(1, 7, 7)
-        quantize_h(0, 3)
-        quantize_h(1, 3)
-        for v in (4, 5):
-            project(v, 1, 3 * PAIR, PAIR, ("vector", "scalar")[v - 4], (4, 2)[v - 4])
-        store(4, 2, HALF, HALF)
-        for c in range(2):
-            project(2 * c, 2, 3 * PAIR, PAIR, ("vector", "scalar")[c], (6, 7)[c])
-            store(2 * c, 2, 3 * PAIR, PAIR)
+            project(v, 1, 0, 4, v - 3, "scalar")
+            store(v, 1, 0, 4)
+        project(4, 2, 4, 2, 3, "scalar")
+        store(4, 2, 4, 2)
+        hidden(0, 7)
+        hidden(1, 6)
+        quantize_h("C0")
+        hidden(1, 7)
+        quantize_h("C1")
+        for c in range(3):
+            project(2 * c, 2, 6, 2, (4, 5, 0)[c], ("vector", "scalar", "vector")[c])
+            store(2 * c, 2, 6, 2)

@@ -46,13 +46,14 @@ def tile_list_memory_kv_swiglu_kernel(tc, tab_words, tab_scales, tab2_words, tab
         key_tab = held([P, T], U32, "key_tab")
         val_tab = [held([P, T2], U32, "val_tab%d" % a) for a in range(2)]
         key_codes = held([P, S], U32, "key_codes")
-        key_plane = held([P, S], U8, "key_plane")
         val_codes = {}
-        val_plane = held([P, S], U8, "val_plane")
+        staged = [held([P, 2 * S], U8, "staged%d" % g) for g in range(2)]
+        planes = [held([P, 2 * S], U8, "planes%d" % g) for g in range(2)]
+        key_plane, wk_plane = planes[0][:, :S], planes[0][:, S:]
+        val_plane = [planes[1][:, a * S:(a + 1) * S] for a in range(2)]
         key_rows = held([P, S], U8, "key_rows")
         val_rows = held([P, S], U8, "val_rows")
         wk_codes = held([P, 2 * H], U8, "wk_codes")
-        wk_plane = held([P, H], U8, "wk_plane")
 
         def copy_on(engine, dst, src):
             if engine == "scalar":
@@ -67,21 +68,16 @@ def tile_list_memory_kv_swiglu_kernel(tc, tab_words, tab_scales, tab2_words, tab
             words = table[a].rearrange("p t i -> p (t i)").bitcast(I32)
             nc.sync.dma_start(out=tile[:].bitcast(I32), in_=words)
 
-        def load_rows(tile, step, rows):
-            nc.sync.dma_start(out=tile[0:P:step, :].bitcast(I32), in_=rows.bitcast(I32))
+        def load_rows(tile, p0, p1, rows):
+            nc.sync.dma_start(out=tile[p0:p1:4, :].bitcast(I32), in_=rows.bitcast(I32))
 
-        def load_wk_scales():
+        def stage_rows(g, place, rows, p0):
+            nc.vector.tensor_copy(out=staged[g][:P // 2, place * S:(place + 1) * S].bitcast(I32),
+                                  in_=rows[p0:p0 + P // 2, :].bitcast(I32))
+
+        def place_planes(g):
             for r in range(4):
-                nc.sync.dma_start(out=wk_scale_raw[r:P:32, :].bitcast(I32), in_=wk_scales[0, r:16:4, :].bitcast(I32))
-
-        def place_key_rows():
-            for r in range(4):
-                nc.sync.dma_start(out=key_plane[r:P:32, :].bitcast(I32), in_=key_rows[8 * r:P:32, :].bitcast(I32))
-
-        def place_val_rows(first, last):
-            for a, r in [divmod(e, 4) for e in range(first, last)]:
-                nc.sync.dma_start(out=val_plane[4 * a + r:P:32, :].bitcast(I32),
-                                  in_=val_rows[64 * a + 4 * r:64 * (a + 1):16, :].bitcast(I32))
+                nc.sync.dma_start(out=planes[g][r:P:32, :].bitcast(I32), in_=staged[g][4 * r:P // 2:16, :].bitcast(I32))
 
         def gather(picked, window, lst, j0, j1):
             nc.vector.tensor_copy(out=picked[:, j0:j1], in_=window[:].indirect(lst[:, j0 // 16:j1 // 16]))
@@ -93,13 +89,13 @@ def tile_list_memory_kv_swiglu_kernel(tc, tab_words, tab_scales, tab2_words, tab
                 val_codes[a, jc] = picked[:, (jc - jc0) * CHUNK:(jc - jc0 + 1) * CHUNK]
 
         def deal_wk_words():
-            nc.vector.tensor_copy(
+            nc.scalar.copy(
                 out=wk_codes[:].bitcast(U16).rearrange("p (b t m) -> p b t m", b=2, t=PACK),
                 in_=wk_raw[:].bitcast(U16).rearrange("p (b m t) -> p b t m", b=2, t=PACK))
 
         def deal_wk_scales():
             nc.vector.tensor_copy(
-                out=wk_plane[:].rearrange("p (b t m) -> p b t m", b=2, t=PACK),
+                out=staged[0][:, S:].rearrange("p (b t m) -> p b t m", b=2, t=PACK),
                 in_=wk_scale_raw[:].rearrange("p (b m t) -> p b t m", b=2, t=PACK))
 
         wv_raw = {}
@@ -137,10 +133,10 @@ def tile_list_memory_kv_swiglu_kernel(tc, tab_words, tab_scales, tab2_words, tab
             nc.sync.dma_start(out=wd_raw[b, c][:].rearrange("p (i n) -> p i n", i=PACK),
                               in_=rows.rearrange("(p i) n -> p i n", i=PACK))
 
-        def cast_wd(b, c, engine):
-            words = WD_COLS * PACK
-            copy_on(engine, wd_bf[c][:, b * words:(b + 1) * words].rearrange("p (m e i) -> p m i e", e=4, i=PACK),
-                    wd_raw[b, c][:].rearrange("p (i m e) -> p m i e", i=PACK, e=4))
+        def cast_wd(b, c, engine, n0=0, n1=WD_COLS):
+            at = b * WD_COLS
+            copy_on(engine, wd_bf[c][:, (at + n0) * PACK:(at + n1) * PACK].rearrange("p (m e i) -> p m i e", e=4, i=PACK),
+                    wd_raw[b, c][:].rearrange("p (i n) -> p i n", i=PACK)[:, :, n0:n1].rearrange("p i (m e) -> p m i e", e=4))
 
         def quantize_wd(c, b0=0, b1=2):
             cols = slice(b0 * WD_COLS, b1 * WD_COLS)
@@ -175,7 +171,7 @@ def tile_list_memory_kv_swiglu_kernel(tc, tab_words, tab_scales, tab2_words, tab
                                     lhsT=wv_codes[a, b][:, t * P:(t + 1) * P].bitcast(FP8X4),
                                     lhsT_scale=wv_planes[a, b][:, t * P:(t + 1) * P],
                                     rhs=val_codes[a, jc].bitcast(FP8X4),
-                                    rhs_scale=val_plane[4 * a:, c0:c0 + CHUNK],
+                                    rhs_scale=val_plane[a][:, c0:c0 + CHUNK],
                                     start=(a == 0 and t == 0), stop=(a == 1 and t == PACK - 1))
 
         def values_both(b, jc, bank):
@@ -185,28 +181,32 @@ def tile_list_memory_kv_swiglu_kernel(tc, tab_words, tab_scales, tab2_words, tab
         h_bf = {}
         h_codes = {}
         h_planes = {}
-        h_place = {}
 
-        def h_group(name, members, room=None, codes_room=None):
-            h_bf[name] = held([P, len(members) * PASS], BF16, "h_bf" + name, room)
-            h_codes[name] = held([P, len(members) * CHUNK], U32, "h_codes" + name, codes_room)
-            h_planes[name] = held([P, len(members) * CHUNK], U8, "h_plane" + name)
-            for w, member in enumerate(members):
-                h_place[member] = (name, w)
+        def h_room(b, jc0, jc1, room=None):
+            tile = held([P, (jc1 - jc0) * PASS], BF16, "h_bf%d%d" % (b, jc0), room)
+            for jc in range(jc0, jc1):
+                h_bf[b, jc] = (tile, (jc - jc0) * PASS)
 
         def hidden(b, jc):
-            name, w = h_place[b, jc]
-            nc.vector.tensor_tensor(out=h_bf[name][:, w * PASS:(w + 1) * PASS].rearrange("p (j t) -> p j t", t=PACK),
+            tile, at = h_bf[b, jc]
+            nc.vector.tensor_tensor(out=tile[:, at:at + PASS].rearrange("p (j t) -> p j t", t=PACK),
                                     in0=val_banks[b, jc][:].rearrange("p t j -> p j t"), in1=gates[b, jc], op=MULT)
 
-        def quantize_h(name):
-            quantize(h_codes[name][:], h_planes[name][:], h_bf[name][:])
+        def quantize_h(b, jc0, jc1, room=None, group=None):
+            first, last = group or (jc0, jc1)
+            if (b, first) not in h_codes:
+                h_codes[b, first] = held([P, (last - first) * CHUNK], U32, "h_codes%d%d" % (b, first), room)
+                h_planes[b, first] = held([P, (last - first) * CHUNK], U8, "h_plane%d%d" % (b, first))
+            tile, at = h_bf[b, jc0]
+            cols = slice((jc0 - first) * CHUNK, (jc1 - first) * CHUNK)
+            quantize(h_codes[b, first][:, cols], h_planes[b, first][:, cols], tile[:, at:at + (jc1 - jc0) * PASS])
 
         results = {}
 
-        def result_room(jc, chunks, tag):
-            results[jc] = held([P, (N // P) * chunks * CHUNK], F32, "result%d" % jc, tag)[:].rearrange(
-                "p (v j) -> p v j", v=N // P)
+        def result_room(jc0, chunks, tag):
+            room = held([P, (N // P) * chunks * CHUNK], F32, "result%d" % jc0, tag)[:].rearrange("p (v j) -> p v j", v=N // P)
+            for jc in range(jc0, jc0 + chunks):
+                results[jc] = room[:, :, (jc - jc0) * CHUNK:]
 
         def project(v0, nv, jc, chunks, bank_index, engine):
             width = chunks * CHUNK
@@ -215,125 +215,123 @@ def tile_list_memory_kv_swiglu_kernel(tc, tab_words, tab_scales, tab2_words, tab
             for b, w in passes:
                 c, n0 = divmod((v0 + w) * P, WD_COLS)
                 n0 = n0 + b * WD_COLS
-                name, place = h_place[b, jc]
-                cols = slice(place * CHUNK, place * CHUNK + width)
                 nc.tensor.matmul_mx(out=bank[:, w, :],
                                     lhsT=wd_codes[c][:, n0:n0 + P].bitcast(FP8X4),
                                     lhsT_scale=wd_planes[c][:, n0:n0 + P],
-                                    rhs=h_codes[name][:, cols].bitcast(FP8X4),
-                                    rhs_scale=h_planes[name][:, cols],
+                                    rhs=h_codes[b, jc][:].bitcast(FP8X4),
+                                    rhs_scale=h_planes[b, jc][:],
                                     start=(b, w) == passes[0], stop=(b, w) == passes[-1])
-            copy_on(engine, results[jc][:, v0:v0 + nv, :], bank[:])
+            copy_on(engine, results[jc][:, v0:v0 + nv, :width], bank[:])
 
         def store(v0, nv, jc, chunks):
             rows = out[v0 * P:(v0 + nv) * P, jc * CHUNK:(jc + chunks) * CHUNK]
-            nc.sync.dma_start(out=rows.rearrange("(v p) j -> p v j", p=P), in_=results[jc][:, v0:v0 + nv, :])
+            nc.sync.dma_start(out=rows.rearrange("(v p) j -> p v j", p=P), in_=results[jc][:, v0:v0 + nv, :chunks * CHUNK])
 
         nc.vector.memset(key_scale_tab[:].bitcast(I32), 0)
         nc.vector.memset(val_scale_tab[:].bitcast(I32), 0)
         nc.vector.memset(wk_scale_raw[:].bitcast(I32), 0)
-        nc.vector.memset(key_plane[:].bitcast(I32), 0)
-        nc.vector.memset(val_plane[:].bitcast(I32), 0)
+        for g in range(2):
+            nc.vector.memset(planes[g][:].bitcast(I32), 0)
         nc.sync.dma_start(key_list[:], offs)
         nc.sync.dma_start(val_list[:], offs2)
         nc.sync.dma_start(out=wk_raw[:], in_=wk_words[0].bitcast(I32))
-        load_rows(key_scale_tab, 8, tab_scales[0])
-        load_rows(val_scale_tab, 4, tab2_scales.rearrange("a q t -> (a q) t"))
-        load_wk_scales()
+        load_rows(key_scale_tab, P // 2, P, tab_scales[0])
+        load_rows(wk_scale_raw, 0, P // 2, wk_scales[0])
+        load_rows(val_scale_tab, 0, P, tab2_scales.rearrange("a q t -> (a q) t"))
         load_words(key_tab, tab_words, 0)
         deal_wk_words()
         gather(key_rows, key_scale_tab, key_list, 0, S)
-        place_key_rows()
-        load_words(val_tab[0], tab2_words, 0)
-        gather(val_rows, val_scale_tab, val_list, 0, S)
         deal_wk_scales()
-        load_wv(0, 0, 0, P)
-        place_val_rows(0, 2)
-        load_wv(1, 0, 0, P)
+        stage_rows(0, 0, key_rows, P // 2)
+        load_words(val_tab[0], tab2_words, 0)
+        place_planes(0)
+        gather(val_rows, val_scale_tab, val_list, 0, S)
+        for a in range(2):
+            load_wv(a, 0, 0, P)
         load_words(val_tab[1], tab2_words, 1)
-        place_val_rows(2, 8)
+        for u in range(2):
+            gather(key_codes, key_tab, key_list, u * S // 2, (u + 1) * S // 2)
+        for a in range(2):
+            stage_rows(1, a, val_rows, a * P // 2)
+        place_planes(1)
         for a in range(2):
             load_wv(a, 1, 0, P)
         for c in range(3):
             for b in range(2):
                 load_wd(b, c)
 
-        for j0, j1 in ((0, 256), (256, 512), (512, S)):
-            gather(key_codes, key_tab, key_list, j0, j1)
         gather_values(0, 0, 8)
         for b, jc in [divmod(e, 8) for e in range(8)]:
             gate(b, jc)
         for a in range(2):
             cast_wv(a, 0, 0, 0, P, "vector")
             quantize_wv(a, 0)
-        for e in range(8, 16):
-            w = e - 8
-            gate(1, e - 8, wv_raw[0, 0, 0][:, w * PASS:(w + 1) * PASS] if w < 4 else None)
+        for jc in range(8):
+            gate(1, jc, wv_raw[0, 0, 0][:, jc * PASS:(jc + 1) * PASS] if jc < PACK else None)
         gather_values(1, 0, 4)
         gather_values(1, 4, 8)
         cast_wv(0, 1, 0, 0, P, "scalar")
-        cast_wv(1, 1, 0, 0, 64, "scalar")
-        for b, c in ((0, 0), (1, 0), (0, 1), (1, 1)):
+        cast_wv(1, 1, 0, 0, P // 2, "scalar")
+        for b, c in ((0, 0), (1, 0), (0, 1), (1, 1), (0, 2)):
             cast_wd(b, c, "scalar")
 
-        h_group("A0", [(0, jc) for jc in range(4)])
-        h_group("A1", [(1, jc) for jc in range(4)])
-        h_group("B0", [(0, 4), (0, 5)], None, "wv_raw01_0")
+        h_room(0, 0, 4)
+        h_room(0, 4, 6)
+        h_room(1, 0, 4)
         result_room(0, 4, "key_tab")
-        result_room(4, 2, "val_tab0")
-        result_room(6, 2, "val_tab1")
+        result_room(4, 4, "val_tab0")
 
-        for jc in range(5):
-            values_both(0, jc, 3 + jc)
+        for jc in range(6):
+            values_both(0, jc, 3 + jc % 3)
             hidden(0, jc)
-        values_both(0, 5, 3)
-        quantize_h("A0")
-        hidden(0, 5)
-        values_both(0, 6, 6)
+        values_both(0, 6, 3)
+        values_both(0, 7, 4)
         quantize_wv(0, 1)
-        cast_wv(1, 1, 0, 64, P, "vector")
-        quantize_h("B0")
+        cast_wv(1, 1, 0, P // 2, P, "vector")
+        quantize_h(0, 0, 4, "wv_raw01_0")
         quantize_wv(1, 1)
-        h_group("C0", [(0, 6), (0, 7)], "wv_raw11_0")
+        h_room(0, 6, 7, "wv_raw11_0")
         hidden(0, 6)
         quantize_wd(0, 0, 1)
         for jc in range(4):
-            values_both(1, jc, jc)
+            values_both(1, jc, (6, 7, 0, 1)[jc])
             hidden(1, jc)
-        values_both(1, 4, 4)
+        values_both(1, 4, 2)
         values_both(1, 5, 5)
         quantize_wd(0, 1, 2)
-        quantize_h("A1")
-        h_group("B1", [(1, 4), (1, 5)])
-        quantize_wd(1, 0, 1)
-        hidden(1, 4)
-        quantize_wd(1, 1, 2)
+        quantize_h(1, 0, 4)
+        quantize_wd(1)
         for v in range(4):
-            project(v, 1, 0, 4, v, "scalar")
+            project(v, 1, 0, 4, (3, 0, 1, 3)[v], "scalar")
             store(v, 1, 0, 4)
-        values_both(0, 7, 4)
         values_both(1, 6, 6)
         values_both(1, 7, 7)
+        h_room(1, 4, 6, "wd_raw11")
+        hidden(1, 4)
         hidden(1, 5)
-        cast_wd(0, 2, "vector")
-        quantize_h("B1")
+        quantize_h(0, 4, 6, "wd_bf1")
+        quantize_h(1, 4, 6)
         for c in range(2):
-            project(2 * c, 2, 4, 2, (5, 0)[c], "scalar")
+            project(2 * c, 2, 4, 2, (2, 5)[c], "scalar")
             store(2 * c, 2, 4, 2)
         cast_wd(1, 2, "vector")
-        h_group("C1", [(1, 6), (1, 7)], "wd_raw02")
+        h_room(0, 7, 8, "wd_raw02")
+        h_room(1, 6, 8, "wd_raw12")
         quantize_wd(2, 0, 1)
         quantize_wd(2, 1, 2)
         for v in (4, 5):
-            project(v, 1, 0, 4, v - 3, "scalar")
+            project(v, 1, 0, 4, v - 4, "scalar")
             store(v, 1, 0, 4)
         project(4, 2, 4, 2, 3, "scalar")
-        store(4, 2, 4, 2)
         hidden(0, 7)
         hidden(1, 6)
-        quantize_h("C0")
         hidden(1, 7)
-        quantize_h("C1")
-        for c in range(3):
-            project(2 * c, 2, 6, 2, (4, 5, 0)[c], ("vector", "scalar", "vector")[c])
+        quantize_h(0, 6, 7, "wd_bf2", (6, 8))
+        quantize_h(0, 7, 8, None, (6, 8))
+        quantize_h(1, 6, 8)
+        for v in (4, 5):
+            project(v, 1, 6, 2, (4, 2)[v - 4], ("vector", "scalar")[v - 4])
+        store(4, 2, 4, 4)
+        for c in range(2):
+            project(2 * c, 2, 6, 2, (6, 7)[c], ("vector", "scalar")[c])
             store(2 * c, 2, 6, 2)

@@ -46,14 +46,13 @@ def tile_list_memory_kv_swiglu_kernel(tc, tab_words, tab_scales, tab2_words, tab
         key_tab = held([P, T], U32, "key_tab")
         val_tab = [held([P, T2], U32, "val_tab%d" % a) for a in range(2)]
         key_codes = held([P, S], U32, "key_codes")
+        key_plane = held([P, S], U8, "key_plane")
         val_codes = {}
-        staged = [held([P, 2 * S], U8, "staged%d" % g) for g in range(2)]
-        planes = [held([P, 2 * S], U8, "planes%d" % g) for g in range(2)]
-        key_plane, wk_plane = planes[0][:, :S], planes[0][:, S:]
-        val_plane = [planes[1][:, a * S:(a + 1) * S] for a in range(2)]
+        val_plane = held([P, S], U8, "val_plane")
         key_rows = held([P, S], U8, "key_rows")
         val_rows = held([P, S], U8, "val_rows")
         wk_codes = held([P, 2 * H], U8, "wk_codes")
+        wk_plane = held([P, H], U8, "wk_plane")
 
         def copy_on(engine, dst, src):
             if engine == "scalar":
@@ -68,16 +67,21 @@ def tile_list_memory_kv_swiglu_kernel(tc, tab_words, tab_scales, tab2_words, tab
             words = table[a].rearrange("p t i -> p (t i)").bitcast(I32)
             nc.sync.dma_start(out=tile[:].bitcast(I32), in_=words)
 
-        def load_rows(tile, p0, p1, rows):
-            nc.sync.dma_start(out=tile[p0:p1:4, :].bitcast(I32), in_=rows.bitcast(I32))
+        def load_rows(tile, step, rows):
+            nc.sync.dma_start(out=tile[0:P:step, :].bitcast(I32), in_=rows.bitcast(I32))
 
-        def stage_rows(g, place, rows, p0):
-            nc.vector.tensor_copy(out=staged[g][:P // 2, place * S:(place + 1) * S].bitcast(I32),
-                                  in_=rows[p0:p0 + P // 2, :].bitcast(I32))
-
-        def place_planes(g):
+        def load_wk_scales():
             for r in range(4):
-                nc.sync.dma_start(out=planes[g][r:P:32, :].bitcast(I32), in_=staged[g][4 * r:P // 2:16, :].bitcast(I32))
+                nc.sync.dma_start(out=wk_scale_raw[r:P:32, :].bitcast(I32), in_=wk_scales[0, r:16:4, :].bitcast(I32))
+
+        def place_key_rows():
+            for r in range(4):
+                nc.sync.dma_start(out=key_plane[r:P:32, :].bitcast(I32), in_=key_rows[8 * r:P:32, :].bitcast(I32))
+
+        def place_val_rows(first, last):
+            for a, r in [divmod(e, 4) for e in range(first, last)]:
+                nc.sync.dma_start(out=val_plane[4 * a + r:P:32, :].bitcast(I32),
+                                  in_=val_rows[64 * a + 4 * r:64 * (a + 1):16, :].bitcast(I32))
 
         def gather(picked, window, lst, j0, j1):
             nc.vector.tensor_copy(out=picked[:, j0:j1], in_=window[:].indirect(lst[:, j0 // 16:j1 // 16]))
@@ -89,13 +93,13 @@ def tile_list_memory_kv_swiglu_kernel(tc, tab_words, tab_scales, tab2_words, tab
                 val_codes[a, jc] = picked[:, (jc - jc0) * CHUNK:(jc - jc0 + 1) * CHUNK]
 
         def deal_wk_words():
-            nc.scalar.copy(
+            nc.vector.tensor_copy(
                 out=wk_codes[:].bitcast(U16).rearrange("p (b t m) -> p b t m", b=2, t=PACK),
                 in_=wk_raw[:].bitcast(U16).rearrange("p (b m t) -> p b t m", b=2, t=PACK))
 
         def deal_wk_scales():
             nc.vector.tensor_copy(
-                out=staged[0][:, S:].rearrange("p (b t m) -> p b t m", b=2, t=PACK),
+                out=wk_plane[:].rearrange("p (b t m) -> p b t m", b=2, t=PACK),
                 in_=wk_scale_raw[:].rearrange("p (b m t) -> p b t m", b=2, t=PACK))
 
         wv_raw = {}
@@ -171,7 +175,7 @@ def tile_list_memory_kv_swiglu_kernel(tc, tab_words, tab_scales, tab2_words, tab
                                     lhsT=wv_codes[a, b][:, t * P:(t + 1) * P].bitcast(FP8X4),
                                     lhsT_scale=wv_planes[a, b][:, t * P:(t + 1) * P],
                                     rhs=val_codes[a, jc].bitcast(FP8X4),
-                                    rhs_scale=val_plane[a][:, c0:c0 + CHUNK],
+                                    rhs_scale=val_plane[4 * a:, c0:c0 + CHUNK],
                                     start=(a == 0 and t == 0), stop=(a == 1 and t == PACK - 1))
 
         def values_both(b, jc, bank):
@@ -211,16 +215,18 @@ def tile_list_memory_kv_swiglu_kernel(tc, tab_words, tab_scales, tab2_words, tab
         def project(v0, nv, jc, chunks, bank_index, engine):
             width = chunks * CHUNK
             bank = bank_tile(bank_index, [P, nv, width])
-            passes = [(b, w) for b in range(2) for w in range(nv)]
-            for b, w in passes:
+            passes = [(b, w, first) for b in range(2) for w in range(nv) for first in range(jc, jc + chunks)
+                      if (b, first) in h_codes]
+            for b, w, first in passes:
                 c, n0 = divmod((v0 + w) * P, WD_COLS)
                 n0 = n0 + b * WD_COLS
-                nc.tensor.matmul_mx(out=bank[:, w, :],
+                j0 = (first - jc) * CHUNK
+                nc.tensor.matmul_mx(out=bank[:, w, j0:j0 + h_codes[b, first].shape[1]],
                                     lhsT=wd_codes[c][:, n0:n0 + P].bitcast(FP8X4),
                                     lhsT_scale=wd_planes[c][:, n0:n0 + P],
-                                    rhs=h_codes[b, jc][:].bitcast(FP8X4),
-                                    rhs_scale=h_planes[b, jc][:],
-                                    start=(b, w) == passes[0], stop=(b, w) == passes[-1])
+                                    rhs=h_codes[b, first][:].bitcast(FP8X4),
+                                    rhs_scale=h_planes[b, first][:],
+                                    start=(b, w, first) == passes[0], stop=(b, w, first) == passes[-1])
             copy_on(engine, results[jc][:, v0:v0 + nv, :width], bank[:])
 
         def store(v0, nv, jc, chunks):
@@ -230,44 +236,43 @@ def tile_list_memory_kv_swiglu_kernel(tc, tab_words, tab_scales, tab2_words, tab
         nc.vector.memset(key_scale_tab[:].bitcast(I32), 0)
         nc.vector.memset(val_scale_tab[:].bitcast(I32), 0)
         nc.vector.memset(wk_scale_raw[:].bitcast(I32), 0)
-        for g in range(2):
-            nc.vector.memset(planes[g][:].bitcast(I32), 0)
+        nc.vector.memset(key_plane[:].bitcast(I32), 0)
+        nc.vector.memset(val_plane[:].bitcast(I32), 0)
         nc.sync.dma_start(key_list[:], offs)
         nc.sync.dma_start(val_list[:], offs2)
         nc.sync.dma_start(out=wk_raw[:], in_=wk_words[0].bitcast(I32))
-        load_rows(key_scale_tab, P // 2, P, tab_scales[0])
-        load_rows(wk_scale_raw, 0, P // 2, wk_scales[0])
-        load_rows(val_scale_tab, 0, P, tab2_scales.rearrange("a q t -> (a q) t"))
+        load_rows(key_scale_tab, 8, tab_scales[0])
+        load_rows(val_scale_tab, 4, tab2_scales.rearrange("a q t -> (a q) t"))
+        load_wk_scales()
         load_words(key_tab, tab_words, 0)
         deal_wk_words()
         gather(key_rows, key_scale_tab, key_list, 0, S)
-        deal_wk_scales()
-        stage_rows(0, 0, key_rows, P // 2)
+        place_key_rows()
         load_words(val_tab[0], tab2_words, 0)
-        place_planes(0)
         gather(val_rows, val_scale_tab, val_list, 0, S)
-        for a in range(2):
-            load_wv(a, 0, 0, P)
+        deal_wk_scales()
+        load_wv(0, 0, 0, P)
+        place_val_rows(0, 2)
+        load_wv(1, 0, 0, P)
         load_words(val_tab[1], tab2_words, 1)
-        for u in range(2):
-            gather(key_codes, key_tab, key_list, u * S // 2, (u + 1) * S // 2)
-        for a in range(2):
-            stage_rows(1, a, val_rows, a * P // 2)
-        place_planes(1)
+        place_val_rows(2, 8)
         for a in range(2):
             load_wv(a, 1, 0, P)
         for c in range(3):
             for b in range(2):
                 load_wd(b, c)
 
+        for u in range(2):
+            gather(key_codes, key_tab, key_list, u * S // 2, (u + 1) * S // 2)
         gather_values(0, 0, 8)
         for b, jc in [divmod(e, 8) for e in range(8)]:
             gate(b, jc)
         for a in range(2):
             cast_wv(a, 0, 0, 0, P, "vector")
             quantize_wv(a, 0)
-        for jc in range(8):
-            gate(1, jc, wv_raw[0, 0, 0][:, jc * PASS:(jc + 1) * PASS] if jc < PACK else None)
+        for e in range(8, 16):
+            w = e - 8
+            gate(1, e - 8, wv_raw[0, 0, 0][:, w * PASS:(w + 1) * PASS] if w < 4 else None)
         gather_values(1, 0, 4)
         gather_values(1, 4, 8)
         cast_wv(0, 1, 0, 0, P, "scalar")
@@ -275,8 +280,8 @@ def tile_list_memory_kv_swiglu_kernel(tc, tab_words, tab_scales, tab2_words, tab
         for b, c in ((0, 0), (1, 0), (0, 1), (1, 1), (0, 2)):
             cast_wd(b, c, "scalar")
 
-        h_room(0, 0, 4)
-        h_room(0, 4, 6)
+        for jc in (0, 2, 4):
+            h_room(0, jc, jc + 2)
         h_room(1, 0, 4)
         result_room(0, 4, "key_tab")
         result_room(4, 4, "val_tab0")
@@ -284,11 +289,13 @@ def tile_list_memory_kv_swiglu_kernel(tc, tab_words, tab_scales, tab2_words, tab
         for jc in range(6):
             values_both(0, jc, 3 + jc % 3)
             hidden(0, jc)
+            if jc == 2:
+                quantize_h(0, 0, 2)
         values_both(0, 6, 3)
         values_both(0, 7, 4)
         quantize_wv(0, 1)
         cast_wv(1, 1, 0, P // 2, P, "vector")
-        quantize_h(0, 0, 4, "wv_raw01_0")
+        quantize_h(0, 2, 4, "wv_raw01_0")
         quantize_wv(1, 1)
         h_room(0, 6, 7, "wv_raw11_0")
         hidden(0, 6)

@@ -93,7 +93,7 @@ def tile_list_memory_kv_swiglu_kernel(tc, tab_words, tab_scales, tab2_words, tab
                 val_codes[a, jc] = picked[:, (jc - jc0) * CHUNK:(jc - jc0 + 1) * CHUNK]
 
         def deal_wk_words():
-            nc.vector.tensor_copy(
+            nc.scalar.copy(
                 out=wk_codes[:].bitcast(U16).rearrange("p (b t m) -> p b t m", b=2, t=PACK),
                 in_=wk_raw[:].bitcast(U16).rearrange("p (b m t) -> p b t m", b=2, t=PACK))
 
@@ -262,8 +262,8 @@ def tile_list_memory_kv_swiglu_kernel(tc, tab_words, tab_scales, tab2_words, tab
             for b in range(2):
                 load_wd(b, c)
 
-        for u in range(2):
-            gather(key_codes, key_tab, key_list, u * S // 2, (u + 1) * S // 2)
+        for j0, j1 in ((0, 256), (256, 512), (512, S)):
+            gather(key_codes, key_tab, key_list, j0, j1)
         gather_values(0, 0, 8)
         for b, jc in [divmod(e, 8) for e in range(8)]:
             gate(b, jc)

@@ -63,15 +63,15 @@ def tile_list_memory_kv_swiglu_kernel(tc, tab_words, tab_scales, tab2_words, tab
         def quantize(codes, plane, src):
             nc.vector.quantize_mx(out=codes.bitcast(FP8X4), scales=plane, in_=src)
 
-        def load_words(tile, table, a):
+        def load_words(tile, table, a, t0, t1):
             words = table[a].rearrange("p t i -> p (t i)").bitcast(I32)
-            nc.sync.dma_start(out=tile[:].bitcast(I32), in_=words)
+            nc.sync.dma_start(out=tile[:, t0:t1].bitcast(I32), in_=words[:, t0:t1])
 
         def load_rows(tile, step, rows):
             nc.sync.dma_start(out=tile[0:P:step, :].bitcast(I32), in_=rows.bitcast(I32))
 
-        def load_wk_scales():
-            for r in range(4):
+        def load_wk_scales(first, last):
+            for r in range(first, last):
                 nc.sync.dma_start(out=wk_scale_raw[r:P:32, :].bitcast(I32), in_=wk_scales[0, r:16:4, :].bitcast(I32))
 
         def place_key_rows():
@@ -243,18 +243,19 @@ def tile_list_memory_kv_swiglu_kernel(tc, tab_words, tab_scales, tab2_words, tab
         nc.sync.dma_start(out=wk_raw[:], in_=wk_words[0].bitcast(I32))
         load_rows(key_scale_tab, 8, tab_scales[0])
         load_rows(val_scale_tab, 4, tab2_scales.rearrange("a q t -> (a q) t"))
-        load_wk_scales()
-        load_words(key_tab, tab_words, 0)
+        for half in range(2):
+            load_wk_scales(2 * half, 2 * half + 2)
+            load_words(key_tab, tab_words, 0, half * T // 2, (half + 1) * T // 2)
         deal_wk_words()
         gather(key_rows, key_scale_tab, key_list, 0, S)
         place_key_rows()
-        load_words(val_tab[0], tab2_words, 0)
+        load_words(val_tab[0], tab2_words, 0, 0, T2)
         gather(val_rows, val_scale_tab, val_list, 0, S)
         deal_wk_scales()
         load_wv(0, 0, 0, P)
         place_val_rows(0, 2)
         load_wv(1, 0, 0, P)
-        load_words(val_tab[1], tab2_words, 1)
+        load_words(val_tab[1], tab2_words, 1, 0, T2)
         place_val_rows(2, 8)
         for a in range(2):
             load_wv(a, 1, 0, P)

@@ -207,10 +207,11 @@ def tile_list_memory_kv_swiglu_kernel(tc, tab_words, tab_scales, tab2_words, tab
 
         results = {}
 
-        def result_room(jc0, chunks, tag):
-            room = held([P, (N // P) * chunks * CHUNK], F32, "result%d" % jc0, tag)[:].rearrange("p (v j) -> p v j", v=N // P)
-            for jc in range(jc0, jc0 + chunks):
-                results[jc] = room[:, :, (jc - jc0) * CHUNK:]
+        def result_room(c, tag):
+            results[c] = held([P, 2 * S], F32, "result%d" % c, tag)[:].rearrange("p (w j) -> p w j", w=2)
+
+        def staged(v0, nv, jc, chunks):
+            return results[v0 // 2][:, v0 % 2:v0 % 2 + nv, jc * CHUNK:(jc + chunks) * CHUNK]
 
         def project(v0, nv, jc, chunks, bank_index, engine):
             width = chunks * CHUNK
@@ -227,11 +228,11 @@ def tile_list_memory_kv_swiglu_kernel(tc, tab_words, tab_scales, tab2_words, tab
                                     rhs=h_codes[b, first][:].bitcast(FP8X4),
                                     rhs_scale=h_planes[b, first][:],
                                     start=(b, w, first) == passes[0], stop=(b, w, first) == passes[-1])
-            copy_on(engine, results[jc][:, v0:v0 + nv, :width], bank[:])
+            copy_on(engine, staged(v0, nv, jc, chunks), bank[:])
 
         def store(v0, nv, jc, chunks):
             rows = out[v0 * P:(v0 + nv) * P, jc * CHUNK:(jc + chunks) * CHUNK]
-            nc.sync.dma_start(out=rows.rearrange("(v p) j -> p v j", p=P), in_=results[jc][:, v0:v0 + nv, :chunks * CHUNK])
+            nc.sync.dma_start(out=rows.rearrange("(v p) j -> p v j", p=P), in_=staged(v0, nv, jc, chunks))
 
         nc.vector.memset(key_scale_tab[:].bitcast(I32), 0)
         nc.vector.memset(val_scale_tab[:].bitcast(I32), 0)
@@ -253,8 +254,8 @@ def tile_list_memory_kv_swiglu_kernel(tc, tab_words, tab_scales, tab2_words, tab
         gather(val_rows, val_scale_tab, val_list, 0, S)
         deal_wk_scales()
         load_wv(0, 0, 0, P)
-        place_val_rows(0, 2)
         load_wv(1, 0, 0, P)
+        place_val_rows(0, 2)
         load_words(val_tab[1], tab2_words, 1, 0, T2)
         place_val_rows(2, 8)
         for a in range(2):
@@ -284,8 +285,8 @@ def tile_list_memory_kv_swiglu_kernel(tc, tab_words, tab_scales, tab2_words, tab
         for jc in (0, 2, 4):
             h_room(0, jc, jc + 2)
         h_room(1, 0, 4)
-        result_room(0, 4, "key_tab")
-        result_room(4, 4, "val_tab0")
+        for c, room in enumerate(("key_tab", "val_tab0", "val_tab1")):
+            result_room(c, room)
 
         for jc in range(6):
             values_both(0, jc, 3 + jc % 3)
@@ -327,10 +328,10 @@ def tile_list_memory_kv_swiglu_kernel(tc, tab_words, tab_scales, tab2_words, tab
         h_room(1, 6, 8, "wd_raw12")
         quantize_wd(2, 0, 1)
         quantize_wd(2, 1, 2)
+        project(4, 2, 4, 2, 3, "scalar")
         for v in (4, 5):
             project(v, 1, 0, 4, v - 4, "scalar")
-            store(v, 1, 0, 4)
-        project(4, 2, 4, 2, 3, "scalar")
+            store(v, 1, 0, 6)
         hidden(0, 7)
         hidden(1, 6)
         hidden(1, 7)
@@ -339,7 +340,7 @@ def tile_list_memory_kv_swiglu_kernel(tc, tab_words, tab_scales, tab2_words, tab
         quantize_h(1, 6, 8)
         for v in (4, 5):
             project(v, 1, 6, 2, (4, 2)[v - 4], ("vector", "scalar")[v - 4])
-        store(4, 2, 4, 4)
+        store(4, 2, 6, 2)
         for c in range(2):
             project(2 * c, 2, 6, 2, (6, 7)[c], ("vector", "scalar")[c])
             store(2 * c, 2, 6, 2)

@@ -32,7 +32,7 @@ def tile_list_memory_kv_swiglu_kernel(tc, tab_words, tab_scales, tab2_words, tab
         psum = ctx.enter_context(tc.psum_pool(name="psum", bufs=1))
 
         def held(shape, dtype, name, tag=None):
-            return keep.tile(shape, dtype, name=name, tag=tag or name, align_bytes=64)
+            return keep.tile(shape, dtype, name=name, tag=tag or name, align_bytes=256)
 
         def bank_tile(index, shape):
             return psum.tile(shape, F32, name="bank%d" % index)

@@ -67,8 +67,8 @@ def tile_list_memory_kv_swiglu_kernel(tc, tab_words, tab_scales, tab2_words, tab
             words = table[a].rearrange("p t i -> p (t i)").bitcast(I32)
             nc.sync.dma_start(out=tile[:, t0:t1].bitcast(I32), in_=words[:, t0:t1])
 
-        def load_rows(tile, step, rows):
-            nc.sync.dma_start(out=tile[0:P:step, :].bitcast(I32), in_=rows.bitcast(I32))
+        def load_rows(tile, first, last, rows):
+            nc.sync.dma_start(out=tile[first:last:4, :].bitcast(I32), in_=rows.bitcast(I32))
 
         def load_wk_scales(first, last):
             for r in range(first, last):
@@ -76,7 +76,7 @@ def tile_list_memory_kv_swiglu_kernel(tc, tab_words, tab_scales, tab2_words, tab
 
         def place_key_rows():
             for r in range(4):
-                nc.sync.dma_start(out=key_plane[r:P:32, :].bitcast(I32), in_=key_rows[8 * r:P:32, :].bitcast(I32))
+                nc.sync.dma_start(out=key_plane[r:P:32, :].bitcast(I32), in_=key_rows[32 + 4 * r:96:16, :].bitcast(I32))
 
         def place_val_rows(first, last):
             for a, r in [divmod(e, 4) for e in range(first, last)]:
@@ -242,8 +242,8 @@ def tile_list_memory_kv_swiglu_kernel(tc, tab_words, tab_scales, tab2_words, tab
         nc.sync.dma_start(key_list[:], offs)
         nc.sync.dma_start(val_list[:], offs2)
         nc.sync.dma_start(out=wk_raw[:], in_=wk_words[0].bitcast(I32))
-        load_rows(key_scale_tab, 8, tab_scales[0])
-        load_rows(val_scale_tab, 4, tab2_scales.rearrange("a q t -> (a q) t"))
+        load_rows(key_scale_tab, 32, 96, tab_scales[0])
+        load_rows(val_scale_tab, 0, P, tab2_scales.rearrange("a q t -> (a q) t"))
         for half in range(2):
             load_wk_scales(2 * half, 2 * half + 2)
             load_words(key_tab, tab_words, 0, half * T // 2, (half + 1) * T // 2)

@@ -79,8 +79,8 @@ def tile_list_memory_kv_swiglu_kernel(tc, tab_words, tab_scales, tab2_words, tab
                 nc.sync.dma_start(out=key_plane[r:P:32, :].bitcast(I32), in_=key_rows[32 + 4 * r:96:16, :].bitcast(I32))
 
         def place_val_rows(first, last):
-            for a, r in [divmod(e, 4) for e in range(first, last)]:
-                nc.sync.dma_start(out=val_plane[4 * a + r:P:32, :].bitcast(I32),
+            for r, a in [divmod(e, 2) for e in range(first, last)]:
+                nc.sync.dma_start(out=val_plane[4 * (a + 1) + r:P:32, :].bitcast(I32),
                                   in_=val_rows[64 * a + 4 * r:64 * (a + 1):16, :].bitcast(I32))
 
         def gather(picked, window, lst, j0, j1):
@@ -175,7 +175,7 @@ def tile_list_memory_kv_swiglu_kernel(tc, tab_words, tab_scales, tab2_words, tab
                                     lhsT=wv_codes[a, b][:, t * P:(t + 1) * P].bitcast(FP8X4),
                                     lhsT_scale=wv_planes[a, b][:, t * P:(t + 1) * P],
                                     rhs=val_codes[a, jc].bitcast(FP8X4),
-                                    rhs_scale=val_plane[4 * a:, c0:c0 + CHUNK],
+                                    rhs_scale=val_plane[4 * (a + 1):, c0:c0 + CHUNK],
                                     start=(a == 0 and t == 0), stop=(a == 1 and t == PACK - 1))
 
         def values_both(b, jc, bank):

@@ -278,7 +278,7 @@ def tile_list_memory_kv_swiglu_kernel(tc, tab_words, tab_scales, tab2_words, tab
         gather_values(1, 0, 4)
         gather_values(1, 4, 8)
         cast_wv(0, 1, 0, 0, P, "scalar")
-        cast_wv(1, 1, 0, 0, P // 2, "scalar")
+        cast_wv(1, 1, 0, 0, 72, "scalar")
         for b, c in ((0, 0), (1, 0), (0, 1), (1, 1), (0, 2)):
             cast_wd(b, c, "scalar")
 
@@ -295,8 +295,8 @@ def tile_list_memory_kv_swiglu_kernel(tc, tab_words, tab_scales, tab2_words, tab
                 quantize_h(0, 0, 2)
         values_both(0, 6, 3)
         values_both(0, 7, 4)
+        cast_wv(1, 1, 0, 72, P, "vector")
         quantize_wv(0, 1)
-        cast_wv(1, 1, 0, P // 2, P, "vector")
         quantize_h(0, 2, 4, "wv_raw01_0")
         quantize_wv(1, 1)
         h_room(0, 6, 7, "wv_raw11_0")
@@ -307,14 +307,14 @@ def tile_list_memory_kv_swiglu_kernel(tc, tab_words, tab_scales, tab2_words, tab
             hidden(1, jc)
         values_both(1, 4, 2)
         values_both(1, 5, 5)
+        values_both(1, 6, 6)
+        values_both(1, 7, 7)
         quantize_wd(0, 1, 2)
         quantize_h(1, 0, 4)
         quantize_wd(1)
         for v in range(4):
             project(v, 1, 0, 4, (3, 0, 1, 3)[v], "scalar")
             store(v, 1, 0, 4)
-        values_both(1, 6, 6)
-        values_both(1, 7, 7)
         h_room(1, 4, 6, "wd_raw11")
         hidden(1, 4)
         hidden(1, 5)

@@ -334,13 +334,14 @@ def tile_list_memory_kv_swiglu_kernel(tc, tab_words, tab_scales, tab2_words, tab
             store(v, 1, 0, 6)
         hidden(0, 7)
         hidden(1, 6)
-        hidden(1, 7)
         quantize_h(0, 6, 7, "wd_bf2", (6, 8))
         quantize_h(0, 7, 8, None, (6, 8))
-        quantize_h(1, 6, 8)
+        hidden(1, 7)
+        quantize_h(1, 6, 7, None, (6, 8))
+        quantize_h(1, 7, 8, None, (6, 8))
         for v in (4, 5):
             project(v, 1, 6, 2, (4, 2)[v - 4], ("vector", "scalar")[v - 4])
         store(4, 2, 6, 2)
         for c in range(2):
-            project(2 * c, 2, 6, 2, (6, 7)[c], ("vector", "scalar")[c])
+            project(2 * c, 2, 6, 2, (6, 5)[c], ("vector", "scalar")[c])
             store(2 * c, 2, 6, 2)

from contextlib import ExitStack

import concourse.mybir as mybir

K1, K2, H, N, T, T2, S = 512, 1024, 1024, 768, 4096, 2048, 1024
FLOPS = 2 * S * (K1 * H + K2 * H + H * N)

F32 = mybir.dt.float32
BF16 = mybir.dt.bfloat16
I32 = mybir.dt.int32
U32 = mybir.dt.uint32
U16 = mybir.dt.uint16
U8 = mybir.dt.uint8
FP8X4 = mybir.dt.float8_e4m3fn_x4
FP4X4 = mybir.dt.float4_e2m1fn_x4
SILU = mybir.ActivationFunctionType.Silu
MULT = mybir.AluOpType.mult

P = 128
PACK = 4
PASS = P * PACK
CHUNK = 128
WD_COLS = 256
GATE_BANKS = 3


def tile_list_memory_kv_swiglu_kernel(tc, tab_words, tab_scales, tab2_words, tab2_scales, offs, offs2,
                                                   wk_words, wk_scales, wv, wd, out):
    nc = tc.nc
    with ExitStack() as ctx:
        keep = ctx.enter_context(tc.tile_pool(name="keep", bufs=1))
        psum = ctx.enter_context(tc.psum_pool(name="psum", bufs=1))

        def held(shape, dtype, name, tag=None):
            return keep.tile(shape, dtype, name=name, tag=tag or name, align_bytes=256)

        def bank_tile(index, shape):
            return psum.tile(shape, F32, name="bank%d" % index)

        key_list = keep.tile([P, S // 16], U16, name="key_list")
        val_list = keep.tile([P, S // 16], U16, name="val_list")
        key_scale_tab = held([P, T], U8, "key_scale_tab")
        val_scale_tab = held([P, T2], U8, "val_scale_tab")
        wk_scale_raw = held([P, H], U8, "wk_scale_raw")
        wk_raw = held([P, H // 2], I32, "wk_raw")
        key_tab = held([P, T], U32, "key_tab")
        val_tab = [held([P, T2], U32, "val_tab%d" % a) for a in range(2)]
        key_codes = held([P, S], U32, "key_codes")
        key_plane = held([P, S], U8, "key_plane")
        val_codes = {}
        val_plane = held([P, S], U8, "val_plane")
        key_rows = held([P, S], U8, "key_rows")
        val_rows = held([P, S], U8, "val_rows")
        wk_codes = held([P, 2 * H], U8, "wk_codes")
        wk_plane = held([P, H], U8, "wk_plane")

        def copy_on(engine, dst, src):
            if engine == "scalar":
                nc.scalar.copy(out=dst, in_=src)
            else:
                nc.vector.tensor_copy(out=dst, in_=src)

        def quantize(codes, plane, src):
            nc.vector.quantize_mx(out=codes.bitcast(FP8X4), scales=plane, in_=src)

        def load_words(tile, table, a, t0, t1):
            words = table[a].rearrange("p t i -> p (t i)").bitcast(I32)
            nc.sync.dma_start(out=tile[:, t0:t1].bitcast(I32), in_=words[:, t0:t1])

        def load_rows(tile, first, last, rows):
            nc.sync.dma_start(out=tile[first:last:4, :].bitcast(I32), in_=rows.bitcast(I32))

        def load_wk_scales(first, last):
            for r in range(first, last):
                nc.sync.dma_start(out=wk_scale_raw[r:P:32, :].bitcast(I32), in_=wk_scales[0, r:16:4, :].bitcast(I32))

        def place_key_rows():
            for r in range(4):
                nc.sync.dma_start(out=key_plane[r:P:32, :].bitcast(I32), in_=key_rows[32 + 4 * r:96:16, :].bitcast(I32))

        def place_val_rows(first, last):
            for r, a in [divmod(e, 2) for e in range(first, last)]:
                nc.sync.dma_start(out=val_plane[4 * (a + 1) + r:P:32, :].bitcast(I32),
                                  in_=val_rows[64 * a + 4 * r:64 * (a + 1):16, :].bitcast(I32))

        def gather(picked, window, lst, j0, j1):
            nc.vector.tensor_copy(out=picked[:, j0:j1], in_=window[:].indirect(lst[:, j0 // 16:j1 // 16]))

        def gather_values(a, jc0, jc1, room=None):
            picked = held([P, (jc1 - jc0) * CHUNK], U32, "val_codes%d%d" % (a, jc0), room)
            nc.vector.tensor_copy(out=picked[:], in_=val_tab[a][:].indirect(val_list[:, jc0 * CHUNK // 16:jc1 * CHUNK // 16]))
            for jc in range(jc0, jc1):
                val_codes[a, jc] = picked[:, (jc - jc0) * CHUNK:(jc - jc0 + 1) * CHUNK]

        def deal_wk_words():
            nc.scalar.copy(
                out=wk_codes[:].bitcast(U16).rearrange("p (b t m) -> p b t m", b=2, t=PACK),
                in_=wk_raw[:].bitcast(U16).rearrange("p (b m t) -> p b t m", b=2, t=PACK))

        def deal_wk_scales():
            nc.vector.tensor_copy(
                out=wk_plane[:].rearrange("p (b t m) -> p b t m", b=2, t=PACK),
                in_=wk_scale_raw[:].rearrange("p (b m t) -> p b t m", b=2, t=PACK))

        wv_raw = {}
        wv_bf = {}
        wv_codes = {}
        wv_planes = {}

        def load_wv(a, b, m0, m1):
            width = (m1 - m0) * PACK
            wv_raw[a, b, m0] = held([P, PACK * width], F32, "wv_raw%d%d_%d" % (a, b, m0))
            rows = wv[a * PASS:(a + 1) * PASS, b * PASS + m0 * PACK:b * PASS + m1 * PACK]
            nc.sync.dma_start(out=wv_raw[a, b, m0][:].rearrange("p (i r) -> p i r", i=PACK),
                              in_=rows.rearrange("(p i) r -> p i r", i=PACK))

        def cast_wv(a, b, piece, m0, m1, engine):
            if (a, b) not in wv_bf:
                wv_bf[a, b] = held([P, PACK * PASS], BF16, "wv_bf%d%d" % (a, b))
            dst = wv_bf[a, b][:].rearrange("p (t m i) -> p m i t", t=PACK, i=PACK)[:, m0:m1, :, :]
            src = wv_raw[a, b, piece][:].rearrange("p (i m t) -> p m i t", i=PACK, t=PACK)[:, m0 - piece:m1 - piece, :, :]
            copy_on(engine, dst, src)

        def quantize_wv(a, b, room=None):
            wv_codes[a, b] = held([P, PASS], U32, "wv_codes%d%d" % (a, b), room)
            wv_planes[a, b] = held([P, PASS], U8, "wv_plane%d%d" % (a, b))
            quantize(wv_codes[a, b][:], wv_planes[a, b][:], wv_bf[a, b][:])

        wd_raw = {}
        wd_bf = [held([P, 2 * WD_COLS * PACK], BF16, "wd_bf%d" % c) for c in range(3)]
        wd_codes = [held([P, 2 * WD_COLS], U32, "wd_codes%d" % c) for c in range(3)]
        wd_planes = [held([P, 2 * WD_COLS], U8, "wd_plane%d" % c) for c in range(3)]

        def load_wd(b, c):
            wd_raw[b, c] = held([P, PACK * WD_COLS], F32, "wd_raw%d%d" % (b, c))
            rows = wd[b * PASS:(b + 1) * PASS, c * WD_COLS:(c + 1) * WD_COLS]
            nc.sync.dma_start(out=wd_raw[b, c][:].rearrange("p (i n) -> p i n", i=PACK),
                              in_=rows.rearrange("(p i) n -> p i n", i=PACK))

        def cast_wd(b, c, engine, n0=0, n1=WD_COLS):
            at = b * WD_COLS
            copy_on(engine, wd_bf[c][:, (at + n0) * PACK:(at + n1) * PACK].rearrange("p (m e i) -> p m i e", e=4, i=PACK),
                    wd_raw[b, c][:].rearrange("p (i n) -> p i n", i=PACK)[:, :, n0:n1].rearrange("p i (m e) -> p m i e", e=4))

        def quantize_wd(c, b0=0, b1=2):
            cols = slice(b0 * WD_COLS, b1 * WD_COLS)
            quantize(wd_codes[c][:, cols], wd_planes[c][:, cols], wd_bf[c][:, b0 * WD_COLS * PACK:b1 * WD_COLS * PACK])

        gates = {}

        def gate(b, jc, room=None):
            c0 = jc * CHUNK
            bank = bank_tile((8 * b + jc) % GATE_BANKS, [P, PACK, CHUNK])
            for t in range(PACK):
                r0 = b * PASS + t * P
                nc.tensor.matmul_mx(out=bank[:, t, :],
                                    lhsT=wk_codes[:, 2 * r0:2 * (r0 + P)].bitcast(FP4X4),
                                    lhsT_scale=wk_plane[:, r0:r0 + P],
                                    rhs=key_codes[:, c0:c0 + CHUNK].bitcast(FP8X4),
                                    rhs_scale=key_plane[:, c0:c0 + CHUNK],
                                    start=True, stop=True)
            if room is None:
                room = held([P, CHUNK * PACK], F32, "gate%d%d" % (b, jc))[:]
            gates[b, jc] = room.rearrange("p (j t) -> p j t", t=PACK)
            nc.scalar.activation(out=gates[b, jc], in_=bank[:].rearrange("p t j -> p j t"), func=SILU)

        val_banks = {}

        def values(b, jc, a, bank=None):
            c0 = jc * CHUNK
            if a == 0:
                val_banks[b, jc] = bank_tile(bank, [P, PACK, CHUNK])
            for t in range(PACK):
                nc.tensor.matmul_mx(out=val_banks[b, jc][:, t, :],
                                    lhsT=wv_codes[a, b][:, t * P:(t + 1) * P].bitcast(FP8X4),
                                    lhsT_scale=wv_planes[a, b][:, t * P:(t + 1) * P],
                                    rhs=val_codes[a, jc].bitcast(FP8X4),
                                    rhs_scale=val_plane[4 * (a + 1):, c0:c0 + CHUNK],
                                    start=(a == 0 and t == 0), stop=(a == 1 and t == PACK - 1))

        def values_both(b, jc, bank):
            values(b, jc, 0, bank)
            values(b, jc, 1)

        h_bf = {}
        h_codes = {}
        h_planes = {}

        def h_room(b, jc0, jc1, room=None):
            tile = held([P, (jc1 - jc0) * PASS], BF16, "h_bf%d%d" % (b, jc0), room)
            for jc in range(jc0, jc1):
                h_bf[b, jc] = (tile, (jc - jc0) * PASS)

        def hidden(b, jc):
            tile, at = h_bf[b, jc]
            nc.vector.tensor_tensor(out=tile[:, at:at + PASS].rearrange("p (j t) -> p j t", t=PACK),
                                    in0=val_banks[b, jc][:].rearrange("p t j -> p j t"), in1=gates[b, jc], op=MULT)

        def quantize_h(b, jc0, jc1, room=None, group=None):
            first, last = group or (jc0, jc1)
            if (b, first) not in h_codes:
                h_codes[b, first] = held([P, (last - first) * CHUNK], U32, "h_codes%d%d" % (b, first), room)
                h_planes[b, first] = held([P, (last - first) * CHUNK], U8, "h_plane%d%d" % (b, first))
            tile, at = h_bf[b, jc0]
            cols = slice((jc0 - first) * CHUNK, (jc1 - first) * CHUNK)
            quantize(h_codes[b, first][:, cols], h_planes[b, first][:, cols], tile[:, at:at + (jc1 - jc0) * PASS])

        results = {}

        def result_room(c, tag):
            results[c] = held([P, 2 * S], F32, "result%d" % c, tag)[:].rearrange("p (w j) -> p w j", w=2)

        def staged(v0, nv, jc, chunks):
            return results[v0 // 2][:, v0 % 2:v0 % 2 + nv, jc * CHUNK:(jc + chunks) * CHUNK]

        def project(v0, nv, jc, chunks, bank_index, engine):
            width = chunks * CHUNK
            bank = bank_tile(bank_index, [P, nv, width])
            passes = [(b, w, first) for b in range(2) for w in range(nv) for first in range(jc, jc + chunks)
                      if (b, first) in h_codes]
            for b, w, first in passes:
                c, n0 = divmod((v0 + w) * P, WD_COLS)
                n0 = n0 + b * WD_COLS
                j0 = (first - jc) * CHUNK
                nc.tensor.matmul_mx(out=bank[:, w, j0:j0 + h_codes[b, first].shape[1]],
                                    lhsT=wd_codes[c][:, n0:n0 + P].bitcast(FP8X4),
                                    lhsT_scale=wd_planes[c][:, n0:n0 + P],
                                    rhs=h_codes[b, first][:].bitcast(FP8X4),
                                    rhs_scale=h_planes[b, first][:],
                                    start=(b, w, first) == passes[0], stop=(b, w, first) == passes[-1])
            copy_on(engine, staged(v0, nv, jc, chunks), bank[:])

        def store(v0, nv, jc, chunks):
            rows = out[v0 * P:(v0 + nv) * P, jc * CHUNK:(jc + chunks) * CHUNK]
            nc.sync.dma_start(out=rows.rearrange("(v p) j -> p v j", p=P), in_=staged(v0, nv, jc, chunks))

        nc.vector.memset(key_scale_tab[:].bitcast(I32), 0)
        nc.vector.memset(val_scale_tab[:].bitcast(I32), 0)
        nc.vector.memset(wk_scale_raw[:].bitcast(I32), 0)
        nc.vector.memset(key_plane[:].bitcast(I32), 0)
        nc.vector.memset(val_plane[:].bitcast(I32), 0)
        nc.sync.dma_start(key_list[:], offs)
        nc.sync.dma_start(val_list[:], offs2)
        nc.sync.dma_start(out=wk_raw[:], in_=wk_words[0].bitcast(I32))
        load_rows(key_scale_tab, 32, 96, tab_scales[0])
        load_rows(val_scale_tab, 0, P, tab2_scales.rearrange("a q t -> (a q) t"))
        for half in range(2):
            load_wk_scales(2 * half, 2 * half + 2)
            load_words(key_tab, tab_words, 0, half * T // 2, (half + 1) * T // 2)
        deal_wk_words()
        gather(key_rows, key_scale_tab, key_list, 0, S)
        place_key_rows()
        load_words(val_tab[0], tab2_words, 0, 0, T2)
        gather(val_rows, val_scale_tab, val_list, 0, S)
        deal_wk_scales()
        load_wv(0, 0, 0, P)
        load_wv(1, 0, 0, P)
        place_val_rows(0, 2)
        load_words(val_tab[1], tab2_words, 1, 0, T2)
        place_val_rows(2, 8)
        for a in range(2):
            load_wv(a, 1, 0, P)
        for c in range(3):
            for b in range(2):
                load_wd(b, c)

        for j0, j1 in ((0, 256), (256, 512), (512, S)):
            gather(key_codes, key_tab, key_list, j0, j1)
        gather_values(0, 0, 8)
        for b, jc in [divmod(e, 8) for e in range(8)]:
            gate(b, jc)
        for a in range(2):
            cast_wv(a, 0, 0, 0, P, "vector")
            quantize_wv(a, 0)
        for e in range(8, 16):
            w = e - 8
            gate(1, e - 8, wv_raw[0, 0, 0][:, w * PASS:(w + 1) * PASS] if w < 4 else None)
        gather_values(1, 0, 4)
        gather_values(1, 4, 8)
        cast_wv(0, 1, 0, 0, P, "scalar")
        cast_wv(1, 1, 0, 0, 72, "scalar")
        for b, c in ((0, 0), (1, 0), (0, 1), (1, 1), (0, 2)):
            cast_wd(b, c, "scalar")

        for jc in (0, 2, 4):
            h_room(0, jc, jc + 2)
        h_room(1, 0, 4)
        for c, room in enumerate(("key_tab", "val_tab0", "val_tab1")):
            result_room(c, room)

        for jc in range(6):
            values_both(0, jc, 3 + jc % 3)
            hidden(0, jc)
            if jc == 2:
                quantize_h(0, 0, 2)
        values_both(0, 6, 3)
        values_both(0, 7, 4)
        cast_wv(1, 1, 0, 72, P, "vector")
        quantize_wv(0, 1)
        quantize_h(0, 2, 4, "wv_raw01_0")
        quantize_wv(1, 1)
        h_room(0, 6, 7, "wv_raw11_0")
        hidden(0, 6)
        quantize_wd(0, 0, 1)
        for jc in range(4):
            values_both(1, jc, (6, 7, 0, 1)[jc])
            hidden(1, jc)
        values_both(1, 4, 2)
        values_both(1, 5, 5)
        values_both(1, 6, 6)
        values_both(1, 7, 7)
        quantize_wd(0, 1, 2)
        quantize_h(1, 0, 4)
        quantize_wd(1)
        for v in range(4):
            project(v, 1, 0, 4, (3, 0, 1, 3)[v], "scalar")
            store(v, 1, 0, 4)
        h_room(1, 4, 6, "wd_raw11")
        hidden(1, 4)
        hidden(1, 5)
        quantize_h(0, 4, 6, "wd_bf1")
        quantize_h(1, 4, 6)
        for c in range(2):
            project(2 * c, 2, 4, 2, (2, 5)[c], "scalar")
            store(2 * c, 2, 4, 2)
        cast_wd(1, 2, "vector")
        h_room(0, 7, 8, "wd_raw02")
        h_room(1, 6, 8, "wd_raw12")
        quantize_wd(2, 0, 1)
        quantize_wd(2, 1, 2)
        project(4, 2, 4, 2, 3, "scalar")
        for v in (4, 5):
            project(v, 1, 0, 4, v - 4, "scalar")
            store(v, 1, 0, 6)
        hidden(0, 7)
        hidden(1, 6)
        quantize_h(0, 6, 7, "wd_bf2", (6, 8))
        quantize_h(0, 7, 8, None, (6, 8))
        hidden(1, 7)
        quantize_h(1, 6, 7, None, (6, 8))
        quantize_h(1, 7, 8, None, (6, 8))
        for v in (4, 5):
            project(v, 1, 6, 2, (4, 2)[v - 4], ("vector", "scalar")[v - 4])
        store(4, 2, 6, 2)
        for c in range(2):
            project(2 * c, 2, 6, 2, (6, 5)[c], ("vector", "scalar")[c])
            store(2 * c, 2, 6, 2)
